import numpy as np
import ml_dtypes


def mxq(x, axis, fmt="e4m3"):
    dtype, down = {"e4m3": (ml_dtypes.float8_e4m3fn, 7), "e5m2": (ml_dtypes.float8_e5m2, 14)}[fmt]
    v = np.moveaxis(np.asarray(x, np.float32).astype(ml_dtypes.bfloat16).astype(np.float64), axis, -1)
    blocks = v.reshape(v.shape[:-1] + (-1, 32))
    amax = np.abs(blocks).max(-1, keepdims=True)
    byte = np.maximum(np.where(amax > 0, np.frexp(amax)[1] - 1 + 127, 0) - down, 1)
    scale = np.exp2(byte - 127.0)
    codes = (blocks / scale).astype(np.float32).astype(dtype).astype(np.float64)
    return np.moveaxis((codes * scale).reshape(v.shape), -1, axis)


WIDE = False


def mx_kscale(k):
    if not WIDE:
        return np.ones(k)
    levels = np.array([10, -10, 5, -5, 0])
    if k % 512:
        return np.exp2(np.random.permutation(np.resize(levels, k // 32))).repeat(32)
    a = np.empty((k // 512, 16))
    for p in range(k // 512):
        a[p, :8] = np.random.permutation(np.resize(levels, 8))
        for g in range(8):
            far = levels[np.abs(levels - a[p, g]) >= 10]
            a[p, g + 8] = far[np.random.randint(len(far))]
    return np.exp2(a.ravel()).repeat(32)


def f64(x):
    return np.asarray(x).astype(np.float64)


def striped(idx):
    return np.tile(np.asarray(idx).reshape(-1, 16).T, (8, 1)).astype(np.uint16)


def unstriped(offs):
    return offs[:16].T.reshape(-1).astype(np.int64)


B, N, T, D, DV, NQ = 1, 512, 1024, 512, 512, 128
NEW = 256


def setup_inputs():
    n = np.random.standard_normal
    idx = np.random.permutation(T)[:B * N]
    s = mx_kscale(D)[:, None]
    u = np.ones(T)
    u[idx] = mx_kscale(B * N)
    r = np.random.uniform(0.5, 2.0, T)
    raw = n((D, T)) / s / (u * r)
    new = np.random.permutation(idx.reshape(B, N)[:, -NEW // B:].reshape(-1))
    return {
        "qT": (n((B, D, NQ)) * s * (0.60 / np.sqrt(D))).astype(np.float32),
        "cT": np.where(np.isin(np.arange(T), new)[None, :], n((D, T)), raw).astype(np.float32),
        "new_cT": raw[:, new].astype(np.float32),
        "ts": np.tile(u * r, (128, 1)).astype(np.float32),
        "ch": np.tile(s[:, 0] * np.random.uniform(0.5, 2.0, D), (128, 1)).astype(np.float32),
        "offs": striped(idx),
        "slots": striped(new),
    }


def reference(qT, cT, new_cT, ts, ch, offs, slots):
    idx = unstriped(offs)
    c = f64(cT)
    c[:, unstriped(slots)] = f64(new_cT)
    pick = lambda x: x[:, idx].reshape(x.shape[0], B, N).transpose(1, 0, 2)
    q = f64(qT)
    score = mxq(q, 1, "e4m3").transpose(0, 2, 1) @ mxq(pick(c), 1, "e4m3")
    score = score * pick(f64(ts))[:, :1, :]
    m = score.max(-1, keepdims=True)
    p = np.exp(score - m)
    total = p.sum(-1, keepdims=True)
    w = p * pick(f64(ts))[:, :1, :]
    y = mxq(w, 2, "e4m3") @ mxq(pick(c).transpose(0, 2, 1), 1, "e4m3")
    y = y / total
    y = y * f64(ch)[:1]
    return y

@@ -1,0 +1,187 @@
+from contextlib import ExitStack
+
+import concourse.mybir as mybir
+from concourse.masks import make_identity
+
+F32 = mybir.dt.float32
+BF16 = mybir.dt.bfloat16
+U32 = mybir.dt.uint32
+U16 = mybir.dt.uint16
+U8 = mybir.dt.uint8
+FP8X4 = mybir.dt.float8_e4m3fn_x4
+MULT = mybir.AluOpType.mult
+ADD = mybir.AluOpType.add
+MAX = mybir.AluOpType.max
+AX = mybir.AxisListType
+ACT = mybir.ActivationFunctionType
+
+P = 128
+T = 1024
+NEW = 256
+N = 512
+D = 512
+NQ = 128
+HALF = 256
+
+FLOPS = 2 * NQ * N * D * 2
+
+
+def tile_attend_x_mla_append256_topk_kernel(tc, qT, cT, new_cT, ts, ch, offs, slots, out):
+    nc = tc.nc
+    with ExitStack() as ctx:
+        lists = ctx.enter_context(tc.tile_pool(name="lists", bufs=1))
+        keep = ctx.enter_context(tc.tile_pool(name="keep", bufs=1))
+        psum = ctx.enter_context(tc.psum_pool(name="psum", bufs=1))
+
+        slots_sb = lists.tile([P, NEW // 16], U16, name="slots_sb")
+        offs_sb = lists.tile([P, N // 16], U16, name="offs_sb")
+
+        new01 = [keep.tile([P, NEW], F32, name=f"new{t}") for t in range(2)]
+        new23 = keep.tile([P, 2, NEW], F32, name="new23", tag="new23", align_bytes=64)
+        new_sb = [new01[0][:], new01[1][:], new23[:, 0, :], new23[:, 1, :]]
+        pool = [keep.tile([P, T], F32, name=f"pool{t}", tag=f"pool{t}", align_bytes=64) for t in range(4)]
+        q_raw = keep.tile([P, 4, NQ], F32, name="q_raw")
+        ts_sb = keep.tile([P, T], F32, name="ts_sb")
+        ch_sb = keep.tile([P, D], F32, name="ch_sb")
+
+        new_view = new_cT.rearrange("(p j) w -> p j w", j=4)
+        pool_view = cT.rearrange("(p j) w -> p j w", j=4)
+
+        nc.sync.dma_start(slots_sb[:], slots)
+        for t in range(4):
+            if t < 2:
+                nc.sync.dma_start(new_sb[t], new_view[:, t, :])
+            elif t == 2:
+                nc.sync.dma_start(new23[:], new_view[:, 2:4, :])
+            nc.sync.dma_start(pool[t][:], pool_view[:, t, :])
+            if t == 0:
+                nc.sync.dma_start(offs_sb[:], offs)
+        nc.sync.dma_start(ts_sb[:], ts)
+        nc.sync.dma_start(q_raw[:], qT[0].rearrange("(p j) w -> p j w", j=4))
+        nc.sync.dma_start(ch_sb[:], ch)
+
+        warm = keep.tile([P, 1], F32, name="warm")
+        nc.vector.memset(warm[:], 0.0)
+        warm_out = keep.tile([P, 1], F32, name="warm_out")
+        nc.scalar.activation(out=warm_out[:], in_=warm[:], func=ACT.Exp)
+
+        ident = keep.tile([P, P], F32, name="ident")
+        make_identity(nc, ident[:])
+
+        pairs = [keep.tile([P, 2 * T], BF16, name=f"pairs{u}", align_bytes=64) for u in range(2)]
+        for t in range(4):
+            nc.vector.tensor_copy(pool[t][:].indirect(slots_sb[:]), new_sb[t])
+            place = pairs[t // 2][:].rearrange("p (n j) -> p n j", j=2)[:, :, t % 2]
+            share = T if t < 2 else 704
+            nc.scalar.activation(out=place[:, 0:share], in_=pool[t][:, 0:share], func=ACT.Copy)
+            if share < T:
+                nc.gpsimd.tensor_copy(place[:, share:T], pool[t][:, share:T])
+        q_bf = keep.tile([P, NQ, 4], BF16, name="q_bf", tag="pool3", align_bytes=64)
+        q_codes = keep.tile([P, NQ], U32, name="q_codes", align_bytes=64)
+        q_scales = keep.tile([P, NQ], U8, name="q_scales", align_bytes=64)
+        nc.gpsimd.tensor_copy(q_bf[:], q_raw[:].rearrange("p j q -> p q j"))
+
+        latents = keep.tile([P, 4 * N], BF16, name="latents", align_bytes=64)
+        words = latents[:].bitcast(U32).rearrange("p (n u) -> p n u", u=2)
+        words0 = keep.tile([P, N], U32, name="words0", tag="new23", align_bytes=64)
+        nc.vector.tensor_copy(words0[:], pairs[0][:].bitcast(U32).indirect(offs_sb[:]))
+        nc.scalar.copy(
+            latents[:].rearrange("p (n u j) -> p n u j", u=2, j=2)[:, :, 0, :],
+            words0[:].bitcast(BF16).rearrange("p (n j) -> p n j", j=2),
+        )
+        nc.vector.tensor_copy(words[:, :, 1], pairs[1][:].bitcast(U32).indirect(offs_sb[:]))
+
+        k_codes = keep.tile([P, N], U32, name="k_codes", align_bytes=64)
+        k_scales = keep.tile([P, N], U8, name="k_scales", align_bytes=64)
+        scores = psum.tile([P, N], F32, name="scores")
+        nc.vector.quantize_mx(
+            out=q_codes[:].bitcast(FP8X4), scales=q_scales[:], in_=q_bf[:].rearrange("p q j -> p (q j)")
+        )
+        nc.vector.quantize_mx(out=k_codes[:].bitcast(FP8X4), scales=k_scales[:], in_=latents[:])
+
+        ts_g = keep.tile([P, N], F32, name="ts_g", tag="pool3", align_bytes=64)
+        nc.vector.tensor_copy(ts_g[:], ts_sb[:].indirect(offs_sb[:]))
+
+        turned = [psum.tile([P, 4, P], F32, name=f"turned{u}") for u in range(2)]
+        word_views = [
+            words0[:].bitcast(F32).rearrange("p (m s) -> p s m", s=4),
+            latents[:].bitcast(F32).rearrange("p (m s u) -> p u s m", s=4, u=2)[:, 1],
+        ]
+        values = keep.tile([P, 4 * D], BF16, name="values", align_bytes=64)
+        value_view = values[:].rearrange("p (m u j s) -> p u m j s", u=2, j=2, s=4)
+        for u in range(2):
+            for s in range(4):
+                nc.tensor.transpose(turned[u][:, s, :], word_views[u][:, s, :], ident[:])
+        for h in range(2):
+            part = slice(h * 64, (h + 1) * 64)
+            for u in range(2):
+                bank = turned[u][:].rearrange("p s m -> p (s m)").bitcast(BF16)
+                nc.scalar.copy(
+                    value_view[:, u, part], bank.rearrange("p (s m j) -> p m j s", s=4, j=2)[:, part]
+                )
+
+        a = keep.tile([P, N], F32, name="a")
+        neg_m = keep.tile([P, 1], F32, name="neg_m")
+        nc.tensor.matmul_mx(
+            out=scores[:],
+            lhsT=q_codes[:].bitcast(FP8X4),
+            lhsT_scale=q_scales[:],
+            rhs=k_codes[:].bitcast(FP8X4),
+            rhs_scale=k_scales[:],
+            start=True,
+            stop=True,
+        )
+        nc.vector.tensor_tensor(a[:], scores[:], ts_g[:], MULT)
+        nc.vector.tensor_reduce(out=neg_m[:], in_=a[:], axis=AX.X, op=MAX, negate=True)
+
+        v_codes = keep.tile([P, D], U32, name="v_codes", align_bytes=64)
+        v_scales = keep.tile([P, D], U8, name="v_scales", align_bytes=64)
+        for h in range(2):
+            cols = slice(h * HALF, (h + 1) * HALF)
+            nc.vector.quantize_mx(
+                out=v_codes[:, cols].bitcast(FP8X4),
+                scales=v_scales[:, cols],
+                in_=values[:, 4 * h * HALF : 4 * (h + 1) * HALF],
+            )
+
+        prob = keep.tile([P, 2, N // 4, 2], F32, name="prob")
+        sums = keep.tile([P, 2], F32, name="sums")
+        w = keep.tile([P, 2, N // 4, 2], BF16, name="w", align_bytes=64)
+        a_view = a[:].rearrange("p (m u j) -> p u m j", u=2, j=2)
+        ts_view = ts_g[:].rearrange("p (m u j) -> p u m j", u=2, j=2)
+        w_turned = psum.tile([P, 2, P], F32, name="w_turned")
+        w_words = w[:].rearrange("p u m j -> p (u m j)").bitcast(F32)
+        for u in range(2):
+            nc.scalar.activation(
+                out=prob[:, u], in_=a_view[:, u], func=ACT.Exp, bias=neg_m[:], scale=1.0, accum_out=sums[:, u : u + 1]
+            )
+            nc.vector.tensor_tensor(w[:, u], prob[:, u], ts_view[:, u], MULT)
+            nc.tensor.transpose(w_turned[:, u, :], w_words[:, u * P : (u + 1) * P], ident[:])
+
+        w_grouped = keep.tile([P, 4 * NQ], BF16, name="w_grouped", align_bytes=64)
+        nc.scalar.copy(
+            w_grouped[:].bitcast(F32).rearrange("p (q u) -> p q u", u=2), w_turned[:].rearrange("p u q -> p q u")
+        )
+        total = keep.tile([P, 1], F32, name="total")
+        inv = keep.tile([P, 1], F32, name="inv")
+        nc.vector.tensor_tensor(total[:], sums[:, 0:1], sums[:, 1:2], ADD)
+        nc.vector.reciprocal(inv[:], total[:])
+        w_codes = keep.tile([P, NQ], U32, name="w_codes", align_bytes=64)
+        w_scales = keep.tile([P, NQ], U8, name="w_scales", align_bytes=64)
+        nc.vector.quantize_mx(out=w_codes[:].bitcast(FP8X4), scales=w_scales[:], in_=w_grouped[:])
+
+        y = [psum.tile([P, HALF], F32, name=f"y{h}") for h in range(2)]
+        result = keep.tile([P, D], F32, name="result")
+        for h in range(2):
+            cols = slice(h * HALF, (h + 1) * HALF)
+            nc.tensor.matmul_mx(
+                out=y[h][:],
+                lhsT=w_codes[:].bitcast(FP8X4),
+                lhsT_scale=w_scales[:],
+                rhs=v_codes[:, cols].bitcast(FP8X4),
+                rhs_scale=v_scales[:, cols],
+                start=True,
+                stop=True,
+            )
+            nc.vector.scalar_tensor_tensor(result[:, cols], y[h][:], inv[:], ch_sb[:, cols], MULT, MULT)
+            nc.sync.dma_start(out[0][:, cols], result[:, cols])

@@ -31,16 +31,17 @@ def tile_attend_x_mla_append256_topk_kernel(tc, qT, cT, new_cT, ts, ch, offs, sl
     with ExitStack() as ctx:
         lists = ctx.enter_context(tc.tile_pool(name="lists", bufs=1))
         keep = ctx.enter_context(tc.tile_pool(name="keep", bufs=1))
+        reuse = ctx.enter_context(tc.tile_pool(name="reuse", bufs=1))
         psum = ctx.enter_context(tc.psum_pool(name="psum", bufs=1))
 
         slots_sb = lists.tile([P, NEW // 16], U16, name="slots_sb")
         offs_sb = lists.tile([P, N // 16], U16, name="offs_sb")
 
         new01 = [keep.tile([P, NEW], F32, name=f"new{t}") for t in range(2)]
-        new23 = keep.tile([P, 2, NEW], F32, name="new23", tag="new23", align_bytes=64)
+        new23 = reuse.tile([P, 2, NEW], F32, name="new23", offset=3072, align_bytes=64)
         new_sb = [new01[0][:], new01[1][:], new23[:, 0, :], new23[:, 1, :]]
         pool = [keep.tile([P, T], F32, name=f"pool{t}", tag=f"pool{t}", align_bytes=64) for t in range(4)]
-        q_raw = keep.tile([P, 4, NQ], F32, name="q_raw")
+        q_raw = keep.tile([P, 4, NQ], F32, name="q_raw", tag="pairs0", align_bytes=64)
         ts_sb = keep.tile([P, T], F32, name="ts_sb")
         ch_sb = keep.tile([P, D], F32, name="ch_sb")
 
@@ -56,8 +57,8 @@ def tile_attend_x_mla_append256_topk_kernel(tc, qT, cT, new_cT, ts, ch, offs, sl
             nc.sync.dma_start(pool[t][:], pool_view[:, t, :])
             if t == 0:
                 nc.sync.dma_start(offs_sb[:], offs)
+                nc.sync.dma_start(q_raw[:], qT[0].rearrange("(p j) w -> p j w", j=4))
         nc.sync.dma_start(ts_sb[:], ts)
-        nc.sync.dma_start(q_raw[:], qT[0].rearrange("(p j) w -> p j w", j=4))
         nc.sync.dma_start(ch_sb[:], ch)
 
         warm = keep.tile([P, 1], F32, name="warm")
@@ -68,50 +69,66 @@ def tile_attend_x_mla_append256_topk_kernel(tc, qT, cT, new_cT, ts, ch, offs, sl
         ident = keep.tile([P, P], F32, name="ident")
         make_identity(nc, ident[:])
 
-        pairs = [keep.tile([P, 2 * T], BF16, name=f"pairs{u}", align_bytes=64) for u in range(2)]
+        q_bf = keep.tile([P, NQ, 4], BF16, name="q_bf", align_bytes=64)
+        q_codes = reuse.tile([P, NQ], U32, name="q_codes", offset=4096, align_bytes=64)
+        q_scales = keep.tile([P, NQ], U8, name="q_scales", align_bytes=64)
+        nc.scalar.activation(out=q_bf[:], in_=q_raw[:].rearrange("p j q -> p q j"), func=ACT.Copy)
+
+        pairs = [keep.tile([P, 2 * T], BF16, name=f"pairs{u}", tag=f"pairs{u}", align_bytes=64) for u in range(2)]
         for t in range(4):
             nc.vector.tensor_copy(pool[t][:].indirect(slots_sb[:]), new_sb[t])
             place = pairs[t // 2][:].rearrange("p (n j) -> p n j", j=2)[:, :, t % 2]
-            share = T if t < 2 else 704
-            nc.scalar.activation(out=place[:, 0:share], in_=pool[t][:, 0:share], func=ACT.Copy)
-            if share < T:
-                nc.gpsimd.tensor_copy(place[:, share:T], pool[t][:, share:T])
-        q_bf = keep.tile([P, NQ, 4], BF16, name="q_bf", tag="pool3", align_bytes=64)
-        q_codes = keep.tile([P, NQ], U32, name="q_codes", align_bytes=64)
-        q_scales = keep.tile([P, NQ], U8, name="q_scales", align_bytes=64)
-        nc.gpsimd.tensor_copy(q_bf[:], q_raw[:].rearrange("p j q -> p q j"))
+            nc.scalar.activation(out=place, in_=pool[t][:], func=ACT.Copy)
 
-        latents = keep.tile([P, 4 * N], BF16, name="latents", align_bytes=64)
-        words = latents[:].bitcast(U32).rearrange("p (n u) -> p n u", u=2)
-        words0 = keep.tile([P, N], U32, name="words0", tag="new23", align_bytes=64)
-        nc.vector.tensor_copy(words0[:], pairs[0][:].bitcast(U32).indirect(offs_sb[:]))
-        nc.scalar.copy(
-            latents[:].rearrange("p (n u j) -> p n u j", u=2, j=2)[:, :, 0, :],
-            words0[:].bitcast(BF16).rearrange("p (n j) -> p n j", j=2),
+        words = reuse.tile([P, 2, 4, P], U32, name="words", offset=0, align_bytes=64)
+        ts_g = [
+            keep.tile([P, HALF], F32, name="ts_g0", align_bytes=64),
+            keep.tile([P, HALF], F32, name="ts_g1", tag="pairs1", align_bytes=64),
+        ]
+        list_half = [offs_sb[:, 16 * h : 16 * (h + 1)] for h in range(2)]
+        nc.vector.tensor_copy(
+            words[:, 0].rearrange("p s m -> p m s"), pairs[0][:].bitcast(U32).indirect(offs_sb[:])
         )
-        nc.vector.tensor_copy(words[:, :, 1], pairs[1][:].bitcast(U32).indirect(offs_sb[:]))
-
-        k_codes = keep.tile([P, N], U32, name="k_codes", align_bytes=64)
-        k_scales = keep.tile([P, N], U8, name="k_scales", align_bytes=64)
-        scores = psum.tile([P, N], F32, name="scores")
+        nc.vector.tensor_copy(ts_g[0][:], ts_sb[:].indirect(list_half[0]))
         nc.vector.quantize_mx(
             out=q_codes[:].bitcast(FP8X4), scales=q_scales[:], in_=q_bf[:].rearrange("p q j -> p (q j)")
         )
-        nc.vector.quantize_mx(out=k_codes[:].bitcast(FP8X4), scales=k_scales[:], in_=latents[:])
+        latents = [keep.tile([P, 4, 64, 2], U32, name=f"latents{h}", align_bytes=64) for h in range(2)]
+        for h in range(2):
+            part = slice(h * 64, (h + 1) * 64)
+            nc.vector.tensor_copy(
+                words[:, 1, :, part].rearrange("p s m -> p m s"), pairs[1][:].bitcast(U32).indirect(list_half[h])
+            )
+            nc.scalar.copy(latents[h][:], words[:].rearrange("p u s m -> p s m u")[:, :, part, :])
+        nc.vector.tensor_copy(ts_g[1][:], ts_sb[:].indirect(list_half[1]))
 
-        ts_g = keep.tile([P, N], F32, name="ts_g", tag="pool3", align_bytes=64)
-        nc.vector.tensor_copy(ts_g[:], ts_sb[:].indirect(offs_sb[:]))
+        k_codes = [keep.tile([P, HALF], U32, name=f"k_codes{h}", align_bytes=64) for h in range(2)]
+        k_scales = [keep.tile([P, HALF], U8, name=f"k_scales{h}", align_bytes=64) for h in range(2)]
+        scores = [psum.tile([P, HALF], F32, name=f"scores{h}") for h in range(2)]
+        for h in range(2):
+            nc.vector.quantize_mx(
+                out=k_codes[h][:].bitcast(FP8X4),
+                scales=k_scales[h][:],
+                in_=latents[h][:].rearrange("p s m u -> p (s m u)").bitcast(BF16),
+            )
+            nc.tensor.matmul_mx(
+                out=scores[h][:],
+                lhsT=q_codes[:].bitcast(FP8X4),
+                lhsT_scale=q_scales[:],
+                rhs=k_codes[h][:].bitcast(FP8X4),
+                rhs_scale=k_scales[h][:],
+                start=True,
+                stop=True,
+            )
 
         turned = [psum.tile([P, 4, P], F32, name=f"turned{u}") for u in range(2)]
-        word_views = [
-            words0[:].bitcast(F32).rearrange("p (m s) -> p s m", s=4),
-            latents[:].bitcast(F32).rearrange("p (m s u) -> p u s m", s=4, u=2)[:, 1],
-        ]
         values = keep.tile([P, 4 * D], BF16, name="values", align_bytes=64)
         value_view = values[:].rearrange("p (m u j s) -> p u m j s", u=2, j=2, s=4)
+        word_floats = words[:].rearrange("p u s m -> p (u s m)").bitcast(F32)
         for u in range(2):
             for s in range(4):
-                nc.tensor.transpose(turned[u][:, s, :], word_views[u][:, s, :], ident[:])
+                first = (4 * u + s) * P
+                nc.tensor.transpose(turned[u][:, s, :], word_floats[:, first : first + P], ident[:])
         for h in range(2):
             part = slice(h * 64, (h + 1) * 64)
             for u in range(2):
@@ -122,16 +139,13 @@ def tile_attend_x_mla_append256_topk_kernel(tc, qT, cT, new_cT, ts, ch, offs, sl
 
         a = keep.tile([P, N], F32, name="a")
         neg_m = keep.tile([P, 1], F32, name="neg_m")
-        nc.tensor.matmul_mx(
-            out=scores[:],
-            lhsT=q_codes[:].bitcast(FP8X4),
-            lhsT_scale=q_scales[:],
-            rhs=k_codes[:].bitcast(FP8X4),
-            rhs_scale=k_scales[:],
-            start=True,
-            stop=True,
-        )
-        nc.vector.tensor_tensor(a[:], scores[:], ts_g[:], MULT)
+        for h in range(2):
+            nc.vector.tensor_tensor(
+                a[:, h * HALF : (h + 1) * HALF].rearrange("p (m s) -> p m s", s=4),
+                scores[h][:].rearrange("p (s m) -> p m s", s=4),
+                ts_g[h][:].rearrange("p (m s) -> p m s", s=4),
+                MULT,
+            )
         nc.vector.tensor_reduce(out=neg_m[:], in_=a[:], axis=AX.X, op=MAX, negate=True)
 
         v_codes = keep.tile([P, D], U32, name="v_codes", align_bytes=64)
@@ -148,14 +162,16 @@ def tile_attend_x_mla_append256_topk_kernel(tc, qT, cT, new_cT, ts, ch, offs, sl
         sums = keep.tile([P, 2], F32, name="sums")
         w = keep.tile([P, 2, N // 4, 2], BF16, name="w", align_bytes=64)
         a_view = a[:].rearrange("p (m u j) -> p u m j", u=2, j=2)
-        ts_view = ts_g[:].rearrange("p (m u j) -> p u m j", u=2, j=2)
+        ts_view = [ts_g[h][:].rearrange("p (m u j) -> p u m j", u=2, j=2) for h in range(2)]
         w_turned = psum.tile([P, 2, P], F32, name="w_turned")
         w_words = w[:].rearrange("p u m j -> p (u m j)").bitcast(F32)
         for u in range(2):
             nc.scalar.activation(
                 out=prob[:, u], in_=a_view[:, u], func=ACT.Exp, bias=neg_m[:], scale=1.0, accum_out=sums[:, u : u + 1]
             )
-            nc.vector.tensor_tensor(w[:, u], prob[:, u], ts_view[:, u], MULT)
+            for h in range(2):
+                part = slice(h * 64, (h + 1) * 64)
+                nc.vector.tensor_tensor(w[:, u, part], prob[:, u, part], ts_view[h][:, u], MULT)
             nc.tensor.transpose(w_turned[:, u, :], w_words[:, u * P : (u + 1) * P], ident[:])
 
         w_grouped = keep.tile([P, 4 * NQ], BF16, name="w_grouped", align_bytes=64)

@@ -37,11 +37,10 @@ def tile_attend_x_mla_append256_topk_kernel(tc, qT, cT, new_cT, ts, ch, offs, sl
         slots_sb = lists.tile([P, NEW // 16], U16, name="slots_sb")
         offs_sb = lists.tile([P, N // 16], U16, name="offs_sb")
 
-        new01 = [keep.tile([P, NEW], F32, name=f"new{t}") for t in range(2)]
-        new23 = reuse.tile([P, 2, NEW], F32, name="new23", offset=3072, align_bytes=64)
-        new_sb = [new01[0][:], new01[1][:], new23[:, 0, :], new23[:, 1, :]]
-        pool = [keep.tile([P, T], F32, name=f"pool{t}", tag=f"pool{t}", align_bytes=64) for t in range(4)]
-        q_raw = keep.tile([P, 4, NQ], F32, name="q_raw", tag="pairs0", align_bytes=64)
+        new_sb = [keep.tile([P, NEW], F32, name=f"new{t}") for t in range(3)]
+        new_sb.append(reuse.tile([P, NEW], F32, name="new3", offset=3584, align_bytes=64))
+        pool = [keep.tile([P, T], F32, name=f"pool{t}", align_bytes=64) for t in range(4)]
+        q_raw = keep.tile([P, 4, NQ], F32, name="q_raw")
         ts_sb = keep.tile([P, T], F32, name="ts_sb")
         ch_sb = keep.tile([P, D], F32, name="ch_sb")
 
@@ -50,13 +49,11 @@ def tile_attend_x_mla_append256_topk_kernel(tc, qT, cT, new_cT, ts, ch, offs, sl
 
         nc.sync.dma_start(slots_sb[:], slots)
         for t in range(4):
-            if t < 2:
-                nc.sync.dma_start(new_sb[t], new_view[:, t, :])
-            elif t == 2:
-                nc.sync.dma_start(new23[:], new_view[:, 2:4, :])
+            nc.sync.dma_start(new_sb[t][:], new_view[:, t, :])
             nc.sync.dma_start(pool[t][:], pool_view[:, t, :])
             if t == 0:
                 nc.sync.dma_start(offs_sb[:], offs)
+            if t == 1:
                 nc.sync.dma_start(q_raw[:], qT[0].rearrange("(p j) w -> p j w", j=4))
         nc.sync.dma_start(ts_sb[:], ts)
         nc.sync.dma_start(ch_sb[:], ch)
@@ -72,34 +69,30 @@ def tile_attend_x_mla_append256_topk_kernel(tc, qT, cT, new_cT, ts, ch, offs, sl
         q_bf = keep.tile([P, NQ, 4], BF16, name="q_bf", align_bytes=64)
         q_codes = reuse.tile([P, NQ], U32, name="q_codes", offset=4096, align_bytes=64)
         q_scales = keep.tile([P, NQ], U8, name="q_scales", align_bytes=64)
-        nc.scalar.activation(out=q_bf[:], in_=q_raw[:].rearrange("p j q -> p q j"), func=ACT.Copy)
+        nc.gpsimd.tensor_copy(q_bf[:], q_raw[:].rearrange("p j q -> p q j"))
 
         pairs = [keep.tile([P, 2 * T], BF16, name=f"pairs{u}", tag=f"pairs{u}", align_bytes=64) for u in range(2)]
         for t in range(4):
-            nc.vector.tensor_copy(pool[t][:].indirect(slots_sb[:]), new_sb[t])
+            nc.vector.tensor_copy(pool[t][:].indirect(slots_sb[:]), new_sb[t][:])
             place = pairs[t // 2][:].rearrange("p (n j) -> p n j", j=2)[:, :, t % 2]
             nc.scalar.activation(out=place, in_=pool[t][:], func=ACT.Copy)
 
-        words = reuse.tile([P, 2, 4, P], U32, name="words", offset=0, align_bytes=64)
+        words = reuse.tile([P, 2, N], U32, name="words", offset=0, align_bytes=64)
         ts_g = [
             keep.tile([P, HALF], F32, name="ts_g0", align_bytes=64),
             keep.tile([P, HALF], F32, name="ts_g1", tag="pairs1", align_bytes=64),
         ]
         list_half = [offs_sb[:, 16 * h : 16 * (h + 1)] for h in range(2)]
-        nc.vector.tensor_copy(
-            words[:, 0].rearrange("p s m -> p m s"), pairs[0][:].bitcast(U32).indirect(offs_sb[:])
-        )
+        nc.vector.tensor_copy(words[:, 0, :], pairs[0][:].bitcast(U32).indirect(offs_sb[:]))
         nc.vector.tensor_copy(ts_g[0][:], ts_sb[:].indirect(list_half[0]))
         nc.vector.quantize_mx(
             out=q_codes[:].bitcast(FP8X4), scales=q_scales[:], in_=q_bf[:].rearrange("p q j -> p (q j)")
         )
-        latents = [keep.tile([P, 4, 64, 2], U32, name=f"latents{h}", align_bytes=64) for h in range(2)]
+        latents = [keep.tile([P, HALF, 2], U32, name=f"latents{h}", align_bytes=64) for h in range(2)]
         for h in range(2):
-            part = slice(h * 64, (h + 1) * 64)
-            nc.vector.tensor_copy(
-                words[:, 1, :, part].rearrange("p s m -> p m s"), pairs[1][:].bitcast(U32).indirect(list_half[h])
-            )
-            nc.scalar.copy(latents[h][:], words[:].rearrange("p u s m -> p s m u")[:, :, part, :])
+            part = slice(h * HALF, (h + 1) * HALF)
+            nc.vector.tensor_copy(words[:, 1, part], pairs[1][:].bitcast(U32).indirect(list_half[h]))
+            nc.scalar.copy(latents[h][:], words[:].rearrange("p u n -> p n u")[:, part, :])
         nc.vector.tensor_copy(ts_g[1][:], ts_sb[:].indirect(list_half[1]))
 
         k_codes = [keep.tile([P, HALF], U32, name=f"k_codes{h}", align_bytes=64) for h in range(2)]
@@ -109,7 +102,7 @@ def tile_attend_x_mla_append256_topk_kernel(tc, qT, cT, new_cT, ts, ch, offs, sl
             nc.vector.quantize_mx(
                 out=k_codes[h][:].bitcast(FP8X4),
                 scales=k_scales[h][:],
-                in_=latents[h][:].rearrange("p s m u -> p (s m u)").bitcast(BF16),
+                in_=latents[h][:].rearrange("p n u -> p (n u)").bitcast(BF16),
             )
             nc.tensor.matmul_mx(
                 out=scores[h][:],
@@ -124,11 +117,10 @@ def tile_attend_x_mla_append256_topk_kernel(tc, qT, cT, new_cT, ts, ch, offs, sl
         turned = [psum.tile([P, 4, P], F32, name=f"turned{u}") for u in range(2)]
         values = keep.tile([P, 4 * D], BF16, name="values", align_bytes=64)
         value_view = values[:].rearrange("p (m u j s) -> p u m j s", u=2, j=2, s=4)
-        word_floats = words[:].rearrange("p u s m -> p (u s m)").bitcast(F32)
+        word_floats = words[:].bitcast(F32).rearrange("p u (m s) -> p u s m", s=4)
         for u in range(2):
             for s in range(4):
-                first = (4 * u + s) * P
-                nc.tensor.transpose(turned[u][:, s, :], word_floats[:, first : first + P], ident[:])
+                nc.tensor.transpose(turned[u][:, s, :], word_floats[:, u, s, :], ident[:])
         for h in range(2):
             part = slice(h * 64, (h + 1) * 64)
             for u in range(2):
@@ -140,12 +132,7 @@ def tile_attend_x_mla_append256_topk_kernel(tc, qT, cT, new_cT, ts, ch, offs, sl
         a = keep.tile([P, N], F32, name="a")
         neg_m = keep.tile([P, 1], F32, name="neg_m")
         for h in range(2):
-            nc.vector.tensor_tensor(
-                a[:, h * HALF : (h + 1) * HALF].rearrange("p (m s) -> p m s", s=4),
-                scores[h][:].rearrange("p (s m) -> p m s", s=4),
-                ts_g[h][:].rearrange("p (m s) -> p m s", s=4),
-                MULT,
-            )
+            nc.vector.tensor_tensor(a[:, h * HALF : (h + 1) * HALF], scores[h][:], ts_g[h][:], MULT)
         nc.vector.tensor_reduce(out=neg_m[:], in_=a[:], axis=AX.X, op=MAX, negate=True)
 
         v_codes = keep.tile([P, D], U32, name="v_codes", align_bytes=64)

@@ -135,17 +135,7 @@ def tile_attend_x_mla_append256_topk_kernel(tc, qT, cT, new_cT, ts, ch, offs, sl
             nc.vector.tensor_tensor(a[:, h * HALF : (h + 1) * HALF], scores[h][:], ts_g[h][:], MULT)
         nc.vector.tensor_reduce(out=neg_m[:], in_=a[:], axis=AX.X, op=MAX, negate=True)
 
-        v_codes = keep.tile([P, D], U32, name="v_codes", align_bytes=64)
-        v_scales = keep.tile([P, D], U8, name="v_scales", align_bytes=64)
-        for h in range(2):
-            cols = slice(h * HALF, (h + 1) * HALF)
-            nc.vector.quantize_mx(
-                out=v_codes[:, cols].bitcast(FP8X4),
-                scales=v_scales[:, cols],
-                in_=values[:, 4 * h * HALF : 4 * (h + 1) * HALF],
-            )
-
-        prob = keep.tile([P, 2, N // 4, 2], F32, name="prob")
+        prob = [keep.tile([P, N // 4, 2], F32, name=f"prob{u}", tag=f"prob{u}", align_bytes=64) for u in range(2)]
         sums = keep.tile([P, 2], F32, name="sums")
         w = keep.tile([P, 2, N // 4, 2], BF16, name="w", align_bytes=64)
         a_view = a[:].rearrange("p (m u j) -> p u m j", u=2, j=2)
@@ -154,12 +144,15 @@ def tile_attend_x_mla_append256_topk_kernel(tc, qT, cT, new_cT, ts, ch, offs, sl
         w_words = w[:].rearrange("p u m j -> p (u m j)").bitcast(F32)
         for u in range(2):
             nc.scalar.activation(
-                out=prob[:, u], in_=a_view[:, u], func=ACT.Exp, bias=neg_m[:], scale=1.0, accum_out=sums[:, u : u + 1]
+                out=prob[u][:], in_=a_view[:, u], func=ACT.Exp, bias=neg_m[:], scale=1.0, accum_out=sums[:, u : u + 1]
             )
             for h in range(2):
                 part = slice(h * 64, (h + 1) * 64)
-                nc.vector.tensor_tensor(w[:, u, part], prob[:, u, part], ts_view[h][:, u], MULT)
+                nc.vector.tensor_tensor(w[:, u, part], prob[u][:, part], ts_view[h][:, u], MULT)
             nc.tensor.transpose(w_turned[:, u, :], w_words[:, u * P : (u + 1) * P], ident[:])
+        v_codes = keep.tile([P, D], U32, name="v_codes", tag="prob1", align_bytes=64)
+        v_scales = keep.tile([P, D], U8, name="v_scales", align_bytes=64)
+        nc.vector.quantize_mx(out=v_codes[:].bitcast(FP8X4), scales=v_scales[:], in_=values[:])
 
         w_grouped = keep.tile([P, 4 * NQ], BF16, name="w_grouped", align_bytes=64)
         nc.scalar.copy(

@@ -77,22 +77,26 @@ def tile_attend_x_mla_append256_topk_kernel(tc, qT, cT, new_cT, ts, ch, offs, sl
             place = pairs[t // 2][:].rearrange("p (n j) -> p n j", j=2)[:, :, t % 2]
             nc.scalar.activation(out=place, in_=pool[t][:], func=ACT.Copy)
 
-        words = reuse.tile([P, 2, N], U32, name="words", offset=0, align_bytes=64)
+        words = reuse.tile([P, 2, 2, P, 2], U32, name="words", offset=0, align_bytes=64)
         ts_g = [
             keep.tile([P, HALF], F32, name="ts_g0", align_bytes=64),
             keep.tile([P, HALF], F32, name="ts_g1", tag="pairs1", align_bytes=64),
         ]
         list_half = [offs_sb[:, 16 * h : 16 * (h + 1)] for h in range(2)]
-        nc.vector.tensor_copy(words[:, 0, :], pairs[0][:].bitcast(U32).indirect(offs_sb[:]))
+        nc.vector.tensor_copy(
+            words[:, 0].rearrange("p v m j -> p m v j"), pairs[0][:].bitcast(U32).indirect(offs_sb[:])
+        )
         nc.vector.tensor_copy(ts_g[0][:], ts_sb[:].indirect(list_half[0]))
         nc.vector.quantize_mx(
             out=q_codes[:].bitcast(FP8X4), scales=q_scales[:], in_=q_bf[:].rearrange("p q j -> p (q j)")
         )
-        latents = [keep.tile([P, HALF, 2], U32, name=f"latents{h}", align_bytes=64) for h in range(2)]
+        latents = [keep.tile([P, 2, P, 2], U32, name=f"latents{h}", align_bytes=64) for h in range(2)]
         for h in range(2):
-            part = slice(h * HALF, (h + 1) * HALF)
-            nc.vector.tensor_copy(words[:, 1, part], pairs[1][:].bitcast(U32).indirect(list_half[h]))
-            nc.scalar.copy(latents[h][:], words[:].rearrange("p u n -> p n u")[:, part, :])
+            nc.vector.tensor_copy(
+                words[:, 1, :, h * 64 : (h + 1) * 64, :].rearrange("p v m j -> p m v j"),
+                pairs[1][:].bitcast(U32).indirect(list_half[h]),
+            )
+            nc.scalar.copy(latents[h][:], words[:].rearrange("p u v m j -> p v (m j) u")[:, :, h * P : (h + 1) * P, :])
         nc.vector.tensor_copy(ts_g[1][:], ts_sb[:].indirect(list_half[1]))
 
         k_codes = [keep.tile([P, HALF], U32, name=f"k_codes{h}", align_bytes=64) for h in range(2)]
@@ -102,7 +106,7 @@ def tile_attend_x_mla_append256_topk_kernel(tc, qT, cT, new_cT, ts, ch, offs, sl
             nc.vector.quantize_mx(
                 out=k_codes[h][:].bitcast(FP8X4),
                 scales=k_scales[h][:],
-                in_=latents[h][:].rearrange("p n u -> p (n u)").bitcast(BF16),
+                in_=latents[h][:].rearrange("p v n u -> p (v n u)").bitcast(BF16),
             )
             nc.tensor.matmul_mx(
                 out=scores[h][:],
@@ -117,10 +121,10 @@ def tile_attend_x_mla_append256_topk_kernel(tc, qT, cT, new_cT, ts, ch, offs, sl
         turned = [psum.tile([P, 4, P], F32, name=f"turned{u}") for u in range(2)]
         values = keep.tile([P, 4 * D], BF16, name="values", align_bytes=64)
         value_view = values[:].rearrange("p (m u j s) -> p u m j s", u=2, j=2, s=4)
-        word_floats = words[:].bitcast(F32).rearrange("p u (m s) -> p u s m", s=4)
+        word_floats = words[:].bitcast(F32)
         for u in range(2):
             for s in range(4):
-                nc.tensor.transpose(turned[u][:, s, :], word_floats[:, u, s, :], ident[:])
+                nc.tensor.transpose(turned[u][:, s, :], word_floats[:, u, s // 2, :, s % 2], ident[:])
         for h in range(2):
             part = slice(h * 64, (h + 1) * 64)
             for u in range(2):
@@ -129,22 +133,28 @@ def tile_attend_x_mla_append256_topk_kernel(tc, qT, cT, new_cT, ts, ch, offs, sl
                     value_view[:, u, part], bank.rearrange("p (s m j) -> p m j s", s=4, j=2)[:, part]
                 )
 
-        a = keep.tile([P, N], F32, name="a")
+        a = keep.tile([P, 2, N // 4, 2], F32, name="a")
         neg_m = keep.tile([P, 1], F32, name="neg_m")
+        ts_view = [ts_g[h][:].rearrange("p (m v j) -> p v m j", v=2, j=2) for h in range(2)]
         for h in range(2):
-            nc.vector.tensor_tensor(a[:, h * HALF : (h + 1) * HALF], scores[h][:], ts_g[h][:], MULT)
-        nc.vector.tensor_reduce(out=neg_m[:], in_=a[:], axis=AX.X, op=MAX, negate=True)
+            nc.vector.tensor_tensor(
+                a[:, :, h * 64 : (h + 1) * 64, :],
+                scores[h][:].rearrange("p (v m j) -> p v m j", v=2, j=2),
+                ts_view[h],
+                MULT,
+            )
+        nc.vector.tensor_reduce(
+            out=neg_m[:], in_=a[:].rearrange("p v m j -> p (v m j)"), axis=AX.X, op=MAX, negate=True
+        )
 
         prob = [keep.tile([P, N // 4, 2], F32, name=f"prob{u}", tag=f"prob{u}", align_bytes=64) for u in range(2)]
         sums = keep.tile([P, 2], F32, name="sums")
         w = keep.tile([P, 2, N // 4, 2], BF16, name="w", align_bytes=64)
-        a_view = a[:].rearrange("p (m u j) -> p u m j", u=2, j=2)
-        ts_view = [ts_g[h][:].rearrange("p (m u j) -> p u m j", u=2, j=2) for h in range(2)]
         w_turned = psum.tile([P, 2, P], F32, name="w_turned")
         w_words = w[:].rearrange("p u m j -> p (u m j)").bitcast(F32)
         for u in range(2):
             nc.scalar.activation(
-                out=prob[u][:], in_=a_view[:, u], func=ACT.Exp, bias=neg_m[:], scale=1.0, accum_out=sums[:, u : u + 1]
+                out=prob[u][:], in_=a[:, u], func=ACT.Exp, bias=neg_m[:], scale=1.0, accum_out=sums[:, u : u + 1]
             )
             for h in range(2):
                 part = slice(h * 64, (h + 1) * 64)

@@ -22,6 +22,7 @@ N = 512
 D = 512
 NQ = 128
 HALF = 256
+EARLY = 96
 
 FLOPS = 2 * NQ * N * D * 2
 
@@ -47,15 +48,15 @@ def tile_attend_x_mla_append256_topk_kernel(tc, qT, cT, new_cT, ts, ch, offs, sl
         new_view = new_cT.rearrange("(p j) w -> p j w", j=4)
         pool_view = cT.rearrange("(p j) w -> p j w", j=4)
 
-        nc.sync.dma_start(slots_sb[:], slots)
         for t in range(4):
-            nc.sync.dma_start(new_sb[t][:], new_view[:, t, :])
             nc.sync.dma_start(pool[t][:], pool_view[:, t, :])
+            nc.sync.dma_start(new_sb[t][:], new_view[:, t, :])
             if t == 0:
-                nc.sync.dma_start(offs_sb[:], offs)
+                nc.sync.dma_start(slots_sb[:], slots)
             if t == 1:
-                nc.sync.dma_start(q_raw[:], qT[0].rearrange("(p j) w -> p j w", j=4))
+                nc.sync.dma_start(offs_sb[:], offs)
         nc.sync.dma_start(ts_sb[:], ts)
+        nc.sync.dma_start(q_raw[:], qT[0].rearrange("(p j) w -> p j w", j=4))
         nc.sync.dma_start(ch_sb[:], ch)
 
         warm = keep.tile([P, 1], F32, name="warm")
@@ -67,11 +68,14 @@ def tile_attend_x_mla_append256_topk_kernel(tc, qT, cT, new_cT, ts, ch, offs, sl
         make_identity(nc, ident[:])
 
         q_bf = keep.tile([P, NQ, 4], BF16, name="q_bf", align_bytes=64)
-        q_codes = reuse.tile([P, NQ], U32, name="q_codes", offset=4096, align_bytes=64)
+        q_codes = keep.tile([P, NQ], U32, name="q_codes", align_bytes=64)
         q_scales = keep.tile([P, NQ], U8, name="q_scales", align_bytes=64)
-        nc.gpsimd.tensor_copy(q_bf[:], q_raw[:].rearrange("p j q -> p q j"))
+        nc.scalar.activation(out=q_bf[:], in_=q_raw[:].rearrange("p j q -> p q j"), func=ACT.Copy)
 
-        pairs = [keep.tile([P, 2 * T], BF16, name=f"pairs{u}", tag=f"pairs{u}", align_bytes=64) for u in range(2)]
+        pairs = [
+            keep.tile([P, 2 * T], BF16, name="pairs0", align_bytes=64),
+            reuse.tile([P, 2 * T], BF16, name="pairs1", offset=8192, align_bytes=64),
+        ]
         for t in range(4):
             nc.vector.tensor_copy(pool[t][:].indirect(slots_sb[:]), new_sb[t][:])
             place = pairs[t // 2][:].rearrange("p (n j) -> p n j", j=2)[:, :, t % 2]
@@ -80,16 +84,29 @@ def tile_attend_x_mla_append256_topk_kernel(tc, qT, cT, new_cT, ts, ch, offs, sl
         words = reuse.tile([P, 2, 2, P, 2], U32, name="words", offset=0, align_bytes=64)
         ts_g = [
             keep.tile([P, HALF], F32, name="ts_g0", align_bytes=64),
-            keep.tile([P, HALF], F32, name="ts_g1", tag="pairs1", align_bytes=64),
+            reuse.tile([P, HALF], F32, name="ts_g1", offset=8192, align_bytes=64),
         ]
         list_half = [offs_sb[:, 16 * h : 16 * (h + 1)] for h in range(2)]
         nc.vector.tensor_copy(
             words[:, 0].rearrange("p v m j -> p m v j"), pairs[0][:].bitcast(U32).indirect(offs_sb[:])
         )
         nc.vector.tensor_copy(ts_g[0][:], ts_sb[:].indirect(list_half[0]))
-        nc.vector.quantize_mx(
-            out=q_codes[:].bitcast(FP8X4), scales=q_scales[:], in_=q_bf[:].rearrange("p q j -> p (q j)")
-        )
+        turned = [psum.tile([P, 4, P], F32, name=f"turned{u}") for u in range(2)]
+        early = reuse.tile([P, 16 * EARLY], BF16, name="early", offset=9216, align_bytes=64)
+        word_floats = words[:].bitcast(F32)
+
+        def turn_words(u):
+            for s in range(4):
+                nc.tensor.transpose(turned[u][:, s, :], word_floats[:, u, s // 2, :, s % 2], ident[:])
+
+        def copy_values(values, u, part):
+            bank = turned[u][:].rearrange("p s m -> p (s m)").bitcast(BF16)
+            nc.scalar.copy(
+                values[:].rearrange("p (m u j s) -> p u m j s", u=2, j=2, s=4)[:, u],
+                bank.rearrange("p (s m j) -> p m j s", s=4, j=2)[:, part],
+            )
+
+        turn_words(0)
         latents = [keep.tile([P, 2, P, 2], U32, name=f"latents{h}", align_bytes=64) for h in range(2)]
         for h in range(2):
             nc.vector.tensor_copy(
@@ -98,6 +115,10 @@ def tile_attend_x_mla_append256_topk_kernel(tc, qT, cT, new_cT, ts, ch, offs, sl
             )
             nc.scalar.copy(latents[h][:], words[:].rearrange("p u v m j -> p v (m j) u")[:, :, h * P : (h + 1) * P, :])
         nc.vector.tensor_copy(ts_g[1][:], ts_sb[:].indirect(list_half[1]))
+
+        nc.vector.quantize_mx(
+            out=q_codes[:].bitcast(FP8X4), scales=q_scales[:], in_=q_bf[:].rearrange("p q j -> p (q j)")
+        )
 
         k_codes = [keep.tile([P, HALF], U32, name=f"k_codes{h}", align_bytes=64) for h in range(2)]
         k_scales = [keep.tile([P, HALF], U8, name=f"k_scales{h}", align_bytes=64) for h in range(2)]
@@ -118,22 +139,11 @@ def tile_attend_x_mla_append256_topk_kernel(tc, qT, cT, new_cT, ts, ch, offs, sl
                 stop=True,
             )
 
-        turned = [psum.tile([P, 4, P], F32, name=f"turned{u}") for u in range(2)]
-        values = keep.tile([P, 4 * D], BF16, name="values", align_bytes=64)
-        value_view = values[:].rearrange("p (m u j s) -> p u m j s", u=2, j=2, s=4)
-        word_floats = words[:].bitcast(F32)
+        turn_words(1)
         for u in range(2):
-            for s in range(4):
-                nc.tensor.transpose(turned[u][:, s, :], word_floats[:, u, s // 2, :, s % 2], ident[:])
-        for h in range(2):
-            part = slice(h * 64, (h + 1) * 64)
-            for u in range(2):
-                bank = turned[u][:].rearrange("p s m -> p (s m)").bitcast(BF16)
-                nc.scalar.copy(
-                    value_view[:, u, part], bank.rearrange("p (s m j) -> p m j s", s=4, j=2)[:, part]
-                )
+            copy_values(early, u, slice(0, EARLY))
 
-        a = keep.tile([P, 2, N // 4, 2], F32, name="a")
+        a = keep.tile([P, 2, N // 4, 2], F32, name="a", tag="a", align_bytes=64)
         neg_m = keep.tile([P, 1], F32, name="neg_m")
         ts_view = [ts_g[h][:].rearrange("p (m v j) -> p v m j", v=2, j=2) for h in range(2)]
         for h in range(2):
@@ -162,7 +172,13 @@ def tile_attend_x_mla_append256_topk_kernel(tc, qT, cT, new_cT, ts, ch, offs, sl
             nc.tensor.transpose(w_turned[:, u, :], w_words[:, u * P : (u + 1) * P], ident[:])
         v_codes = keep.tile([P, D], U32, name="v_codes", tag="prob1", align_bytes=64)
         v_scales = keep.tile([P, D], U8, name="v_scales", align_bytes=64)
-        nc.vector.quantize_mx(out=v_codes[:].bitcast(FP8X4), scales=v_scales[:], in_=values[:])
+        late = keep.tile([P, 16 * (P - EARLY)], BF16, name="late", tag="a", align_bytes=64)
+        for u in range(2):
+            copy_values(late, u, slice(EARLY, P))
+        for first, last, source in [(0, 256, early[:, 0:1024]), (256, 384, early[:, 1024:1536]), (384, 512, late[:])]:
+            nc.vector.quantize_mx(
+                out=v_codes[:, first:last].bitcast(FP8X4), scales=v_scales[:, first:last], in_=source
+            )
 
         w_grouped = keep.tile([P, 4 * NQ], BF16, name="w_grouped", align_bytes=64)
         nc.scalar.copy(
@@ -176,12 +192,12 @@ def tile_attend_x_mla_append256_topk_kernel(tc, qT, cT, new_cT, ts, ch, offs, sl
         w_scales = keep.tile([P, NQ], U8, name="w_scales", align_bytes=64)
         nc.vector.quantize_mx(out=w_codes[:].bitcast(FP8X4), scales=w_scales[:], in_=w_grouped[:])
 
-        y = [psum.tile([P, HALF], F32, name=f"y{h}") for h in range(2)]
         result = keep.tile([P, D], F32, name="result")
-        for h in range(2):
-            cols = slice(h * HALF, (h + 1) * HALF)
+        for first, last in [(0, 128), (128, 256), (256, 512)]:
+            cols = slice(first, last)
+            y = psum.tile([P, last - first], F32, name=f"y{first}")
             nc.tensor.matmul_mx(
-                out=y[h][:],
+                out=y[:],
                 lhsT=w_codes[:].bitcast(FP8X4),
                 lhsT_scale=w_scales[:],
                 rhs=v_codes[:, cols].bitcast(FP8X4),
@@ -189,5 +205,6 @@ def tile_attend_x_mla_append256_topk_kernel(tc, qT, cT, new_cT, ts, ch, offs, sl
                 start=True,
                 stop=True,
             )
-            nc.vector.scalar_tensor_tensor(result[:, cols], y[h][:], inv[:], ch_sb[:, cols], MULT, MULT)
-            nc.sync.dma_start(out[0][:, cols], result[:, cols])
+            nc.vector.scalar_tensor_tensor(result[:, cols], y[:], inv[:], ch_sb[:, cols], MULT, MULT)
+            if last % HALF == 0:
+                nc.sync.dma_start(out[0][:, last - HALF : last], result[:, last - HALF : last])

@@ -11,8 +11,7 @@ U8 = mybir.dt.uint8
 FP8X4 = mybir.dt.float8_e4m3fn_x4
 MULT = mybir.AluOpType.mult
 ADD = mybir.AluOpType.add
-MAX = mybir.AluOpType.max
-AX = mybir.AxisListType
+MIN = mybir.AluOpType.min
 ACT = mybir.ActivationFunctionType
 
 P = 128
@@ -41,7 +40,9 @@ def tile_attend_x_mla_append256_topk_kernel(tc, qT, cT, new_cT, ts, ch, offs, sl
         new_sb = [keep.tile([P, NEW], F32, name=f"new{t}") for t in range(3)]
         new_sb.append(reuse.tile([P, NEW], F32, name="new3", offset=3584, align_bytes=64))
         pool = [keep.tile([P, T], F32, name=f"pool{t}", align_bytes=64) for t in range(4)]
-        q_raw = keep.tile([P, 4, NQ], F32, name="q_raw")
+        shared = keep.tile([P, HALF + 4 * NQ], F32, name="shared")
+        q_raw = shared[:, HALF:].rearrange("p (j q) -> p j q", j=4)
+        ts_g = shared[:, 0:N]
         ts_sb = keep.tile([P, T], F32, name="ts_sb")
         ch_sb = keep.tile([P, D], F32, name="ch_sb")
 
@@ -56,7 +57,7 @@ def tile_attend_x_mla_append256_topk_kernel(tc, qT, cT, new_cT, ts, ch, offs, sl
             if t == 1:
                 nc.sync.dma_start(offs_sb[:], offs)
         nc.sync.dma_start(ts_sb[:], ts)
-        nc.sync.dma_start(q_raw[:], qT[0].rearrange("(p j) w -> p j w", j=4))
+        nc.sync.dma_start(q_raw, qT[0].rearrange("(p j) w -> p j w", j=4))
         nc.sync.dma_start(ch_sb[:], ch)
 
         warm = keep.tile([P, 1], F32, name="warm")
@@ -70,7 +71,7 @@ def tile_attend_x_mla_append256_topk_kernel(tc, qT, cT, new_cT, ts, ch, offs, sl
         q_bf = keep.tile([P, NQ, 4], BF16, name="q_bf", align_bytes=64)
         q_codes = keep.tile([P, NQ], U32, name="q_codes", align_bytes=64)
         q_scales = keep.tile([P, NQ], U8, name="q_scales", align_bytes=64)
-        nc.scalar.activation(out=q_bf[:], in_=q_raw[:].rearrange("p j q -> p q j"), func=ACT.Copy)
+        nc.scalar.activation(out=q_bf[:], in_=q_raw.rearrange("p j q -> p q j"), func=ACT.Copy)
 
         pairs = [
             keep.tile([P, 2 * T], BF16, name="pairs0", align_bytes=64),
@@ -82,15 +83,11 @@ def tile_attend_x_mla_append256_topk_kernel(tc, qT, cT, new_cT, ts, ch, offs, sl
             nc.scalar.activation(out=place, in_=pool[t][:], func=ACT.Copy)
 
         words = reuse.tile([P, 2, 2, P, 2], U32, name="words", offset=0, align_bytes=64)
-        ts_g = [
-            keep.tile([P, HALF], F32, name="ts_g0", align_bytes=64),
-            reuse.tile([P, HALF], F32, name="ts_g1", offset=8192, align_bytes=64),
-        ]
         list_half = [offs_sb[:, 16 * h : 16 * (h + 1)] for h in range(2)]
         nc.vector.tensor_copy(
             words[:, 0].rearrange("p v m j -> p m v j"), pairs[0][:].bitcast(U32).indirect(offs_sb[:])
         )
-        nc.vector.tensor_copy(ts_g[0][:], ts_sb[:].indirect(list_half[0]))
+        nc.vector.tensor_copy(ts_g[:, 0:HALF], ts_sb[:].indirect(list_half[0]))
         turned = [psum.tile([P, 4, P], F32, name=f"turned{u}") for u in range(2)]
         early = reuse.tile([P, 16 * EARLY], BF16, name="early", offset=9216, align_bytes=64)
         word_floats = words[:].bitcast(F32)
@@ -114,7 +111,7 @@ def tile_attend_x_mla_append256_topk_kernel(tc, qT, cT, new_cT, ts, ch, offs, sl
                 pairs[1][:].bitcast(U32).indirect(list_half[h]),
             )
             nc.scalar.copy(latents[h][:], words[:].rearrange("p u v m j -> p v (m j) u")[:, :, h * P : (h + 1) * P, :])
-        nc.vector.tensor_copy(ts_g[1][:], ts_sb[:].indirect(list_half[1]))
+        nc.vector.tensor_copy(ts_g[:, HALF:N], ts_sb[:].indirect(list_half[1]))
 
         nc.vector.quantize_mx(
             out=q_codes[:].bitcast(FP8X4), scales=q_scales[:], in_=q_bf[:].rearrange("p q j -> p (q j)")
@@ -122,7 +119,7 @@ def tile_attend_x_mla_append256_topk_kernel(tc, qT, cT, new_cT, ts, ch, offs, sl
 
         k_codes = [keep.tile([P, HALF], U32, name=f"k_codes{h}", align_bytes=64) for h in range(2)]
         k_scales = [keep.tile([P, HALF], U8, name=f"k_scales{h}", align_bytes=64) for h in range(2)]
-        scores = [psum.tile([P, HALF], F32, name=f"scores{h}") for h in range(2)]
+        scores = [psum.tile([P, N], F32, name=f"scores{h}", tag=f"scores{h}") for h in range(2)]
         for h in range(2):
             nc.vector.quantize_mx(
                 out=k_codes[h][:].bitcast(FP8X4),
@@ -130,7 +127,7 @@ def tile_attend_x_mla_append256_topk_kernel(tc, qT, cT, new_cT, ts, ch, offs, sl
                 in_=latents[h][:].rearrange("p v n u -> p (v n u)").bitcast(BF16),
             )
             nc.tensor.matmul_mx(
-                out=scores[h][:],
+                out=scores[h][:, 0:HALF],
                 lhsT=q_codes[:].bitcast(FP8X4),
                 lhsT_scale=q_scales[:],
                 rhs=k_codes[h][:].bitcast(FP8X4),
@@ -143,54 +140,67 @@ def tile_attend_x_mla_append256_topk_kernel(tc, qT, cT, new_cT, ts, ch, offs, sl
         for u in range(2):
             copy_values(early, u, slice(0, EARLY))
 
-        a = keep.tile([P, 2, N // 4, 2], F32, name="a", tag="a", align_bytes=64)
+        a = reuse.tile([P, 2, N // 4, 2], F32, name="a", offset=16384, align_bytes=64)
+        neg_a = keep.tile([P, 2, N // 4, 2], F32, name="neg_a", tag="neg_a", align_bytes=64)
         neg_m = keep.tile([P, 1], F32, name="neg_m")
-        ts_view = [ts_g[h][:].rearrange("p (m v j) -> p v m j", v=2, j=2) for h in range(2)]
+        ts_view = ts_g.rearrange("p (m v j) -> p v m j", v=2, j=2)
         for h in range(2):
+            part = slice(h * 64, (h + 1) * 64)
             nc.vector.tensor_tensor(
-                a[:, :, h * 64 : (h + 1) * 64, :],
-                scores[h][:].rearrange("p (v m j) -> p v m j", v=2, j=2),
-                ts_view[h],
+                a[:, :, part, :],
+                scores[h][:, 0:HALF].rearrange("p (v m j) -> p v m j", v=2, j=2),
+                ts_view[:, :, part, :],
                 MULT,
             )
-        nc.vector.tensor_reduce(
-            out=neg_m[:], in_=a[:].rearrange("p v m j -> p (v m j)"), axis=AX.X, op=MAX, negate=True
-        )
+        nc.vector.tensor_scalar(neg_a[:], a[:], -1.0, None, MULT, MIN, accum_out=neg_m[:])
 
-        prob = [keep.tile([P, N // 4, 2], F32, name=f"prob{u}", tag=f"prob{u}", align_bytes=64) for u in range(2)]
-        sums = keep.tile([P, 2], F32, name="sums")
-        w = keep.tile([P, 2, N // 4, 2], BF16, name="w", align_bytes=64)
-        w_turned = psum.tile([P, 2, P], F32, name="w_turned")
-        w_words = w[:].rearrange("p u m j -> p (u m j)").bitcast(F32)
-        for u in range(2):
-            nc.scalar.activation(
-                out=prob[u][:], in_=a[:, u], func=ACT.Exp, bias=neg_m[:], scale=1.0, accum_out=sums[:, u : u + 1]
+        ts_turned = psum.tile([P, N], F32, name="ts_turned", tag="scores0")
+        for s in range(4):
+            nc.tensor.transpose(
+                ts_turned[:, s * P : (s + 1) * P], ts_g.rearrange("p (m s) -> p s m", s=4)[:, s, :], ident[:]
             )
-            for h in range(2):
-                part = slice(h * 64, (h + 1) * 64)
-                nc.vector.tensor_tensor(w[:, u, part], prob[u][:, part], ts_view[h][:, u], MULT)
-            nc.tensor.transpose(w_turned[:, u, :], w_words[:, u * P : (u + 1) * P], ident[:])
-        v_codes = keep.tile([P, D], U32, name="v_codes", tag="prob1", align_bytes=64)
+        ts_col = reuse.tile([P, 4], F32, name="ts_col", offset=16384, align_bytes=64)
+        nc.vector.tensor_copy(ts_col[:], ts_turned[:].rearrange("p (s q) -> p s q", s=4)[:, :, 0])
+
+        v_codes = reuse.tile([P, D], U32, name="v_codes", offset=17408, align_bytes=64)
         v_scales = keep.tile([P, D], U8, name="v_scales", align_bytes=64)
-        late = keep.tile([P, 16 * (P - EARLY)], BF16, name="late", tag="a", align_bytes=64)
-        for u in range(2):
-            copy_values(late, u, slice(EARLY, P))
-        for first, last, source in [(0, 256, early[:, 0:1024]), (256, 384, early[:, 1024:1536]), (384, 512, late[:])]:
+
+        def quantize_values(first, last, source):
             nc.vector.quantize_mx(
                 out=v_codes[:, first:last].bitcast(FP8X4), scales=v_scales[:, first:last], in_=source
             )
 
-        w_grouped = keep.tile([P, 4 * NQ], BF16, name="w_grouped", align_bytes=64)
-        nc.scalar.copy(
-            w_grouped[:].bitcast(F32).rearrange("p (q u) -> p q u", u=2), w_turned[:].rearrange("p u q -> p q u")
-        )
+        quantize_values(0, 256, early[:, 0:1024])
+        quantize_values(256, 384, early[:, 1024:1536])
+
+        prob = keep.tile([P, 2, N // 4, 2], F32, name="prob")
+        sums = keep.tile([P, 2], F32, name="sums")
+        p_turned = psum.tile([P, 4, NQ], F32, name="p_turned")
+        for v in range(2):
+            nc.scalar.activation(
+                out=prob[:, v], in_=neg_a[:, v], func=ACT.Exp, bias=neg_m[:], scale=-1.0, accum_out=sums[:, v : v + 1]
+            )
+            for j in range(2):
+                nc.tensor.transpose(p_turned[:, 2 * v + j, :], prob[:, v, :, j], ident[:])
+        late = keep.tile([P, 16 * (P - EARLY)], BF16, name="late", tag="neg_a", align_bytes=64)
+        for u in range(2):
+            copy_values(late, u, slice(EARLY, P))
+
         total = keep.tile([P, 1], F32, name="total")
         inv = keep.tile([P, 1], F32, name="inv")
         nc.vector.tensor_tensor(total[:], sums[:, 0:1], sums[:, 1:2], ADD)
         nc.vector.reciprocal(inv[:], total[:])
+        w_grouped = keep.tile([P, NQ, 4], BF16, name="w_grouped", align_bytes=64)
+        nc.vector.tensor_tensor(
+            w_grouped[:],
+            p_turned[:].rearrange("p s q -> p q s"),
+            ts_col[:].unsqueeze(1).to_broadcast([P, NQ, 4]),
+            MULT,
+        )
         w_codes = keep.tile([P, NQ], U32, name="w_codes", align_bytes=64)
         w_scales = keep.tile([P, NQ], U8, name="w_scales", align_bytes=64)
-        nc.vector.quantize_mx(out=w_codes[:].bitcast(FP8X4), scales=w_scales[:], in_=w_grouped[:])
+        nc.vector.quantize_mx(out=w_codes[:].bitcast(FP8X4), scales=w_scales[:], in_=w_grouped[:].rearrange("p q s -> p (q s)"))
+        quantize_values(384, 512, late[:])
 
         result = keep.tile([P, D], F32, name="result")
         for first, last in [(0, 128), (128, 256), (256, 512)]:

@@ -37,8 +37,7 @@ def tile_attend_x_mla_append256_topk_kernel(tc, qT, cT, new_cT, ts, ch, offs, sl
         slots_sb = lists.tile([P, NEW // 16], U16, name="slots_sb")
         offs_sb = lists.tile([P, N // 16], U16, name="offs_sb")
 
-        new_sb = [keep.tile([P, NEW], F32, name=f"new{t}") for t in range(3)]
-        new_sb.append(reuse.tile([P, NEW], F32, name="new3", offset=3584, align_bytes=64))
+        new_sb = [keep.tile([P, NEW], F32, name=f"new{t}") for t in range(4)]
         pool = [keep.tile([P, T], F32, name=f"pool{t}", align_bytes=64) for t in range(4)]
         shared = keep.tile([P, HALF + 4 * NQ], F32, name="shared")
         q_raw = shared[:, HALF:].rearrange("p (j q) -> p j q", j=4)
@@ -54,8 +53,7 @@ def tile_attend_x_mla_append256_topk_kernel(tc, qT, cT, new_cT, ts, ch, offs, sl
             nc.sync.dma_start(new_sb[t][:], new_view[:, t, :])
             if t == 0:
                 nc.sync.dma_start(slots_sb[:], slots)
-            if t == 1:
-                nc.sync.dma_start(offs_sb[:], offs)
+        nc.sync.dma_start(offs_sb[:], offs)
         nc.sync.dma_start(ts_sb[:], ts)
         nc.sync.dma_start(q_raw, qT[0].rearrange("(p j) w -> p j w", j=4))
         nc.sync.dma_start(ch_sb[:], ch)
@@ -82,7 +80,7 @@ def tile_attend_x_mla_append256_topk_kernel(tc, qT, cT, new_cT, ts, ch, offs, sl
             place = pairs[t // 2][:].rearrange("p (n j) -> p n j", j=2)[:, :, t % 2]
             nc.scalar.activation(out=place, in_=pool[t][:], func=ACT.Copy)
 
-        words = reuse.tile([P, 2, 2, P, 2], U32, name="words", offset=0, align_bytes=64)
+        words = keep.tile([P, 2, 2, P, 2], U32, name="words", align_bytes=64)
         list_half = [offs_sb[:, 16 * h : 16 * (h + 1)] for h in range(2)]
         nc.vector.tensor_copy(
             words[:, 0].rearrange("p v m j -> p m v j"), pairs[0][:].bitcast(U32).indirect(offs_sb[:])

@@ -53,8 +53,8 @@ def tile_attend_x_mla_append256_topk_kernel(tc, qT, cT, new_cT, ts, ch, offs, sl
             nc.sync.dma_start(new_sb[t][:], new_view[:, t, :])
             if t == 0:
                 nc.sync.dma_start(slots_sb[:], slots)
-        nc.sync.dma_start(offs_sb[:], offs)
         nc.sync.dma_start(ts_sb[:], ts)
+        nc.sync.dma_start(offs_sb[:], offs)
         nc.sync.dma_start(q_raw, qT[0].rearrange("(p j) w -> p j w", j=4))
         nc.sync.dma_start(ch_sb[:], ch)
 
@@ -78,7 +78,10 @@ def tile_attend_x_mla_append256_topk_kernel(tc, qT, cT, new_cT, ts, ch, offs, sl
         for t in range(4):
             nc.vector.tensor_copy(pool[t][:].indirect(slots_sb[:]), new_sb[t][:])
             place = pairs[t // 2][:].rearrange("p (n j) -> p n j", j=2)[:, :, t % 2]
-            nc.scalar.activation(out=place, in_=pool[t][:], func=ACT.Copy)
+            share = T if t < 2 else 832
+            nc.scalar.activation(out=place[:, 0:share], in_=pool[t][:, 0:share], func=ACT.Copy)
+            if share < T:
+                nc.gpsimd.tensor_copy(place[:, share:T], pool[t][:, share:T])
 
         words = keep.tile([P, 2, 2, P, 2], U32, name="words", align_bytes=64)
         list_half = [offs_sb[:, 16 * h : 16 * (h + 1)] for h in range(2)]

@@ -11,7 +11,7 @@ U8 = mybir.dt.uint8
 FP8X4 = mybir.dt.float8_e4m3fn_x4
 MULT = mybir.AluOpType.mult
 ADD = mybir.AluOpType.add
-MIN = mybir.AluOpType.min
+MAX = mybir.AluOpType.max
 ACT = mybir.ActivationFunctionType
 
 P = 128
@@ -39,7 +39,7 @@ def tile_attend_x_mla_append256_topk_kernel(tc, qT, cT, new_cT, ts, ch, offs, sl
 
         new_sb = [keep.tile([P, NEW], F32, name=f"new{t}") for t in range(4)]
         pool = [keep.tile([P, T], F32, name=f"pool{t}", align_bytes=64) for t in range(4)]
-        shared = keep.tile([P, HALF + 4 * NQ], F32, name="shared")
+        shared = keep.tile([P, HALF + 4 * NQ], F32, name="shared", tag="shared", align_bytes=64)
         q_raw = shared[:, HALF:].rearrange("p (j q) -> p j q", j=4)
         ts_g = shared[:, 0:N]
         ts_sb = keep.tile([P, T], F32, name="ts_sb")
@@ -141,29 +141,28 @@ def tile_attend_x_mla_append256_topk_kernel(tc, qT, cT, new_cT, ts, ch, offs, sl
         for u in range(2):
             copy_values(early, u, slice(0, EARLY))
 
-        a = reuse.tile([P, 2, N // 4, 2], F32, name="a", offset=16384, align_bytes=64)
-        neg_a = keep.tile([P, 2, N // 4, 2], F32, name="neg_a", tag="neg_a", align_bytes=64)
+        a = keep.tile([P, 2, 2, N // 4], F32, name="a", tag="a", align_bytes=64)
         neg_m = keep.tile([P, 1], F32, name="neg_m")
         ts_view = ts_g.rearrange("p (m v j) -> p v m j", v=2, j=2)
         for h in range(2):
             part = slice(h * 64, (h + 1) * 64)
             nc.vector.tensor_tensor(
-                a[:, :, part, :],
+                a[:, :, :, part].rearrange("p v j m -> p v m j"),
                 scores[h][:, 0:HALF].rearrange("p (v m j) -> p v m j", v=2, j=2),
                 ts_view[:, :, part, :],
                 MULT,
             )
-        nc.vector.tensor_scalar(neg_a[:], a[:], -1.0, None, MULT, MIN, accum_out=neg_m[:])
+        nc.vector.tensor_reduce(neg_m[:], a[:].rearrange("p v j m -> p (v j m)"), mybir.AxisListType.X, MAX, negate=True)
 
         ts_turned = psum.tile([P, N], F32, name="ts_turned", tag="scores0")
         for s in range(4):
             nc.tensor.transpose(
                 ts_turned[:, s * P : (s + 1) * P], ts_g.rearrange("p (m s) -> p s m", s=4)[:, s, :], ident[:]
             )
-        ts_col = reuse.tile([P, 4], F32, name="ts_col", offset=16384, align_bytes=64)
+        ts_col = keep.tile([P, 4], F32, name="ts_col")
         nc.vector.tensor_copy(ts_col[:], ts_turned[:].rearrange("p (s q) -> p s q", s=4)[:, :, 0])
 
-        v_codes = reuse.tile([P, D], U32, name="v_codes", offset=17408, align_bytes=64)
+        v_codes = keep.tile([P, D], U32, name="v_codes", tag="shared", align_bytes=64)
         v_scales = keep.tile([P, D], U8, name="v_scales", align_bytes=64)
 
         def quantize_values(first, last, source):
@@ -174,16 +173,16 @@ def tile_attend_x_mla_append256_topk_kernel(tc, qT, cT, new_cT, ts, ch, offs, sl
         quantize_values(0, 256, early[:, 0:1024])
         quantize_values(256, 384, early[:, 1024:1536])
 
-        prob = keep.tile([P, 2, N // 4, 2], F32, name="prob")
+        prob = keep.tile([P, 2, 2, N // 4], F32, name="prob")
         sums = keep.tile([P, 2], F32, name="sums")
         p_turned = psum.tile([P, 4, NQ], F32, name="p_turned")
         for v in range(2):
             nc.scalar.activation(
-                out=prob[:, v], in_=neg_a[:, v], func=ACT.Exp, bias=neg_m[:], scale=-1.0, accum_out=sums[:, v : v + 1]
+                out=prob[:, v], in_=a[:, v], func=ACT.Exp, bias=neg_m[:], accum_out=sums[:, v : v + 1]
             )
             for j in range(2):
-                nc.tensor.transpose(p_turned[:, 2 * v + j, :], prob[:, v, :, j], ident[:])
-        late = keep.tile([P, 16 * (P - EARLY)], BF16, name="late", tag="neg_a", align_bytes=64)
+                nc.tensor.transpose(p_turned[:, 2 * v + j, :], prob[:, v, j, :], ident[:])
+        late = keep.tile([P, 16 * (P - EARLY)], BF16, name="late", tag="a", align_bytes=64)
         for u in range(2):
             copy_values(late, u, slice(EARLY, P))
 

@@ -21,7 +21,7 @@ N = 512
 D = 512
 NQ = 128
 HALF = 256
-EARLY = 96
+EARLY = 64
 
 FLOPS = 2 * NQ * N * D * 2
 
@@ -78,7 +78,7 @@ def tile_attend_x_mla_append256_topk_kernel(tc, qT, cT, new_cT, ts, ch, offs, sl
         for t in range(4):
             nc.vector.tensor_copy(pool[t][:].indirect(slots_sb[:]), new_sb[t][:])
             place = pairs[t // 2][:].rearrange("p (n j) -> p n j", j=2)[:, :, t % 2]
-            share = T if t < 2 else 832
+            share = T if t < 2 else 768
             nc.scalar.activation(out=place[:, 0:share], in_=pool[t][:, 0:share], func=ACT.Copy)
             if share < T:
                 nc.gpsimd.tensor_copy(place[:, share:T], pool[t][:, share:T])
@@ -170,8 +170,7 @@ def tile_attend_x_mla_append256_topk_kernel(tc, qT, cT, new_cT, ts, ch, offs, sl
                 out=v_codes[:, first:last].bitcast(FP8X4), scales=v_scales[:, first:last], in_=source
             )
 
-        quantize_values(0, 256, early[:, 0:1024])
-        quantize_values(256, 384, early[:, 1024:1536])
+        quantize_values(0, 4 * EARLY, early[:])
 
         prob = keep.tile([P, 2, 2, N // 4], F32, name="prob")
         sums = keep.tile([P, 2], F32, name="sums")
@@ -197,10 +196,10 @@ def tile_attend_x_mla_append256_topk_kernel(tc, qT, cT, new_cT, ts, ch, offs, sl
             ts_col[:].unsqueeze(1).to_broadcast([P, NQ, 4]),
             MULT,
         )
+        quantize_values(4 * EARLY, D, late[:])
         w_codes = keep.tile([P, NQ], U32, name="w_codes", align_bytes=64)
         w_scales = keep.tile([P, NQ], U8, name="w_scales", align_bytes=64)
         nc.vector.quantize_mx(out=w_codes[:].bitcast(FP8X4), scales=w_scales[:], in_=w_grouped[:].rearrange("p q s -> p (q s)"))
-        quantize_values(384, 512, late[:])
 
         result = keep.tile([P, D], F32, name="result")
         for first, last in [(0, 128), (128, 256), (256, 512)]:

@@ -50,9 +50,9 @@ def tile_attend_x_mla_append256_topk_kernel(tc, qT, cT, new_cT, ts, ch, offs, sl
 
         for t in range(4):
             nc.sync.dma_start(pool[t][:], pool_view[:, t, :])
-            nc.sync.dma_start(new_sb[t][:], new_view[:, t, :])
             if t == 0:
                 nc.sync.dma_start(slots_sb[:], slots)
+            nc.sync.dma_start(new_sb[t][:], new_view[:, t, :])
         nc.sync.dma_start(ts_sb[:], ts)
         nc.sync.dma_start(offs_sb[:], offs)
         nc.sync.dma_start(q_raw, qT[0].rearrange("(p j) w -> p j w", j=4))
@@ -172,22 +172,21 @@ def tile_attend_x_mla_append256_topk_kernel(tc, qT, cT, new_cT, ts, ch, offs, sl
 
         quantize_values(0, 4 * EARLY, early[:])
 
-        prob = keep.tile([P, 2, 2, N // 4], F32, name="prob")
-        sums = keep.tile([P, 2], F32, name="sums")
+        prob = keep.tile([P, 4, N // 4], F32, name="prob")
+        sums = keep.tile([P, 4], F32, name="sums")
         p_turned = psum.tile([P, 4, NQ], F32, name="p_turned")
-        for v in range(2):
+        for s in range(4):
             nc.scalar.activation(
-                out=prob[:, v], in_=a[:, v], func=ACT.Exp, bias=neg_m[:], accum_out=sums[:, v : v + 1]
+                out=prob[:, s], in_=a[:, s // 2, s % 2], func=ACT.Exp, bias=neg_m[:], accum_out=sums[:, s : s + 1]
             )
-            for j in range(2):
-                nc.tensor.transpose(p_turned[:, 2 * v + j, :], prob[:, v, j, :], ident[:])
+            nc.tensor.transpose(p_turned[:, s, :], prob[:, s, :], ident[:])
         late = keep.tile([P, 16 * (P - EARLY)], BF16, name="late", tag="a", align_bytes=64)
         for u in range(2):
             copy_values(late, u, slice(EARLY, P))
 
         total = keep.tile([P, 1], F32, name="total")
         inv = keep.tile([P, 1], F32, name="inv")
-        nc.vector.tensor_tensor(total[:], sums[:, 0:1], sums[:, 1:2], ADD)
+        nc.vector.tensor_reduce(total[:], sums[:], mybir.AxisListType.X, ADD)
         nc.vector.reciprocal(inv[:], total[:])
         w_grouped = keep.tile([P, NQ, 4], BF16, name="w_grouped", align_bytes=64)
         nc.vector.tensor_tensor(

@@ -105,34 +105,41 @@ def tile_attend_x_mla_append256_topk_kernel(tc, qT, cT, new_cT, ts, ch, offs, sl
             )
 
         turn_words(0)
-        latents = [keep.tile([P, 2, P, 2], U32, name=f"latents{h}", align_bytes=64) for h in range(2)]
+        pieces = [(0, 64), (64, 96), (96, 128)]
+        latents = [
+            keep.tile([P, 2, 2 * (last - first), 2], U32, name=f"latents{first}", align_bytes=64) for first, last in pieces
+        ]
         for h in range(2):
             nc.vector.tensor_copy(
                 words[:, 1, :, h * 64 : (h + 1) * 64, :].rearrange("p v m j -> p m v j"),
                 pairs[1][:].bitcast(U32).indirect(list_half[h]),
             )
-            nc.scalar.copy(latents[h][:], words[:].rearrange("p u v m j -> p v (m j) u")[:, :, h * P : (h + 1) * P, :])
+        for (first, last), target in zip(pieces, latents):
+            nc.scalar.copy(target[:], words[:].rearrange("p u v m j -> p v (m j) u")[:, :, 2 * first : 2 * last, :])
         nc.vector.tensor_copy(ts_g[:, HALF:N], ts_sb[:].indirect(list_half[1]))
 
         nc.vector.quantize_mx(
             out=q_codes[:].bitcast(FP8X4), scales=q_scales[:], in_=q_bf[:].rearrange("p q j -> p (q j)")
         )
 
-        k_codes = [keep.tile([P, HALF], U32, name=f"k_codes{h}", align_bytes=64) for h in range(2)]
-        k_scales = [keep.tile([P, HALF], U8, name=f"k_scales{h}", align_bytes=64) for h in range(2)]
-        scores = [psum.tile([P, N], F32, name=f"scores{h}", tag=f"scores{h}") for h in range(2)]
-        for h in range(2):
+        scores = []
+        for h, (first, last) in enumerate(pieces):
+            width = 4 * (last - first)
+            k_codes = keep.tile([P, width], U32, name=f"k_codes{h}", align_bytes=64)
+            k_scales = keep.tile([P, width], U8, name=f"k_scales{h}", align_bytes=64)
+            bank = psum.tile([P, N], F32, name=f"scores{h}", tag=f"scores{h}")
+            scores.append(bank)
             nc.vector.quantize_mx(
-                out=k_codes[h][:].bitcast(FP8X4),
-                scales=k_scales[h][:],
+                out=k_codes[:].bitcast(FP8X4),
+                scales=k_scales[:],
                 in_=latents[h][:].rearrange("p v n u -> p (v n u)").bitcast(BF16),
             )
             nc.tensor.matmul_mx(
-                out=scores[h][:, 0:HALF],
+                out=bank[:, 0:width],
                 lhsT=q_codes[:].bitcast(FP8X4),
                 lhsT_scale=q_scales[:],
-                rhs=k_codes[h][:].bitcast(FP8X4),
-                rhs_scale=k_scales[h][:],
+                rhs=k_codes[:].bitcast(FP8X4),
+                rhs_scale=k_scales[:],
                 start=True,
                 stop=True,
             )
@@ -144,11 +151,11 @@ def tile_attend_x_mla_append256_topk_kernel(tc, qT, cT, new_cT, ts, ch, offs, sl
         a = keep.tile([P, 2, 2, N // 4], F32, name="a", tag="a", align_bytes=64)
         neg_m = keep.tile([P, 1], F32, name="neg_m")
         ts_view = ts_g.rearrange("p (m v j) -> p v m j", v=2, j=2)
-        for h in range(2):
-            part = slice(h * 64, (h + 1) * 64)
+        for h, (first, last) in enumerate(pieces):
+            part = slice(first, last)
             nc.vector.tensor_tensor(
                 a[:, :, :, part].rearrange("p v j m -> p v m j"),
-                scores[h][:, 0:HALF].rearrange("p (v m j) -> p v m j", v=2, j=2),
+                scores[h][:, 0 : 4 * (last - first)].rearrange("p (v m j) -> p v m j", v=2, j=2),
                 ts_view[:, :, part, :],
                 MULT,
             )
@@ -203,7 +210,7 @@ def tile_attend_x_mla_append256_topk_kernel(tc, qT, cT, new_cT, ts, ch, offs, sl
         result = keep.tile([P, D], F32, name="result")
         for first, last in [(0, 128), (128, 256), (256, 512)]:
             cols = slice(first, last)
-            y = psum.tile([P, last - first], F32, name=f"y{first}")
+            y = psum.tile([P, last - first], F32, name=f"y{first}", tag="scores2" if first == 256 else f"y{first}")
             nc.tensor.matmul_mx(
                 out=y[:],
                 lhsT=w_codes[:].bitcast(FP8X4),

@@ -21,7 +21,7 @@ N = 512
 D = 512
 NQ = 128
 HALF = 256
-EARLY = 64
+EARLY = 96
 
 FLOPS = 2 * NQ * N * D * 2
 
@@ -78,7 +78,7 @@ def tile_attend_x_mla_append256_topk_kernel(tc, qT, cT, new_cT, ts, ch, offs, sl
         for t in range(4):
             nc.vector.tensor_copy(pool[t][:].indirect(slots_sb[:]), new_sb[t][:])
             place = pairs[t // 2][:].rearrange("p (n j) -> p n j", j=2)[:, :, t % 2]
-            share = T if t < 2 else 768
+            share = T if t < 2 else 736
             nc.scalar.activation(out=place[:, 0:share], in_=pool[t][:, 0:share], func=ACT.Copy)
             if share < T:
                 nc.gpsimd.tensor_copy(place[:, share:T], pool[t][:, share:T])
@@ -177,7 +177,8 @@ def tile_attend_x_mla_append256_topk_kernel(tc, qT, cT, new_cT, ts, ch, offs, sl
                 out=v_codes[:, first:last].bitcast(FP8X4), scales=v_scales[:, first:last], in_=source
             )
 
-        quantize_values(0, 4 * EARLY, early[:])
+        quantize_values(0, 256, early[:, 0:1024])
+        quantize_values(256, 384, early[:, 1024:1536])
 
         prob = keep.tile([P, 4, N // 4], F32, name="prob")
         sums = keep.tile([P, 4], F32, name="sums")
@@ -196,16 +197,23 @@ def tile_attend_x_mla_append256_topk_kernel(tc, qT, cT, new_cT, ts, ch, offs, sl
         nc.vector.tensor_reduce(total[:], sums[:], mybir.AxisListType.X, ADD)
         nc.vector.reciprocal(inv[:], total[:])
         w_grouped = keep.tile([P, NQ, 4], BF16, name="w_grouped", align_bytes=64)
-        nc.vector.tensor_tensor(
-            w_grouped[:],
-            p_turned[:].rearrange("p s q -> p q s"),
-            ts_col[:].unsqueeze(1).to_broadcast([P, NQ, 4]),
-            MULT,
-        )
-        quantize_values(4 * EARLY, D, late[:])
+        halves = [slice(0, NQ // 2), slice(NQ // 2, NQ)]
+        for rows in halves:
+            nc.vector.tensor_tensor(
+                w_grouped[:, rows, :],
+                p_turned[:].rearrange("p s q -> p q s")[:, rows, :],
+                ts_col[:].unsqueeze(1).to_broadcast([P, NQ // 2, 4]),
+                MULT,
+            )
         w_codes = keep.tile([P, NQ], U32, name="w_codes", align_bytes=64)
         w_scales = keep.tile([P, NQ], U8, name="w_scales", align_bytes=64)
-        nc.vector.quantize_mx(out=w_codes[:].bitcast(FP8X4), scales=w_scales[:], in_=w_grouped[:].rearrange("p q s -> p (q s)"))
+        for rows in halves:
+            nc.vector.quantize_mx(
+                out=w_codes[:, rows].bitcast(FP8X4),
+                scales=w_scales[:, rows],
+                in_=w_grouped[:, rows, :].rearrange("p q s -> p (q s)"),
+            )
+        quantize_values(4 * EARLY, D, late[:])
 
         result = keep.tile([P, D], F32, name="result")
         for first, last in [(0, 128), (128, 256), (256, 512)]:

@@ -181,11 +181,11 @@ def tile_attend_x_mla_append256_topk_kernel(tc, qT, cT, new_cT, ts, ch, offs, sl
         quantize_values(256, 384, early[:, 1024:1536])
 
         prob = keep.tile([P, 4, N // 4], F32, name="prob")
-        sums = keep.tile([P, 4], F32, name="sums")
+        sums = keep.tile([P, 3], F32, name="sums")
         p_turned = psum.tile([P, 4, NQ], F32, name="p_turned")
         for s in range(4):
             nc.scalar.activation(
-                out=prob[:, s], in_=a[:, s // 2, s % 2], func=ACT.Exp, bias=neg_m[:], accum_out=sums[:, s : s + 1]
+                out=prob[:, s], in_=a[:, s // 2, s % 2], func=ACT.Exp, bias=neg_m[:], accum_out=sums[:, s - 1 : s] if s >= 2 else None
             )
             nc.tensor.transpose(p_turned[:, s, :], prob[:, s, :], ident[:])
         late = keep.tile([P, 16 * (P - EARLY)], BF16, name="late", tag="a", align_bytes=64)
@@ -194,8 +194,7 @@ def tile_attend_x_mla_append256_topk_kernel(tc, qT, cT, new_cT, ts, ch, offs, sl
 
         total = keep.tile([P, 1], F32, name="total")
         inv = keep.tile([P, 1], F32, name="inv")
-        nc.vector.tensor_reduce(total[:], sums[:], mybir.AxisListType.X, ADD)
-        nc.vector.reciprocal(inv[:], total[:])
+        nc.vector.tensor_reduce(sums[:, 0:1], prob[:, 0:2].rearrange("p s m -> p (s m)"), mybir.AxisListType.X, ADD)
         w_grouped = keep.tile([P, NQ, 4], BF16, name="w_grouped", align_bytes=64)
         halves = [slice(0, NQ // 2), slice(NQ // 2, NQ)]
         for rows in halves:
@@ -207,12 +206,18 @@ def tile_attend_x_mla_append256_topk_kernel(tc, qT, cT, new_cT, ts, ch, offs, sl
             )
         w_codes = keep.tile([P, NQ], U32, name="w_codes", align_bytes=64)
         w_scales = keep.tile([P, NQ], U8, name="w_scales", align_bytes=64)
-        for rows in halves:
+
+        def quantize_weights(rows):
             nc.vector.quantize_mx(
                 out=w_codes[:, rows].bitcast(FP8X4),
                 scales=w_scales[:, rows],
                 in_=w_grouped[:, rows, :].rearrange("p q s -> p (q s)"),
             )
+
+        quantize_weights(halves[0])
+        nc.vector.tensor_reduce(total[:], sums[:], mybir.AxisListType.X, ADD)
+        quantize_weights(halves[1])
+        nc.vector.reciprocal(inv[:], total[:])
         quantize_values(4 * EARLY, D, late[:])
 
         result = keep.tile([P, D], F32, name="result")

@@ -78,7 +78,7 @@ def tile_attend_x_mla_append256_topk_kernel(tc, qT, cT, new_cT, ts, ch, offs, sl
         for t in range(4):
             nc.vector.tensor_copy(pool[t][:].indirect(slots_sb[:]), new_sb[t][:])
             place = pairs[t // 2][:].rearrange("p (n j) -> p n j", j=2)[:, :, t % 2]
-            share = T if t < 2 else 736
+            share = T if t < 2 else 704
             nc.scalar.activation(out=place[:, 0:share], in_=pool[t][:, 0:share], func=ACT.Copy)
             if share < T:
                 nc.gpsimd.tensor_copy(place[:, share:T], pool[t][:, share:T])

@@ -31,30 +31,39 @@ def tile_attend_x_mla_append256_topk_kernel(tc, qT, cT, new_cT, ts, ch, offs, sl
     with ExitStack() as ctx:
         lists = ctx.enter_context(tc.tile_pool(name="lists", bufs=1))
         keep = ctx.enter_context(tc.tile_pool(name="keep", bufs=1))
-        reuse = ctx.enter_context(tc.tile_pool(name="reuse", bufs=1))
         psum = ctx.enter_context(tc.psum_pool(name="psum", bufs=1))
 
         slots_sb = lists.tile([P, NEW // 16], U16, name="slots_sb")
         offs_sb = lists.tile([P, N // 16], U16, name="offs_sb")
 
-        new_sb = [keep.tile([P, NEW], F32, name=f"new{t}") for t in range(4)]
-        pool = [keep.tile([P, T], F32, name=f"pool{t}", align_bytes=64) for t in range(4)]
-        shared = keep.tile([P, HALF + 4 * NQ], F32, name="shared", tag="shared", align_bytes=64)
-        q_raw = shared[:, HALF:].rearrange("p (j q) -> p j q", j=4)
-        ts_g = shared[:, 0:N]
+        new_sb = [keep.tile([P, NEW], F32, name=f"new{t}", tag=f"new{t}") for t in range(4)]
+        pool = [
+            keep.tile([P, T], F32, name="pool0", align_bytes=64),
+            keep.tile([P, T], F32, name="pool1", align_bytes=64),
+            keep.tile([P, T], F32, name="pool2", align_bytes=64),
+            keep.tile([P, T], F32, name="pool3", tag="pool3", align_bytes=64),
+        ]
+        words_flat = keep.tile([P, 2 * N], U32, name="words_flat", align_bytes=64)
+        words = words_flat[:].rearrange("p (u v m j) -> p u v m j", u=2, v=2, j=2)
+        halves16 = words_flat[:].bitcast(BF16).rearrange("p (u v m j h) -> p u h m v j", u=2, v=2, j=2, h=2)
+        q_raw = words_flat[:, N : 2 * N].bitcast(F32).rearrange("p (j q) -> p j q", j=4)
         ts_sb = keep.tile([P, T], F32, name="ts_sb")
         ch_sb = keep.tile([P, D], F32, name="ch_sb")
 
         new_view = new_cT.rearrange("(p j) w -> p j w", j=4)
         pool_view = cT.rearrange("(p j) w -> p j w", j=4)
 
-        for t in range(4):
-            nc.sync.dma_start(pool[t][:], pool_view[:, t, :])
-            if t == 0:
-                nc.sync.dma_start(slots_sb[:], slots)
-            nc.sync.dma_start(new_sb[t][:], new_view[:, t, :])
-        nc.sync.dma_start(ts_sb[:], ts)
+        nc.scalar.dma_start(ts_sb[P - 1 : P, :], ts[0:1, :])
         nc.sync.dma_start(offs_sb[:], offs)
+        nc.sync.dma_start(pool[0][:], pool_view[:, 0, :])
+        nc.sync.dma_start(slots_sb[:], slots)
+        nc.sync.dma_start(new_sb[0][:], new_view[:, 0, :])
+        nc.sync.dma_start(pool[1][:], pool_view[:, 1, :])
+        nc.sync.dma_start(new_sb[1][:], new_view[:, 1, :])
+        nc.sync.dma_start(pool[2][:], pool_view[:, 2, :])
+        nc.sync.dma_start(new_sb[2][:], new_view[:, 2, :])
+        nc.sync.dma_start(pool[3][:], pool_view[:, 3, :])
+        nc.sync.dma_start(new_sb[3][:], new_view[:, 3, :])
         nc.sync.dma_start(q_raw, qT[0].rearrange("(p j) w -> p j w", j=4))
         nc.sync.dma_start(ch_sb[:], ch)
 
@@ -66,32 +75,39 @@ def tile_attend_x_mla_append256_topk_kernel(tc, qT, cT, new_cT, ts, ch, offs, sl
         ident = keep.tile([P, P], F32, name="ident")
         make_identity(nc, ident[:])
 
+        nc.vector.memset(ts_sb[0 : P - 1, :], 0.0)
+        ts_row = keep.tile([P, N], F32, name="ts_row")
+        nc.vector.tensor_copy(ts_row[:], ts_sb[:].indirect(offs_sb[:]))
+        ts_turned = psum.tile([P, 4, P], F32, name="ts_turned", tag="p_turned")
+        for s in range(4):
+            nc.tensor.transpose(ts_turned[:, s, :], ts_row[:].rearrange("p (m s) -> p s m", s=4)[:, s, :], ident[:])
+
         q_bf = keep.tile([P, NQ, 4], BF16, name="q_bf", align_bytes=64)
         q_codes = keep.tile([P, NQ], U32, name="q_codes", align_bytes=64)
         q_scales = keep.tile([P, NQ], U8, name="q_scales", align_bytes=64)
-        nc.scalar.activation(out=q_bf[:], in_=q_raw.rearrange("p j q -> p q j"), func=ACT.Copy)
 
-        pairs = [
-            keep.tile([P, 2 * T], BF16, name="pairs0", align_bytes=64),
-            reuse.tile([P, 2 * T], BF16, name="pairs1", offset=8192, align_bytes=64),
-        ]
+        nc.gpsimd.tensor_copy(q_bf[:], q_raw.rearrange("p j q -> p q j"))
+
         for t in range(4):
             nc.vector.tensor_copy(pool[t][:].indirect(slots_sb[:]), new_sb[t][:])
-            place = pairs[t // 2][:].rearrange("p (n j) -> p n j", j=2)[:, :, t % 2]
-            share = T if t < 2 else 704
-            nc.scalar.activation(out=place[:, 0:share], in_=pool[t][:, 0:share], func=ACT.Copy)
-            if share < T:
-                nc.gpsimd.tensor_copy(place[:, share:T], pool[t][:, share:T])
+        rounded = [keep.tile([P, T], BF16, name=f"rounded{t}", align_bytes=64) for t in range(2)]
+        ts_col = keep.tile([P, 4], F32, name="ts_col")
+        ts_spread = psum.tile([P, 4, P], F32, name="ts_spread", tag="turned0")
+        ts_g = keep.tile([P, 4, P], F32, name="ts_g", tag="ts_g", align_bytes=64)
+        for t in range(2):
+            nc.scalar.activation(out=rounded[t][:], in_=pool[t][:], func=ACT.Copy)
+            if t == 0:
+                nc.vector.tensor_copy(ts_col[:], ts_turned[:, :, P - 1])
+                for s in range(4):
+                    nc.tensor.transpose(ts_spread[:, s, :], ts_col[:, s : s + 1].to_broadcast([P, P]), ident[:])
+            else:
+                nc.scalar.copy(ts_g[:], ts_spread[:])
+            nc.scalar.activation(out=halves16[:, 0, t], in_=rounded[t][:].indirect(offs_sb[:]), func=ACT.Copy)
+        nc.vector.tensor_copy(halves16[:, 1, 0], pool[2][:].indirect(offs_sb[:]))
 
-        words = keep.tile([P, 2, 2, P, 2], U32, name="words", align_bytes=64)
-        list_half = [offs_sb[:, 16 * h : 16 * (h + 1)] for h in range(2)]
-        nc.vector.tensor_copy(
-            words[:, 0].rearrange("p v m j -> p m v j"), pairs[0][:].bitcast(U32).indirect(offs_sb[:])
-        )
-        nc.vector.tensor_copy(ts_g[:, 0:HALF], ts_sb[:].indirect(list_half[0]))
-        turned = [psum.tile([P, 4, P], F32, name=f"turned{u}") for u in range(2)]
-        early = reuse.tile([P, 16 * EARLY], BF16, name="early", offset=9216, align_bytes=64)
-        word_floats = words[:].bitcast(F32)
+        turned = [psum.tile([P, 4, P], F32, name=f"turned{u}", tag=f"turned{u}") for u in range(2)]
+        early = keep.tile([P, 16 * EARLY], BF16, name="early", tag="pool3", align_bytes=64)
+        word_floats = words.bitcast(F32)
 
         def turn_words(u):
             for s in range(4):
@@ -105,37 +121,35 @@ def tile_attend_x_mla_append256_topk_kernel(tc, qT, cT, new_cT, ts, ch, offs, sl
             )
 
         turn_words(0)
-        pieces = [(0, 64), (64, 96), (96, 128)]
+        pieces = [(0, 32), (32, 64), (64, 96), (96, 128)]
         latents = [
-            keep.tile([P, 2, 2 * (last - first), 2], U32, name=f"latents{first}", align_bytes=64) for first, last in pieces
+            keep.tile([P, 2, 2 * (last - first), 2], U32, name=f"latents{first}", tag=f"latents{first}", align_bytes=64) for first, last in pieces
         ]
-        for h in range(2):
+        for first, last in pieces:
             nc.vector.tensor_copy(
-                words[:, 1, :, h * 64 : (h + 1) * 64, :].rearrange("p v m j -> p m v j"),
-                pairs[1][:].bitcast(U32).indirect(list_half[h]),
+                halves16[:, 1, 1, first:last],
+                pool[3][:].indirect(offs_sb[:, first // 4 : last // 4]),
             )
         for (first, last), target in zip(pieces, latents):
-            nc.scalar.copy(target[:], words[:].rearrange("p u v m j -> p v (m j) u")[:, :, 2 * first : 2 * last, :])
-        nc.vector.tensor_copy(ts_g[:, HALF:N], ts_sb[:].indirect(list_half[1]))
+            nc.scalar.copy(target[:], words.rearrange("p u v m j -> p v (m j) u")[:, :, 2 * first : 2 * last, :])
 
         nc.vector.quantize_mx(
             out=q_codes[:].bitcast(FP8X4), scales=q_scales[:], in_=q_bf[:].rearrange("p q j -> p (q j)")
         )
 
-        scores = []
+        banks = [psum.tile([P, N], F32, name=f"scores{b}", tag=f"scores{b}") for b in range(3)]
+        scores = [banks[0][:, 0:P], banks[0][:, P : 2 * P], banks[1][:, 0:P], banks[2][:, 0:P]]
         for h, (first, last) in enumerate(pieces):
             width = 4 * (last - first)
             k_codes = keep.tile([P, width], U32, name=f"k_codes{h}", align_bytes=64)
             k_scales = keep.tile([P, width], U8, name=f"k_scales{h}", align_bytes=64)
-            bank = psum.tile([P, N], F32, name=f"scores{h}", tag=f"scores{h}")
-            scores.append(bank)
             nc.vector.quantize_mx(
                 out=k_codes[:].bitcast(FP8X4),
                 scales=k_scales[:],
                 in_=latents[h][:].rearrange("p v n u -> p (v n u)").bitcast(BF16),
             )
             nc.tensor.matmul_mx(
-                out=bank[:, 0:width],
+                out=scores[h],
                 lhsT=q_codes[:].bitcast(FP8X4),
                 lhsT_scale=q_scales[:],
                 rhs=k_codes[:].bitcast(FP8X4),
@@ -148,28 +162,20 @@ def tile_attend_x_mla_append256_topk_kernel(tc, qT, cT, new_cT, ts, ch, offs, sl
         for u in range(2):
             copy_values(early, u, slice(0, EARLY))
 
-        a = keep.tile([P, 2, 2, N // 4], F32, name="a", tag="a", align_bytes=64)
+        a = keep.tile([P, 2, 2, N // 4], F32, name="a", tag="latents96", align_bytes=64)
         neg_m = keep.tile([P, 1], F32, name="neg_m")
-        ts_view = ts_g.rearrange("p (m v j) -> p v m j", v=2, j=2)
+        ts_view = ts_g[:].rearrange("p (v j) m -> p v m j", v=2)
         for h, (first, last) in enumerate(pieces):
             part = slice(first, last)
             nc.vector.tensor_tensor(
                 a[:, :, :, part].rearrange("p v j m -> p v m j"),
-                scores[h][:, 0 : 4 * (last - first)].rearrange("p (v m j) -> p v m j", v=2, j=2),
+                scores[h].rearrange("p (v m j) -> p v m j", v=2, j=2),
                 ts_view[:, :, part, :],
                 MULT,
             )
         nc.vector.tensor_reduce(neg_m[:], a[:].rearrange("p v j m -> p (v j m)"), mybir.AxisListType.X, MAX, negate=True)
 
-        ts_turned = psum.tile([P, N], F32, name="ts_turned", tag="scores0")
-        for s in range(4):
-            nc.tensor.transpose(
-                ts_turned[:, s * P : (s + 1) * P], ts_g.rearrange("p (m s) -> p s m", s=4)[:, s, :], ident[:]
-            )
-        ts_col = keep.tile([P, 4], F32, name="ts_col")
-        nc.vector.tensor_copy(ts_col[:], ts_turned[:].rearrange("p (s q) -> p s q", s=4)[:, :, 0])
-
-        v_codes = keep.tile([P, D], U32, name="v_codes", tag="shared", align_bytes=64)
+        v_codes = keep.tile([P, D], U32, name="v_codes", tag="ts_g", align_bytes=64)
         v_scales = keep.tile([P, D], U8, name="v_scales", align_bytes=64)
 
         def quantize_values(first, last, source):
@@ -182,13 +188,13 @@ def tile_attend_x_mla_append256_topk_kernel(tc, qT, cT, new_cT, ts, ch, offs, sl
 
         prob = keep.tile([P, 4, N // 4], F32, name="prob")
         sums = keep.tile([P, 3], F32, name="sums")
-        p_turned = psum.tile([P, 4, NQ], F32, name="p_turned")
+        p_turned = psum.tile([P, 4, NQ], F32, name="p_turned", tag="p_turned")
         for s in range(4):
             nc.scalar.activation(
                 out=prob[:, s], in_=a[:, s // 2, s % 2], func=ACT.Exp, bias=neg_m[:], accum_out=sums[:, s - 1 : s] if s >= 2 else None
             )
             nc.tensor.transpose(p_turned[:, s, :], prob[:, s, :], ident[:])
-        late = keep.tile([P, 16 * (P - EARLY)], BF16, name="late", tag="a", align_bytes=64)
+        late = keep.tile([P, 16 * (P - EARLY)], BF16, name="late", tag="latents96", align_bytes=64)
         for u in range(2):
             copy_values(late, u, slice(EARLY, P))
 

@@ -21,7 +21,6 @@ N = 512
 D = 512
 NQ = 128
 HALF = 256
-EARLY = 96
 
 FLOPS = 2 * NQ * N * D * 2
 
@@ -44,8 +43,8 @@ def tile_attend_x_mla_append256_topk_kernel(tc, qT, cT, new_cT, ts, ch, offs, sl
             keep.tile([P, T], F32, name="pool3", tag="pool3", align_bytes=64),
         ]
         words_flat = keep.tile([P, 2 * N], U32, name="words_flat", align_bytes=64)
-        words = words_flat[:].rearrange("p (u v m j) -> p u v m j", u=2, v=2, j=2)
-        halves16 = words_flat[:].bitcast(BF16).rearrange("p (u v m j h) -> p u h m v j", u=2, v=2, j=2, h=2)
+        words = words_flat[:].rearrange("p (u s m) -> p u s m", u=2, s=4)
+        halves16 = words_flat[:].bitcast(BF16).rearrange("p (u s m h) -> p u h m s", u=2, s=4, h=2)
         q_raw = words_flat[:, N : 2 * N].bitcast(F32).rearrange("p (j q) -> p j q", j=4)
         ts_sb = keep.tile([P, T], F32, name="ts_sb")
         ch_sb = keep.tile([P, D], F32, name="ch_sb")
@@ -76,7 +75,7 @@ def tile_attend_x_mla_append256_topk_kernel(tc, qT, cT, new_cT, ts, ch, offs, sl
         make_identity(nc, ident[:])
 
         nc.vector.memset(ts_sb[0 : P - 1, :], 0.0)
-        ts_row = keep.tile([P, N], F32, name="ts_row")
+        ts_row = keep.tile([P, N], F32, name="ts_row", tag="rounded1", align_bytes=64)
         nc.vector.tensor_copy(ts_row[:], ts_sb[:].indirect(offs_sb[:]))
         ts_turned = psum.tile([P, 4, P], F32, name="ts_turned", tag="p_turned")
         for s in range(4):
@@ -90,14 +89,14 @@ def tile_attend_x_mla_append256_topk_kernel(tc, qT, cT, new_cT, ts, ch, offs, sl
 
         for t in range(4):
             nc.vector.tensor_copy(pool[t][:].indirect(slots_sb[:]), new_sb[t][:])
-        rounded = [keep.tile([P, T], BF16, name=f"rounded{t}", align_bytes=64) for t in range(2)]
+        rounded = [keep.tile([P, T], BF16, name=f"rounded{t}", tag=f"rounded{t}", align_bytes=64) for t in range(2)]
         ts_col = keep.tile([P, 4], F32, name="ts_col")
         ts_spread = psum.tile([P, 4, P], F32, name="ts_spread", tag="turned0")
         ts_g = keep.tile([P, 4, P], F32, name="ts_g", tag="ts_g", align_bytes=64)
         for t in range(2):
             nc.scalar.activation(out=rounded[t][:], in_=pool[t][:], func=ACT.Copy)
             if t == 0:
-                nc.vector.tensor_copy(ts_col[:], ts_turned[:, :, P - 1])
+                nc.scalar.copy(ts_col[:], ts_turned[:, :, P - 1])
                 for s in range(4):
                     nc.tensor.transpose(ts_spread[:, s, :], ts_col[:, s : s + 1].to_broadcast([P, P]), ident[:])
             else:
@@ -106,24 +105,24 @@ def tile_attend_x_mla_append256_topk_kernel(tc, qT, cT, new_cT, ts, ch, offs, sl
         nc.vector.tensor_copy(halves16[:, 1, 0], pool[2][:].indirect(offs_sb[:]))
 
         turned = [psum.tile([P, 4, P], F32, name=f"turned{u}", tag=f"turned{u}") for u in range(2)]
-        early = keep.tile([P, 16 * EARLY], BF16, name="early", tag="pool3", align_bytes=64)
+        values = keep.tile([P, 4 * D], BF16, name="values", tag="pool3", align_bytes=64)
         word_floats = words.bitcast(F32)
 
         def turn_words(u):
             for s in range(4):
-                nc.tensor.transpose(turned[u][:, s, :], word_floats[:, u, s // 2, :, s % 2], ident[:])
+                nc.tensor.transpose(turned[u][:, s, :], word_floats[:, u, s, :], ident[:])
 
-        def copy_values(values, u, part):
+        def copy_values(u):
             bank = turned[u][:].rearrange("p s m -> p (s m)").bitcast(BF16)
             nc.scalar.copy(
                 values[:].rearrange("p (m u j s) -> p u m j s", u=2, j=2, s=4)[:, u],
-                bank.rearrange("p (s m j) -> p m j s", s=4, j=2)[:, part],
+                bank.rearrange("p (s m j) -> p m j s", s=4, j=2),
             )
 
         turn_words(0)
         pieces = [(0, 32), (32, 64), (64, 96), (96, 128)]
         latents = [
-            keep.tile([P, 2, 2 * (last - first), 2], U32, name=f"latents{first}", tag=f"latents{first}", align_bytes=64) for first, last in pieces
+            keep.tile([P, 4, last - first, 2], U32, name=f"latents{first}", tag=f"latents{first}", align_bytes=64) for first, last in pieces
         ]
         for first, last in pieces:
             nc.vector.tensor_copy(
@@ -131,14 +130,13 @@ def tile_attend_x_mla_append256_topk_kernel(tc, qT, cT, new_cT, ts, ch, offs, sl
                 pool[3][:].indirect(offs_sb[:, first // 4 : last // 4]),
             )
         for (first, last), target in zip(pieces, latents):
-            nc.scalar.copy(target[:], words.rearrange("p u v m j -> p v (m j) u")[:, :, 2 * first : 2 * last, :])
+            nc.scalar.copy(target[:], words.rearrange("p u s m -> p s m u")[:, :, first:last, :])
 
         nc.vector.quantize_mx(
             out=q_codes[:].bitcast(FP8X4), scales=q_scales[:], in_=q_bf[:].rearrange("p q j -> p (q j)")
         )
 
-        banks = [psum.tile([P, N], F32, name=f"scores{b}", tag=f"scores{b}") for b in range(3)]
-        scores = [banks[0][:, 0:P], banks[0][:, P : 2 * P], banks[1][:, 0:P], banks[2][:, 0:P]]
+        scores = [psum.tile([P, P], F32, name=f"scores{b}", tag=f"scores{b}") for b in range(4)]
         for h, (first, last) in enumerate(pieces):
             width = 4 * (last - first)
             k_codes = keep.tile([P, width], U32, name=f"k_codes{h}", align_bytes=64)
@@ -149,7 +147,7 @@ def tile_attend_x_mla_append256_topk_kernel(tc, qT, cT, new_cT, ts, ch, offs, sl
                 in_=latents[h][:].rearrange("p v n u -> p (v n u)").bitcast(BF16),
             )
             nc.tensor.matmul_mx(
-                out=scores[h],
+                out=scores[h][:],
                 lhsT=q_codes[:].bitcast(FP8X4),
                 lhsT_scale=q_scales[:],
                 rhs=k_codes[:].bitcast(FP8X4),
@@ -160,43 +158,33 @@ def tile_attend_x_mla_append256_topk_kernel(tc, qT, cT, new_cT, ts, ch, offs, sl
 
         turn_words(1)
         for u in range(2):
-            copy_values(early, u, slice(0, EARLY))
+            copy_values(u)
 
-        a = keep.tile([P, 2, 2, N // 4], F32, name="a", tag="latents96", align_bytes=64)
+        a = keep.tile([P, 4, N // 4], F32, name="a", tag="latents96", align_bytes=64)
         neg_m = keep.tile([P, 1], F32, name="neg_m")
-        ts_view = ts_g[:].rearrange("p (v j) m -> p v m j", v=2)
         for h, (first, last) in enumerate(pieces):
             part = slice(first, last)
             nc.vector.tensor_tensor(
-                a[:, :, :, part].rearrange("p v j m -> p v m j"),
-                scores[h].rearrange("p (v m j) -> p v m j", v=2, j=2),
-                ts_view[:, :, part, :],
+                a[:, :, part],
+                scores[h][:].rearrange("p (s m) -> p s m", s=4),
+                ts_g[:, :, part],
                 MULT,
             )
-        nc.vector.tensor_reduce(neg_m[:], a[:].rearrange("p v j m -> p (v j m)"), mybir.AxisListType.X, MAX, negate=True)
+        nc.vector.tensor_reduce(neg_m[:], a[:].rearrange("p s m -> p (s m)"), mybir.AxisListType.X, MAX, negate=True)
 
         v_codes = keep.tile([P, D], U32, name="v_codes", tag="ts_g", align_bytes=64)
         v_scales = keep.tile([P, D], U8, name="v_scales", align_bytes=64)
 
-        def quantize_values(first, last, source):
-            nc.vector.quantize_mx(
-                out=v_codes[:, first:last].bitcast(FP8X4), scales=v_scales[:, first:last], in_=source
-            )
-
-        quantize_values(0, 256, early[:, 0:1024])
-        quantize_values(256, 384, early[:, 1024:1536])
+        nc.vector.quantize_mx(out=v_codes[:].bitcast(FP8X4), scales=v_scales[:], in_=values[:])
 
         prob = keep.tile([P, 4, N // 4], F32, name="prob")
         sums = keep.tile([P, 3], F32, name="sums")
         p_turned = psum.tile([P, 4, NQ], F32, name="p_turned", tag="p_turned")
         for s in range(4):
             nc.scalar.activation(
-                out=prob[:, s], in_=a[:, s // 2, s % 2], func=ACT.Exp, bias=neg_m[:], accum_out=sums[:, s - 1 : s] if s >= 2 else None
+                out=prob[:, s], in_=a[:, s], func=ACT.Exp, bias=neg_m[:], accum_out=sums[:, s - 1 : s] if s >= 2 else None
             )
             nc.tensor.transpose(p_turned[:, s, :], prob[:, s, :], ident[:])
-        late = keep.tile([P, 16 * (P - EARLY)], BF16, name="late", tag="latents96", align_bytes=64)
-        for u in range(2):
-            copy_values(late, u, slice(EARLY, P))
 
         total = keep.tile([P, 1], F32, name="total")
         inv = keep.tile([P, 1], F32, name="inv")
@@ -224,12 +212,11 @@ def tile_attend_x_mla_append256_topk_kernel(tc, qT, cT, new_cT, ts, ch, offs, sl
         nc.vector.tensor_reduce(total[:], sums[:], mybir.AxisListType.X, ADD)
         quantize_weights(halves[1])
         nc.vector.reciprocal(inv[:], total[:])
-        quantize_values(4 * EARLY, D, late[:])
 
         result = keep.tile([P, D], F32, name="result")
-        for first, last in [(0, 128), (128, 256), (256, 512)]:
+        for first, last in [(0, 128), (128, 256), (256, 384), (384, 512)]:
             cols = slice(first, last)
-            y = psum.tile([P, last - first], F32, name=f"y{first}", tag="scores2" if first == 256 else f"y{first}")
+            y = psum.tile([P, last - first], F32, name=f"y{first}", tag=f"scores{first // P}")
             nc.tensor.matmul_mx(
                 out=y[:],
                 lhsT=w_codes[:].bitcast(FP8X4),
@@ -240,5 +227,6 @@ def tile_attend_x_mla_append256_topk_kernel(tc, qT, cT, new_cT, ts, ch, offs, sl
                 stop=True,
             )
             nc.vector.scalar_tensor_tensor(result[:, cols], y[:], inv[:], ch_sb[:, cols], MULT, MULT)
-            if last % HALF == 0:
-                nc.sync.dma_start(out[0][:, last - HALF : last], result[:, last - HALF : last])
+            if last >= HALF:
+                stored = slice(0 if last == HALF else first, last)
+                nc.sync.dma_start(out[0][:, stored], result[:, stored])

@@ -21,6 +21,7 @@ N = 512
 D = 512
 NQ = 128
 HALF = 256
+EARLY = 96
 
 FLOPS = 2 * NQ * N * D * 2
 
@@ -30,6 +31,7 @@ def tile_attend_x_mla_append256_topk_kernel(tc, qT, cT, new_cT, ts, ch, offs, sl
     with ExitStack() as ctx:
         lists = ctx.enter_context(tc.tile_pool(name="lists", bufs=1))
         keep = ctx.enter_context(tc.tile_pool(name="keep", bufs=1))
+        reuse = ctx.enter_context(tc.tile_pool(name="reuse", bufs=1))
         psum = ctx.enter_context(tc.psum_pool(name="psum", bufs=1))
 
         slots_sb = lists.tile([P, NEW // 16], U16, name="slots_sb")
@@ -43,8 +45,8 @@ def tile_attend_x_mla_append256_topk_kernel(tc, qT, cT, new_cT, ts, ch, offs, sl
             keep.tile([P, T], F32, name="pool3", tag="pool3", align_bytes=64),
         ]
         words_flat = keep.tile([P, 2 * N], U32, name="words_flat", align_bytes=64)
-        words = words_flat[:].rearrange("p (u s m) -> p u s m", u=2, s=4)
-        halves16 = words_flat[:].bitcast(BF16).rearrange("p (u s m h) -> p u h m s", u=2, s=4, h=2)
+        words = words_flat[:].rearrange("p (u v m j) -> p u v m j", u=2, v=2, j=2)
+        halves16 = words_flat[:].bitcast(BF16).rearrange("p (u v m j h) -> p u h m v j", u=2, v=2, j=2, h=2)
         q_raw = words_flat[:, N : 2 * N].bitcast(F32).rearrange("p (j q) -> p j q", j=4)
         ts_sb = keep.tile([P, T], F32, name="ts_sb")
         ch_sb = keep.tile([P, D], F32, name="ch_sb")
@@ -92,7 +94,7 @@ def tile_attend_x_mla_append256_topk_kernel(tc, qT, cT, new_cT, ts, ch, offs, sl
         rounded = [keep.tile([P, T], BF16, name=f"rounded{t}", tag=f"rounded{t}", align_bytes=64) for t in range(2)]
         ts_col = keep.tile([P, 4], F32, name="ts_col")
         ts_spread = psum.tile([P, 4, P], F32, name="ts_spread", tag="turned0")
-        ts_g = keep.tile([P, 4, P], F32, name="ts_g", tag="ts_g", align_bytes=64)
+        ts_g = reuse.tile([P, 4, P], F32, name="ts_g", offset=0, align_bytes=64)
         for t in range(2):
             nc.scalar.activation(out=rounded[t][:], in_=pool[t][:], func=ACT.Copy)
             if t == 0:
@@ -105,24 +107,24 @@ def tile_attend_x_mla_append256_topk_kernel(tc, qT, cT, new_cT, ts, ch, offs, sl
         nc.vector.tensor_copy(halves16[:, 1, 0], pool[2][:].indirect(offs_sb[:]))
 
         turned = [psum.tile([P, 4, P], F32, name=f"turned{u}", tag=f"turned{u}") for u in range(2)]
-        values = keep.tile([P, 4 * D], BF16, name="values", tag="pool3", align_bytes=64)
+        early = keep.tile([P, 16 * EARLY], BF16, name="early", tag="pool3", align_bytes=64)
         word_floats = words.bitcast(F32)
 
         def turn_words(u):
             for s in range(4):
-                nc.tensor.transpose(turned[u][:, s, :], word_floats[:, u, s, :], ident[:])
+                nc.tensor.transpose(turned[u][:, s, :], word_floats[:, u, s // 2, :, s % 2], ident[:])
 
-        def copy_values(u):
+        def copy_values(copy, values, u, part):
             bank = turned[u][:].rearrange("p s m -> p (s m)").bitcast(BF16)
-            nc.scalar.copy(
-                values[:].rearrange("p (m u j s) -> p u m j s", u=2, j=2, s=4)[:, u],
-                bank.rearrange("p (s m j) -> p m j s", s=4, j=2),
+            copy(
+                values.rearrange("p (m u j s) -> p u m j s", u=2, j=2, s=4)[:, u],
+                bank.rearrange("p (s m j) -> p m j s", s=4, j=2)[:, part],
             )
 
         turn_words(0)
         pieces = [(0, 32), (32, 64), (64, 96), (96, 128)]
         latents = [
-            keep.tile([P, 4, last - first, 2], U32, name=f"latents{first}", tag=f"latents{first}", align_bytes=64) for first, last in pieces
+            keep.tile([P, 2, 2 * (last - first), 2], U32, name=f"latents{first}", tag=f"latents{first}", align_bytes=64) for first, last in pieces
         ]
         for first, last in pieces:
             nc.vector.tensor_copy(
@@ -130,7 +132,7 @@ def tile_attend_x_mla_append256_topk_kernel(tc, qT, cT, new_cT, ts, ch, offs, sl
                 pool[3][:].indirect(offs_sb[:, first // 4 : last // 4]),
             )
         for (first, last), target in zip(pieces, latents):
-            nc.scalar.copy(target[:], words.rearrange("p u s m -> p s m u")[:, :, first:last, :])
+            nc.scalar.copy(target[:], words.rearrange("p u v m j -> p v (m j) u")[:, :, 2 * first : 2 * last, :])
 
         nc.vector.quantize_mx(
             out=q_codes[:].bitcast(FP8X4), scales=q_scales[:], in_=q_bf[:].rearrange("p q j -> p (q j)")
@@ -158,31 +160,36 @@ def tile_attend_x_mla_append256_topk_kernel(tc, qT, cT, new_cT, ts, ch, offs, sl
 
         turn_words(1)
         for u in range(2):
-            copy_values(u)
+            copy_values(nc.scalar.copy, early[:], u, slice(0, EARLY))
 
-        a = keep.tile([P, 4, N // 4], F32, name="a", tag="latents96", align_bytes=64)
+        a = keep.tile([P, 2, 2, N // 4], F32, name="a", tag="latents96", align_bytes=64)
         neg_m = keep.tile([P, 1], F32, name="neg_m")
+        ts_view = ts_g[:].rearrange("p (v j) m -> p v m j", v=2)
         for h, (first, last) in enumerate(pieces):
             part = slice(first, last)
             nc.vector.tensor_tensor(
-                a[:, :, part],
-                scores[h][:].rearrange("p (s m) -> p s m", s=4),
-                ts_g[:, :, part],
+                a[:, :, :, part].rearrange("p v j m -> p v m j"),
+                scores[h][:].rearrange("p (v m j) -> p v m j", v=2, j=2),
+                ts_view[:, :, part, :],
                 MULT,
             )
-        nc.vector.tensor_reduce(neg_m[:], a[:].rearrange("p s m -> p (s m)"), mybir.AxisListType.X, MAX, negate=True)
+        nc.vector.tensor_reduce(neg_m[:], a[:].rearrange("p v j m -> p (v j m)"), mybir.AxisListType.X, MAX, negate=True)
 
-        v_codes = keep.tile([P, D], U32, name="v_codes", tag="ts_g", align_bytes=64)
+        v_codes = reuse.tile([P, D], U32, name="v_codes", offset=1024, align_bytes=64)
         v_scales = keep.tile([P, D], U8, name="v_scales", align_bytes=64)
 
-        nc.vector.quantize_mx(out=v_codes[:].bitcast(FP8X4), scales=v_scales[:], in_=values[:])
+        late = reuse.tile([P, 16 * (P - EARLY)], BF16, name="late", offset=0, align_bytes=64)
+        for u in range(2):
+            copy_values(nc.vector.tensor_copy, late[:], u, slice(EARLY, P))
+        for first, last, source in [(0, 256, early[:, 0:1024]), (256, 384, early[:, 1024:1536]), (384, 512, late[:])]:
+            nc.vector.quantize_mx(out=v_codes[:, first:last].bitcast(FP8X4), scales=v_scales[:, first:last], in_=source)
 
         prob = keep.tile([P, 4, N // 4], F32, name="prob")
         sums = keep.tile([P, 3], F32, name="sums")
         p_turned = psum.tile([P, 4, NQ], F32, name="p_turned", tag="p_turned")
         for s in range(4):
             nc.scalar.activation(
-                out=prob[:, s], in_=a[:, s], func=ACT.Exp, bias=neg_m[:], accum_out=sums[:, s - 1 : s] if s >= 2 else None
+                out=prob[:, s], in_=a[:, s // 2, s % 2], func=ACT.Exp, bias=neg_m[:], accum_out=sums[:, s - 1 : s] if s >= 2 else None
             )
             nc.tensor.transpose(p_turned[:, s, :], prob[:, s, :], ident[:])
 

@@ -178,11 +178,11 @@ def tile_attend_x_mla_append256_topk_kernel(tc, qT, cT, new_cT, ts, ch, offs, sl
         v_codes = reuse.tile([P, D], U32, name="v_codes", offset=1024, align_bytes=64)
         v_scales = keep.tile([P, D], U8, name="v_scales", align_bytes=64)
 
-        late = reuse.tile([P, 16 * (P - EARLY)], BF16, name="late", offset=0, align_bytes=64)
-        for u in range(2):
-            copy_values(nc.vector.tensor_copy, late[:], u, slice(EARLY, P))
-        for first, last, source in [(0, 256, early[:, 0:1024]), (256, 384, early[:, 1024:1536]), (384, 512, late[:])]:
+        def quantize_values(first, last, source):
             nc.vector.quantize_mx(out=v_codes[:, first:last].bitcast(FP8X4), scales=v_scales[:, first:last], in_=source)
+
+        quantize_values(0, 256, early[:, 0:1024])
+        quantize_values(256, 384, early[:, 1024:1536])
 
         prob = keep.tile([P, 4, N // 4], F32, name="prob")
         sums = keep.tile([P, 3], F32, name="sums")
@@ -193,6 +193,9 @@ def tile_attend_x_mla_append256_topk_kernel(tc, qT, cT, new_cT, ts, ch, offs, sl
             )
             nc.tensor.transpose(p_turned[:, s, :], prob[:, s, :], ident[:])
 
+        late = keep.tile([P, 16 * (P - EARLY)], BF16, name="late", tag="latents96", align_bytes=64)
+        for u in range(2):
+            copy_values(nc.scalar.copy, late[:], u, slice(EARLY, P))
         total = keep.tile([P, 1], F32, name="total")
         inv = keep.tile([P, 1], F32, name="inv")
         nc.vector.tensor_reduce(sums[:, 0:1], prob[:, 0:2].rearrange("p s m -> p (s m)"), mybir.AxisListType.X, ADD)
@@ -219,6 +222,7 @@ def tile_attend_x_mla_append256_topk_kernel(tc, qT, cT, new_cT, ts, ch, offs, sl
         nc.vector.tensor_reduce(total[:], sums[:], mybir.AxisListType.X, ADD)
         quantize_weights(halves[1])
         nc.vector.reciprocal(inv[:], total[:])
+        quantize_values(4 * EARLY, D, late[:])
 
         result = keep.tile([P, D], F32, name="result")
         for first, last in [(0, 128), (128, 256), (256, 384), (384, 512)]:

@@ -45,8 +45,8 @@ def tile_attend_x_mla_append256_topk_kernel(tc, qT, cT, new_cT, ts, ch, offs, sl
             keep.tile([P, T], F32, name="pool3", tag="pool3", align_bytes=64),
         ]
         words_flat = keep.tile([P, 2 * N], U32, name="words_flat", align_bytes=64)
-        words = words_flat[:].rearrange("p (u v m j) -> p u v m j", u=2, v=2, j=2)
-        halves16 = words_flat[:].bitcast(BF16).rearrange("p (u v m j h) -> p u h m v j", u=2, v=2, j=2, h=2)
+        words = words_flat[:].rearrange("p (u s m) -> p u s m", u=2, s=4)
+        halves16 = words_flat[:].bitcast(BF16).rearrange("p (u s m h) -> p u h m s", u=2, s=4, h=2)
         q_raw = words_flat[:, N : 2 * N].bitcast(F32).rearrange("p (j q) -> p j q", j=4)
         ts_sb = keep.tile([P, T], F32, name="ts_sb")
         ch_sb = keep.tile([P, D], F32, name="ch_sb")
@@ -112,7 +112,7 @@ def tile_attend_x_mla_append256_topk_kernel(tc, qT, cT, new_cT, ts, ch, offs, sl
 
         def turn_words(u):
             for s in range(4):
-                nc.tensor.transpose(turned[u][:, s, :], word_floats[:, u, s // 2, :, s % 2], ident[:])
+                nc.tensor.transpose(turned[u][:, s, :], word_floats[:, u, s, :], ident[:])
 
         def copy_values(copy, values, u, part):
             bank = turned[u][:].rearrange("p s m -> p (s m)").bitcast(BF16)
@@ -124,7 +124,7 @@ def tile_attend_x_mla_append256_topk_kernel(tc, qT, cT, new_cT, ts, ch, offs, sl
         turn_words(0)
         pieces = [(0, 32), (32, 64), (64, 96), (96, 128)]
         latents = [
-            keep.tile([P, 2, 2 * (last - first), 2], U32, name=f"latents{first}", tag=f"latents{first}", align_bytes=64) for first, last in pieces
+            keep.tile([P, 4, last - first, 2], U32, name=f"latents{first}", tag=f"latents{first}", align_bytes=64) for first, last in pieces
         ]
         for first, last in pieces:
             nc.vector.tensor_copy(
@@ -132,7 +132,7 @@ def tile_attend_x_mla_append256_topk_kernel(tc, qT, cT, new_cT, ts, ch, offs, sl
                 pool[3][:].indirect(offs_sb[:, first // 4 : last // 4]),
             )
         for (first, last), target in zip(pieces, latents):
-            nc.scalar.copy(target[:], words.rearrange("p u v m j -> p v (m j) u")[:, :, 2 * first : 2 * last, :])
+            nc.scalar.copy(target[:], words.rearrange("p u s m -> p s m u")[:, :, first:last, :])
 
         nc.vector.quantize_mx(
             out=q_codes[:].bitcast(FP8X4), scales=q_scales[:], in_=q_bf[:].rearrange("p q j -> p (q j)")
@@ -162,18 +162,17 @@ def tile_attend_x_mla_append256_topk_kernel(tc, qT, cT, new_cT, ts, ch, offs, sl
         for u in range(2):
             copy_values(nc.scalar.copy, early[:], u, slice(0, EARLY))
 
-        a = keep.tile([P, 2, 2, N // 4], F32, name="a", tag="latents96", align_bytes=64)
+        a = keep.tile([P, 4, N // 4], F32, name="a", tag="latents64", align_bytes=64)
         neg_m = keep.tile([P, 1], F32, name="neg_m")
-        ts_view = ts_g[:].rearrange("p (v j) m -> p v m j", v=2)
         for h, (first, last) in enumerate(pieces):
             part = slice(first, last)
             nc.vector.tensor_tensor(
-                a[:, :, :, part].rearrange("p v j m -> p v m j"),
-                scores[h][:].rearrange("p (v m j) -> p v m j", v=2, j=2),
-                ts_view[:, :, part, :],
+                a[:, :, part],
+                scores[h][:].rearrange("p (s m) -> p s m", s=4),
+                ts_g[:, :, part],
                 MULT,
             )
-        nc.vector.tensor_reduce(neg_m[:], a[:].rearrange("p v j m -> p (v j m)"), mybir.AxisListType.X, MAX, negate=True)
+        nc.vector.tensor_reduce(neg_m[:], a[:].rearrange("p s m -> p (s m)"), mybir.AxisListType.X, MAX, negate=True)
 
         v_codes = reuse.tile([P, D], U32, name="v_codes", offset=1024, align_bytes=64)
         v_scales = keep.tile([P, D], U8, name="v_scales", align_bytes=64)
@@ -189,11 +188,11 @@ def tile_attend_x_mla_append256_topk_kernel(tc, qT, cT, new_cT, ts, ch, offs, sl
         p_turned = psum.tile([P, 4, NQ], F32, name="p_turned", tag="p_turned")
         for s in range(4):
             nc.scalar.activation(
-                out=prob[:, s], in_=a[:, s // 2, s % 2], func=ACT.Exp, bias=neg_m[:], accum_out=sums[:, s - 1 : s] if s >= 2 else None
+                out=prob[:, s], in_=a[:, s], func=ACT.Exp, bias=neg_m[:], accum_out=sums[:, s - 1 : s] if s >= 2 else None
             )
             nc.tensor.transpose(p_turned[:, s, :], prob[:, s, :], ident[:])
 
-        late = keep.tile([P, 16 * (P - EARLY)], BF16, name="late", tag="latents96", align_bytes=64)
+        late = keep.tile([P, 16 * (P - EARLY)], BF16, name="late", tag="latents64", align_bytes=64)
         for u in range(2):
             copy_values(nc.scalar.copy, late[:], u, slice(EARLY, P))
         total = keep.tile([P, 1], F32, name="total")

@@ -21,7 +21,9 @@ N = 512
 D = 512
 NQ = 128
 HALF = 256
-EARLY = 96
+EARLY = 64
+SHARE = 512
+ORDER = (0, 2, 3, 1)
 
 FLOPS = 2 * NQ * N * D * 2
 
@@ -40,9 +42,9 @@ def tile_attend_x_mla_append256_topk_kernel(tc, qT, cT, new_cT, ts, ch, offs, sl
         new_sb = [keep.tile([P, NEW], F32, name=f"new{t}", tag=f"new{t}") for t in range(4)]
         pool = [
             keep.tile([P, T], F32, name="pool0", align_bytes=64),
-            keep.tile([P, T], F32, name="pool1", align_bytes=64),
+            keep.tile([P, T], F32, name="pool1", tag="pool1", align_bytes=64),
             keep.tile([P, T], F32, name="pool2", align_bytes=64),
-            keep.tile([P, T], F32, name="pool3", tag="pool3", align_bytes=64),
+            keep.tile([P, T], F32, name="pool3", align_bytes=64),
         ]
         words_flat = keep.tile([P, 2 * N], U32, name="words_flat", align_bytes=64)
         words = words_flat[:].rearrange("p (u s m) -> p u s m", u=2, s=4)
@@ -59,13 +61,11 @@ def tile_attend_x_mla_append256_topk_kernel(tc, qT, cT, new_cT, ts, ch, offs, sl
         nc.sync.dma_start(pool[0][:], pool_view[:, 0, :])
         nc.sync.dma_start(slots_sb[:], slots)
         nc.sync.dma_start(new_sb[0][:], new_view[:, 0, :])
-        nc.sync.dma_start(pool[1][:], pool_view[:, 1, :])
-        nc.sync.dma_start(new_sb[1][:], new_view[:, 1, :])
-        nc.sync.dma_start(pool[2][:], pool_view[:, 2, :])
-        nc.sync.dma_start(new_sb[2][:], new_view[:, 2, :])
-        nc.sync.dma_start(pool[3][:], pool_view[:, 3, :])
-        nc.sync.dma_start(new_sb[3][:], new_view[:, 3, :])
-        nc.sync.dma_start(q_raw, qT[0].rearrange("(p j) w -> p j w", j=4))
+        for t in ORDER[1:]:
+            nc.sync.dma_start(pool[t][:], pool_view[:, t, :])
+            nc.sync.dma_start(new_sb[t][:], new_view[:, t, :])
+            if t == ORDER[2]:
+                nc.sync.dma_start(q_raw, qT[0].rearrange("(p j) w -> p j w", j=4))
         nc.sync.dma_start(ch_sb[:], ch)
 
         warm = keep.tile([P, 1], F32, name="warm")
@@ -77,66 +77,71 @@ def tile_attend_x_mla_append256_topk_kernel(tc, qT, cT, new_cT, ts, ch, offs, sl
         make_identity(nc, ident[:])
 
         nc.vector.memset(ts_sb[0 : P - 1, :], 0.0)
-        ts_row = keep.tile([P, N], F32, name="ts_row", tag="rounded1", align_bytes=64)
+        ts_row = keep.tile([P, N], F32, name="ts_row", align_bytes=64)
         nc.vector.tensor_copy(ts_row[:], ts_sb[:].indirect(offs_sb[:]))
         ts_turned = psum.tile([P, 4, P], F32, name="ts_turned", tag="p_turned")
         for s in range(4):
             nc.tensor.transpose(ts_turned[:, s, :], ts_row[:].rearrange("p (m s) -> p s m", s=4)[:, s, :], ident[:])
 
-        q_bf = keep.tile([P, NQ, 4], BF16, name="q_bf", align_bytes=64)
         q_codes = keep.tile([P, NQ], U32, name="q_codes", align_bytes=64)
         q_scales = keep.tile([P, NQ], U8, name="q_scales", align_bytes=64)
 
-        nc.gpsimd.tensor_copy(q_bf[:], q_raw.rearrange("p j q -> p q j"))
-
-        for t in range(4):
+        for t in ORDER:
             nc.vector.tensor_copy(pool[t][:].indirect(slots_sb[:]), new_sb[t][:])
-        rounded = [keep.tile([P, T], BF16, name=f"rounded{t}", tag=f"rounded{t}", align_bytes=64) for t in range(2)]
+        rounded = {t: keep.tile([P, T], BF16, name=f"rounded{t}", tag=f"rounded{t}", align_bytes=64) for t in ORDER[:3]}
         ts_col = keep.tile([P, 4], F32, name="ts_col")
-        ts_spread = psum.tile([P, 4, P], F32, name="ts_spread", tag="turned0")
+        ts_spread = psum.tile([P, 4, P], F32, name="ts_spread", tag="turned1")
         ts_g = reuse.tile([P, 4, P], F32, name="ts_g", offset=0, align_bytes=64)
-        for t in range(2):
-            nc.scalar.activation(out=rounded[t][:], in_=pool[t][:], func=ACT.Copy)
-            if t == 0:
-                nc.scalar.copy(ts_col[:], ts_turned[:, :, P - 1])
-                for s in range(4):
-                    nc.tensor.transpose(ts_spread[:, s, :], ts_col[:, s : s + 1].to_broadcast([P, P]), ident[:])
-            else:
-                nc.scalar.copy(ts_g[:], ts_spread[:])
-            nc.scalar.activation(out=halves16[:, 0, t], in_=rounded[t][:].indirect(offs_sb[:]), func=ACT.Copy)
-        nc.vector.tensor_copy(halves16[:, 1, 0], pool[2][:].indirect(offs_sb[:]))
+        nc.scalar.copy(ts_col[:], ts_turned[:, :, P - 1])
+        for s in range(4):
+            nc.tensor.transpose(ts_spread[:, s, :], ts_col[:, s : s + 1].to_broadcast([P, P]), ident[:])
+        nc.scalar.activation(out=rounded[0][:, :SHARE], in_=pool[0][:, :SHARE], func=ACT.Copy)
+        nc.gpsimd.tensor_copy(rounded[0][:, SHARE:], pool[0][:, SHARE:])
+        nc.scalar.copy(ts_g[:], ts_spread[:])
+        for t in ORDER[1:3]:
+            nc.gpsimd.tensor_copy(rounded[t][:], pool[t][:])
+        nc.scalar.activation(out=halves16[:, 0, 0], in_=rounded[0][:].indirect(offs_sb[:]), func=ACT.Copy)
+        q_bf = keep.tile([P, NQ, 4], BF16, name="q_bf", align_bytes=64)
+        nc.scalar.activation(out=q_bf[:], in_=q_raw.rearrange("p j q -> p q j"), func=ACT.Copy)
+        nc.scalar.activation(out=halves16[:, 1, 0], in_=rounded[2][:].indirect(offs_sb[:]), func=ACT.Copy)
+        for half in range(2):
+            nc.scalar.activation(
+                out=halves16[:, 1, 1, 64 * half : 64 * half + 64],
+                in_=rounded[3][:].indirect(offs_sb[:, 16 * half : 16 * half + 16]),
+                func=ACT.Copy,
+            )
+        nc.vector.quantize_mx(
+            out=q_codes[:].bitcast(FP8X4), scales=q_scales[:], in_=q_bf[:].rearrange("p q j -> p (q j)")
+        )
 
-        turned = [psum.tile([P, 4, P], F32, name=f"turned{u}", tag=f"turned{u}") for u in range(2)]
-        early = keep.tile([P, 16 * EARLY], BF16, name="early", tag="pool3", align_bytes=64)
         word_floats = words.bitcast(F32)
 
-        def turn_words(u):
+        def turn_words(u, tag):
+            turned = psum.tile([P, 4, P], F32, name=f"turned{u}", tag=tag)
             for s in range(4):
-                nc.tensor.transpose(turned[u][:, s, :], word_floats[:, u, s, :], ident[:])
+                nc.tensor.transpose(turned[:, s, :], word_floats[:, u, s, :], ident[:])
+            return turned
 
-        def copy_values(copy, values, u, part):
-            bank = turned[u][:].rearrange("p s m -> p (s m)").bitcast(BF16)
-            copy(
-                values.rearrange("p (m u j s) -> p u m j s", u=2, j=2, s=4)[:, u],
-                bank.rearrange("p (s m j) -> p m j s", s=4, j=2)[:, part],
+        def copy_values(values, turned, part):
+            bank = turned[:].rearrange("p s m -> p (s m)").bitcast(BF16)
+            nc.scalar.copy(
+                values.rearrange("p h (j m s) -> p h j m s", j=2, s=4)[:, part],
+                bank.rearrange("p (s h m j) -> p h j m s", s=4, h=2, j=2)[:, part],
             )
 
-        turn_words(0)
+        turned1 = turn_words(1, "turned1")
         pieces = [(0, 32), (32, 64), (64, 96), (96, 128)]
         latents = [
             keep.tile([P, 4, last - first, 2], U32, name=f"latents{first}", tag=f"latents{first}", align_bytes=64) for first, last in pieces
         ]
         for first, last in pieces:
             nc.vector.tensor_copy(
-                halves16[:, 1, 1, first:last],
-                pool[3][:].indirect(offs_sb[:, first // 4 : last // 4]),
+                halves16[:, 0, 1, first:last],
+                pool[1][:].indirect(offs_sb[:, first // 4 : last // 4]),
             )
         for (first, last), target in zip(pieces, latents):
-            nc.scalar.copy(target[:], words.rearrange("p u s m -> p s m u")[:, :, first:last, :])
-
-        nc.vector.quantize_mx(
-            out=q_codes[:].bitcast(FP8X4), scales=q_scales[:], in_=q_bf[:].rearrange("p q j -> p (q j)")
-        )
+            copy = nc.gpsimd.tensor_copy if last <= 64 else nc.scalar.copy
+            copy(target[:], words.rearrange("p u s m -> p s m u")[:, :, first:last, :])
 
         scores = [psum.tile([P, P], F32, name=f"scores{b}", tag=f"scores{b}") for b in range(4)]
         for h, (first, last) in enumerate(pieces):
@@ -158,9 +163,8 @@ def tile_attend_x_mla_append256_topk_kernel(tc, qT, cT, new_cT, ts, ch, offs, sl
                 stop=True,
             )
 
-        turn_words(1)
-        for u in range(2):
-            copy_values(nc.scalar.copy, early[:], u, slice(0, EARLY))
+        early = keep.tile([P, 2, 4 * P], BF16, name="early", tag="latents0", align_bytes=64)
+        copy_values(early[:], turned1, slice(0, 2))
 
         a = keep.tile([P, 4, N // 4], F32, name="a", tag="latents64", align_bytes=64)
         neg_m = keep.tile([P, 1], F32, name="neg_m")
@@ -174,14 +178,14 @@ def tile_attend_x_mla_append256_topk_kernel(tc, qT, cT, new_cT, ts, ch, offs, sl
             )
         nc.vector.tensor_reduce(neg_m[:], a[:].rearrange("p s m -> p (s m)"), mybir.AxisListType.X, MAX, negate=True)
 
+        turned0 = turn_words(0, "scores0")
         v_codes = reuse.tile([P, D], U32, name="v_codes", offset=1024, align_bytes=64)
         v_scales = keep.tile([P, D], U8, name="v_scales", align_bytes=64)
 
         def quantize_values(first, last, source):
             nc.vector.quantize_mx(out=v_codes[:, first:last].bitcast(FP8X4), scales=v_scales[:, first:last], in_=source)
 
-        quantize_values(0, 256, early[:, 0:1024])
-        quantize_values(256, 384, early[:, 1024:1536])
+        quantize_values(256, 512, early[:].rearrange("p h c -> p (h c)"))
 
         prob = keep.tile([P, 4, N // 4], F32, name="prob")
         sums = keep.tile([P, 3], F32, name="sums")
@@ -192,9 +196,9 @@ def tile_attend_x_mla_append256_topk_kernel(tc, qT, cT, new_cT, ts, ch, offs, sl
             )
             nc.tensor.transpose(p_turned[:, s, :], prob[:, s, :], ident[:])
 
-        late = keep.tile([P, 16 * (P - EARLY)], BF16, name="late", tag="latents64", align_bytes=64)
-        for u in range(2):
-            copy_values(nc.scalar.copy, late[:], u, slice(EARLY, P))
+        late = keep.tile([P, 2, 4 * P], BF16, name="late", tag="latents64", align_bytes=64)
+        for half in range(2):
+            copy_values(late[:], turned0, slice(half, half + 1))
         total = keep.tile([P, 1], F32, name="total")
         inv = keep.tile([P, 1], F32, name="inv")
         nc.vector.tensor_reduce(sums[:, 0:1], prob[:, 0:2].rearrange("p s m -> p (s m)"), mybir.AxisListType.X, ADD)
@@ -217,26 +221,36 @@ def tile_attend_x_mla_append256_topk_kernel(tc, qT, cT, new_cT, ts, ch, offs, sl
                 in_=w_grouped[:, rows, :].rearrange("p q s -> p (q s)"),
             )
 
-        quantize_weights(halves[0])
         nc.vector.tensor_reduce(total[:], sums[:], mybir.AxisListType.X, ADD)
+        quantize_weights(halves[0])
+        quantize_values(0, 128, late[:, 0])
         quantize_weights(halves[1])
         nc.vector.reciprocal(inv[:], total[:])
-        quantize_values(4 * EARLY, D, late[:])
+        quantize_values(128, 256, late[:, 1])
 
         result = keep.tile([P, D], F32, name="result")
-        for first, last in [(0, 128), (128, 256), (256, 384), (384, 512)]:
-            cols = slice(first, last)
-            y = psum.tile([P, last - first], F32, name=f"y{first}", tag=f"scores{first // P}")
-            nc.tensor.matmul_mx(
-                out=y[:],
-                lhsT=w_codes[:].bitcast(FP8X4),
-                lhsT_scale=w_scales[:],
-                rhs=v_codes[:, cols].bitcast(FP8X4),
-                rhs_scale=v_scales[:, cols],
-                start=True,
-                stop=True,
-            )
-            nc.vector.scalar_tensor_tensor(result[:, cols], y[:], inv[:], ch_sb[:, cols], MULT, MULT)
-            if last >= HALF:
-                stored = slice(0 if last == HALF else first, last)
-                nc.sync.dma_start(out[0][:, stored], result[:, stored])
+        for half in range(2):
+            y = psum.tile([P, 2, P], F32, name=f"y{half}", tag=f"y{half}")
+            for u in (1, 0):
+                cols = slice(256 * u + 128 * half, 256 * u + 128 * half + 128)
+                nc.tensor.matmul_mx(
+                    out=y[:, u, :],
+                    lhsT=w_codes[:].bitcast(FP8X4),
+                    lhsT_scale=w_scales[:],
+                    rhs=v_codes[:, cols].bitcast(FP8X4),
+                    rhs_scale=v_scales[:, cols],
+                    start=True,
+                    stop=True,
+                )
+            fours = y[:].rearrange("p u (j m) -> p m (u j)", j=2)
+            for first, last in [(0, 64)] if half == 0 else [(0, 32), (32, 64)]:
+                cols = slice(256 * half + 4 * first, 256 * half + 4 * last)
+                nc.vector.scalar_tensor_tensor(
+                    result[:, cols].rearrange("p (m t) -> p m t", t=4),
+                    fours[:, first:last],
+                    inv[:],
+                    ch_sb[:, cols].rearrange("p (m t) -> p m t", t=4),
+                    MULT,
+                    MULT,
+                )
+                nc.sync.dma_start(out[0][:, cols], result[:, cols])

@@ -33,13 +33,12 @@ def tile_attend_x_mla_append256_topk_kernel(tc, qT, cT, new_cT, ts, ch, offs, sl
     with ExitStack() as ctx:
         lists = ctx.enter_context(tc.tile_pool(name="lists", bufs=1))
         keep = ctx.enter_context(tc.tile_pool(name="keep", bufs=1))
-        reuse = ctx.enter_context(tc.tile_pool(name="reuse", bufs=1))
         psum = ctx.enter_context(tc.psum_pool(name="psum", bufs=1))
 
         slots_sb = lists.tile([P, NEW // 16], U16, name="slots_sb")
         offs_sb = lists.tile([P, N // 16], U16, name="offs_sb")
 
-        new_sb = [keep.tile([P, NEW], F32, name=f"new{t}", tag=f"new{t}") for t in range(4)]
+        new_sb = [keep.tile([P, NEW], F32, name=f"new{t}", tag=f"new{t}", align_bytes=64) for t in range(4)]
         pool = [
             keep.tile([P, T], F32, name="pool0", align_bytes=64),
             keep.tile([P, T], F32, name="pool1", tag="pool1", align_bytes=64),
@@ -83,24 +82,21 @@ def tile_attend_x_mla_append256_topk_kernel(tc, qT, cT, new_cT, ts, ch, offs, sl
         for s in range(4):
             nc.tensor.transpose(ts_turned[:, s, :], ts_row[:].rearrange("p (m s) -> p s m", s=4)[:, s, :], ident[:])
 
-        q_codes = keep.tile([P, NQ], U32, name="q_codes", align_bytes=64)
         q_scales = keep.tile([P, NQ], U8, name="q_scales", align_bytes=64)
 
         for t in ORDER:
             nc.vector.tensor_copy(pool[t][:].indirect(slots_sb[:]), new_sb[t][:])
         rounded = {t: keep.tile([P, T], BF16, name=f"rounded{t}", tag=f"rounded{t}", align_bytes=64) for t in ORDER[:3]}
-        ts_col = keep.tile([P, 4], F32, name="ts_col")
-        ts_spread = psum.tile([P, 4, P], F32, name="ts_spread", tag="turned1")
-        ts_g = reuse.tile([P, 4, P], F32, name="ts_g", offset=0, align_bytes=64)
-        nc.scalar.copy(ts_col[:], ts_turned[:, :, P - 1])
-        for s in range(4):
-            nc.tensor.transpose(ts_spread[:, s, :], ts_col[:, s : s + 1].to_broadcast([P, P]), ident[:])
+        ts_spread = psum.tile([P, 4, P], F32, name="ts_spread", tag="y0")
         nc.scalar.activation(out=rounded[0][:, :SHARE], in_=pool[0][:, :SHARE], func=ACT.Copy)
         nc.gpsimd.tensor_copy(rounded[0][:, SHARE:], pool[0][:, SHARE:])
-        nc.scalar.copy(ts_g[:], ts_spread[:])
+        nc.scalar.activation(out=halves16[:, 0, 0], in_=rounded[0][:].indirect(offs_sb[:]), func=ACT.Copy)
+        ts_col = keep.tile([P, 4], F32, name="ts_col", tag="rounded0", align_bytes=64)
+        nc.vector.tensor_copy(ts_col[:], ts_turned[:, :, P - 1])
+        for s in range(4):
+            nc.tensor.transpose(ts_spread[:, s, :], ts_col[:, s : s + 1].to_broadcast([P, P]), ident[:])
         for t in ORDER[1:3]:
             nc.gpsimd.tensor_copy(rounded[t][:], pool[t][:])
-        nc.scalar.activation(out=halves16[:, 0, 0], in_=rounded[0][:].indirect(offs_sb[:]), func=ACT.Copy)
         q_bf = keep.tile([P, NQ, 4], BF16, name="q_bf", align_bytes=64)
         nc.scalar.activation(out=q_bf[:], in_=q_raw.rearrange("p j q -> p q j"), func=ACT.Copy)
         nc.scalar.activation(out=halves16[:, 1, 0], in_=rounded[2][:].indirect(offs_sb[:]), func=ACT.Copy)
@@ -110,9 +106,6 @@ def tile_attend_x_mla_append256_topk_kernel(tc, qT, cT, new_cT, ts, ch, offs, sl
                 in_=rounded[3][:].indirect(offs_sb[:, 16 * half : 16 * half + 16]),
                 func=ACT.Copy,
             )
-        nc.vector.quantize_mx(
-            out=q_codes[:].bitcast(FP8X4), scales=q_scales[:], in_=q_bf[:].rearrange("p q j -> p (q j)")
-        )
 
         word_floats = words.bitcast(F32)
 
@@ -140,8 +133,12 @@ def tile_attend_x_mla_append256_topk_kernel(tc, qT, cT, new_cT, ts, ch, offs, sl
                 pool[1][:].indirect(offs_sb[:, first // 4 : last // 4]),
             )
         for (first, last), target in zip(pieces, latents):
-            copy = nc.gpsimd.tensor_copy if last <= 64 else nc.scalar.copy
+            copy = nc.gpsimd.tensor_copy if first == 0 else nc.scalar.copy
             copy(target[:], words.rearrange("p u s m -> p s m u")[:, :, first:last, :])
+        q_codes = keep.tile([P, NQ], U32, name="q_codes", tag="new1", align_bytes=64)
+        nc.vector.quantize_mx(
+            out=q_codes[:].bitcast(FP8X4), scales=q_scales[:], in_=q_bf[:].rearrange("p q j -> p (q j)")
+        )
 
         scores = [psum.tile([P, P], F32, name=f"scores{b}", tag=f"scores{b}") for b in range(4)]
         for h, (first, last) in enumerate(pieces):
@@ -163,7 +160,10 @@ def tile_attend_x_mla_append256_topk_kernel(tc, qT, cT, new_cT, ts, ch, offs, sl
                 stop=True,
             )
 
-        early = keep.tile([P, 2, 4 * P], BF16, name="early", tag="latents0", align_bytes=64)
+        ts_g = keep.tile([P, 4, P], F32, name="ts_g", tag="latents0", align_bytes=64)
+        for half in range(2):
+            nc.scalar.copy(ts_g[:, :, 64 * half : 64 * half + 64], ts_spread[:, :, 64 * half : 64 * half + 64])
+        early = keep.tile([P, 2, 4 * P], BF16, name="early", tag="latents32", align_bytes=64)
         copy_values(early[:], turned1, slice(0, 2))
 
         a = keep.tile([P, 4, N // 4], F32, name="a", tag="latents64", align_bytes=64)
@@ -179,7 +179,7 @@ def tile_attend_x_mla_append256_topk_kernel(tc, qT, cT, new_cT, ts, ch, offs, sl
         nc.vector.tensor_reduce(neg_m[:], a[:].rearrange("p s m -> p (s m)"), mybir.AxisListType.X, MAX, negate=True)
 
         turned0 = turn_words(0, "scores0")
-        v_codes = reuse.tile([P, D], U32, name="v_codes", offset=1024, align_bytes=64)
+        v_codes = keep.tile([P, D], U32, name="v_codes", tag="latents0", align_bytes=64)
         v_scales = keep.tile([P, D], U8, name="v_scales", align_bytes=64)
 
         def quantize_values(first, last, source):

@@ -6,6 +6,7 @@ from concourse.masks import make_identity
 F32 = mybir.dt.float32
 BF16 = mybir.dt.bfloat16
 U32 = mybir.dt.uint32
+I32 = mybir.dt.int32
 U16 = mybir.dt.uint16
 U8 = mybir.dt.uint8
 FP8X4 = mybir.dt.float8_e4m3fn_x4
@@ -48,7 +49,7 @@ def tile_attend_x_mla_append256_topk_kernel(tc, qT, cT, new_cT, ts, ch, offs, sl
         words_flat = keep.tile([P, 2 * N], U32, name="words_flat", align_bytes=64)
         words = words_flat[:].rearrange("p (u s m) -> p u s m", u=2, s=4)
         halves16 = words_flat[:].bitcast(BF16).rearrange("p (u s m h) -> p u h m s", u=2, s=4, h=2)
-        q_raw = words_flat[:, N : 2 * N].bitcast(F32).rearrange("p (j q) -> p j q", j=4)
+        q_raw = keep.tile([P, 4, NQ], F32, name="q_raw")
         ts_sb = keep.tile([P, T], F32, name="ts_sb")
         ch_sb = keep.tile([P, D], F32, name="ch_sb")
 
@@ -63,8 +64,7 @@ def tile_attend_x_mla_append256_topk_kernel(tc, qT, cT, new_cT, ts, ch, offs, sl
         for t in ORDER[1:]:
             nc.sync.dma_start(pool[t][:], pool_view[:, t, :])
             nc.sync.dma_start(new_sb[t][:], new_view[:, t, :])
-            if t == ORDER[2]:
-                nc.sync.dma_start(q_raw, qT[0].rearrange("(p j) w -> p j w", j=4))
+        nc.sync.dma_start(q_raw[:], qT[0].rearrange("(p j) w -> p j w", j=4))
         nc.sync.dma_start(ch_sb[:], ch)
 
         warm = keep.tile([P, 1], F32, name="warm")
@@ -98,7 +98,7 @@ def tile_attend_x_mla_append256_topk_kernel(tc, qT, cT, new_cT, ts, ch, offs, sl
         for t in ORDER[1:3]:
             nc.gpsimd.tensor_copy(rounded[t][:], pool[t][:])
         q_bf = keep.tile([P, NQ, 4], BF16, name="q_bf", align_bytes=64)
-        nc.scalar.activation(out=q_bf[:], in_=q_raw.rearrange("p j q -> p q j"), func=ACT.Copy)
+        nc.gpsimd.tensor_copy(q_bf[:], q_raw[:].rearrange("p j q -> p q j"))
         nc.scalar.activation(out=halves16[:, 1, 0], in_=rounded[2][:].indirect(offs_sb[:]), func=ACT.Copy)
         for half in range(2):
             nc.scalar.activation(
@@ -118,8 +118,8 @@ def tile_attend_x_mla_append256_topk_kernel(tc, qT, cT, new_cT, ts, ch, offs, sl
         def copy_values(values, turned, part):
             bank = turned[:].rearrange("p s m -> p (s m)").bitcast(BF16)
             nc.scalar.copy(
-                values.rearrange("p h (j m s) -> p h j m s", j=2, s=4)[:, part],
-                bank.rearrange("p (s h m j) -> p h j m s", s=4, h=2, j=2)[:, part],
+                values.rearrange("p h (j m s) -> p h m j s", j=2, s=4)[:, part],
+                bank.rearrange("p (s h m j) -> p h m j s", s=4, h=2, j=2)[:, part],
             )
 
         turned1 = turn_words(1, "turned1")
@@ -132,10 +132,10 @@ def tile_attend_x_mla_append256_topk_kernel(tc, qT, cT, new_cT, ts, ch, offs, sl
                 halves16[:, 0, 1, first:last],
                 pool[1][:].indirect(offs_sb[:, first // 4 : last // 4]),
             )
-        for (first, last), target in zip(pieces, latents):
-            copy = nc.gpsimd.tensor_copy if first == 0 else nc.scalar.copy
-            copy(target[:], words.rearrange("p u s m -> p s m u")[:, :, first:last, :])
-        q_codes = keep.tile([P, NQ], U32, name="q_codes", tag="new1", align_bytes=64)
+        side_by_side = words.rearrange("p u s m -> p s m u")
+        for h in range(3):
+            nc.scalar.copy(latents[h][:], side_by_side[:, :, 32 * h : 32 * h + 32, :])
+        q_codes = keep.tile([P, NQ], U32, name="q_codes", align_bytes=64)
         nc.vector.quantize_mx(
             out=q_codes[:].bitcast(FP8X4), scales=q_scales[:], in_=q_bf[:].rearrange("p q j -> p (q j)")
         )
@@ -143,6 +143,10 @@ def tile_attend_x_mla_append256_topk_kernel(tc, qT, cT, new_cT, ts, ch, offs, sl
         scores = [psum.tile([P, P], F32, name=f"scores{b}", tag=f"scores{b}") for b in range(4)]
         for h, (first, last) in enumerate(pieces):
             width = 4 * (last - first)
+            if h == 1:
+                nc.vector.tensor_copy(
+                    latents[3][:].bitcast(I32), words.bitcast(I32).rearrange("p u s m -> p s m u")[:, :, 96:128, :]
+                )
             k_codes = keep.tile([P, width], U32, name=f"k_codes{h}", align_bytes=64)
             k_scales = keep.tile([P, width], U8, name=f"k_scales{h}", align_bytes=64)
             nc.vector.quantize_mx(
@@ -221,10 +225,10 @@ def tile_attend_x_mla_append256_topk_kernel(tc, qT, cT, new_cT, ts, ch, offs, sl
                 in_=w_grouped[:, rows, :].rearrange("p q s -> p (q s)"),
             )
 
-        nc.vector.tensor_reduce(total[:], sums[:], mybir.AxisListType.X, ADD)
         quantize_weights(halves[0])
-        quantize_values(0, 128, late[:, 0])
+        nc.vector.tensor_reduce(total[:], sums[:], mybir.AxisListType.X, ADD)
         quantize_weights(halves[1])
+        quantize_values(0, 128, late[:, 0])
         nc.vector.reciprocal(inv[:], total[:])
         quantize_values(128, 256, late[:, 1])
 

@@ -6,7 +6,6 @@ from concourse.masks import make_identity
 F32 = mybir.dt.float32
 BF16 = mybir.dt.bfloat16
 U32 = mybir.dt.uint32
-I32 = mybir.dt.int32
 U16 = mybir.dt.uint16
 U8 = mybir.dt.uint8
 FP8X4 = mybir.dt.float8_e4m3fn_x4
@@ -21,10 +20,10 @@ NEW = 256
 N = 512
 D = 512
 NQ = 128
-HALF = 256
-EARLY = 64
-SHARE = 512
+ROWS = 32
+HALF_ROWS = 64
 ORDER = (0, 2, 3, 1)
+SCALAR_SHARE = {2: 384, 3: 352}
 
 FLOPS = 2 * NQ * N * D * 2
 
@@ -39,16 +38,11 @@ def tile_attend_x_mla_append256_topk_kernel(tc, qT, cT, new_cT, ts, ch, offs, sl
         slots_sb = lists.tile([P, NEW // 16], U16, name="slots_sb")
         offs_sb = lists.tile([P, N // 16], U16, name="offs_sb")
 
-        new_sb = [keep.tile([P, NEW], F32, name=f"new{t}", tag=f"new{t}", align_bytes=64) for t in range(4)]
-        pool = [
-            keep.tile([P, T], F32, name="pool0", align_bytes=64),
-            keep.tile([P, T], F32, name="pool1", tag="pool1", align_bytes=64),
-            keep.tile([P, T], F32, name="pool2", align_bytes=64),
-            keep.tile([P, T], F32, name="pool3", align_bytes=64),
-        ]
+        new_sb = [keep.tile([P, NEW], F32, name=f"new{t}", align_bytes=64) for t in range(4)]
+        pool = [keep.tile([P, T], F32, name=f"pool{t}", align_bytes=64) for t in range(4)]
         words_flat = keep.tile([P, 2 * N], U32, name="words_flat", align_bytes=64)
         words = words_flat[:].rearrange("p (u s m) -> p u s m", u=2, s=4)
-        halves16 = words_flat[:].bitcast(BF16).rearrange("p (u s m h) -> p u h m s", u=2, s=4, h=2)
+        halves = words_flat[:].bitcast(BF16).rearrange("p (u s m h) -> p u h m s", u=2, s=4, h=2)
         q_raw = keep.tile([P, 4, NQ], F32, name="q_raw")
         ts_sb = keep.tile([P, T], F32, name="ts_sb")
         ch_sb = keep.tile([P, D], F32, name="ch_sb")
@@ -86,73 +80,73 @@ def tile_attend_x_mla_append256_topk_kernel(tc, qT, cT, new_cT, ts, ch, offs, sl
 
         for t in ORDER:
             nc.vector.tensor_copy(pool[t][:].indirect(slots_sb[:]), new_sb[t][:])
+
         rounded = {t: keep.tile([P, T], BF16, name=f"rounded{t}", tag=f"rounded{t}", align_bytes=64) for t in ORDER[:3]}
         ts_spread = psum.tile([P, 4, P], F32, name="ts_spread", tag="y0")
-        nc.scalar.activation(out=rounded[0][:, :SHARE], in_=pool[0][:, :SHARE], func=ACT.Copy)
-        nc.gpsimd.tensor_copy(rounded[0][:, SHARE:], pool[0][:, SHARE:])
-        nc.scalar.activation(out=halves16[:, 0, 0], in_=rounded[0][:].indirect(offs_sb[:]), func=ACT.Copy)
+
+        def round_shared(t):
+            share = SCALAR_SHARE[t]
+            nc.scalar.activation(out=rounded[t][:, :share], in_=pool[t][:, :share], func=ACT.Copy)
+            nc.gpsimd.tensor_copy(rounded[t][:, share:], pool[t][:, share:])
+
+        def gather_rounded(t, parts):
+            rows = P // parts
+            for first in range(0, P, rows):
+                nc.scalar.activation(
+                    out=halves[:, t // 2, t % 2, first : first + rows],
+                    in_=rounded[t][:].indirect(offs_sb[:, first // 4 : (first + rows) // 4]),
+                    func=ACT.Copy,
+                )
+
+        nc.scalar.activation(out=rounded[0][:], in_=pool[0][:], func=ACT.Copy)
+        gather_rounded(0, 1)
         ts_col = keep.tile([P, 4], F32, name="ts_col", tag="rounded0", align_bytes=64)
         nc.vector.tensor_copy(ts_col[:], ts_turned[:, :, P - 1])
         for s in range(4):
             nc.tensor.transpose(ts_spread[:, s, :], ts_col[:, s : s + 1].to_broadcast([P, P]), ident[:])
-        for t in ORDER[1:3]:
-            nc.gpsimd.tensor_copy(rounded[t][:], pool[t][:])
+        round_shared(2)
+        gather_rounded(2, 1)
+        round_shared(3)
         q_bf = keep.tile([P, NQ, 4], BF16, name="q_bf", align_bytes=64)
         nc.gpsimd.tensor_copy(q_bf[:], q_raw[:].rearrange("p j q -> p q j"))
-        nc.scalar.activation(out=halves16[:, 1, 0], in_=rounded[2][:].indirect(offs_sb[:]), func=ACT.Copy)
-        for half in range(2):
-            nc.scalar.activation(
-                out=halves16[:, 1, 1, 64 * half : 64 * half + 64],
-                in_=rounded[3][:].indirect(offs_sb[:, 16 * half : 16 * half + 16]),
-                func=ACT.Copy,
-            )
+        gather_rounded(3, 2)
 
         word_floats = words.bitcast(F32)
 
-        def turn_words(u, tag):
+        def turn_pair(u, tag):
             turned = psum.tile([P, 4, P], F32, name=f"turned{u}", tag=tag)
             for s in range(4):
                 nc.tensor.transpose(turned[:, s, :], word_floats[:, u, s, :], ident[:])
             return turned
 
         def copy_values(values, turned, part):
-            bank = turned[:].rearrange("p s m -> p (s m)").bitcast(BF16)
+            bank = turned[:].rearrange("p s f -> p (s f)").bitcast(BF16)
             nc.scalar.copy(
-                values.rearrange("p h (j m s) -> p h m j s", j=2, s=4)[:, part],
-                bank.rearrange("p (s h m j) -> p h m j s", s=4, h=2, j=2)[:, part],
+                values.rearrange("p c (j f s) -> p c f j s", j=2, s=4)[:, part],
+                bank.rearrange("p (s c f j) -> p c f j s", s=4, c=2, j=2)[:, part],
             )
 
-        turned1 = turn_words(1, "turned1")
-        pieces = [(0, 32), (32, 64), (64, 96), (96, 128)]
-        latents = [
-            keep.tile([P, 4, last - first, 2], U32, name=f"latents{first}", tag=f"latents{first}", align_bytes=64) for first, last in pieces
-        ]
-        for first, last in pieces:
-            nc.vector.tensor_copy(
-                halves16[:, 0, 1, first:last],
-                pool[1][:].indirect(offs_sb[:, first // 4 : last // 4]),
-            )
-        side_by_side = words.rearrange("p u s m -> p s m u")
-        for h in range(3):
-            nc.scalar.copy(latents[h][:], side_by_side[:, :, 32 * h : 32 * h + 32, :])
+        turned1 = turn_pair(1, "turned1")
+
+        quarters = [slice(ROWS * h, ROWS * (h + 1)) for h in range(4)]
+        keys = [keep.tile([P, 4, ROWS, 2], U32, name=f"keys{h}", tag=f"keys{h}", align_bytes=64) for h in range(4)]
+        for h, rows in enumerate(quarters):
+            nc.vector.tensor_copy(halves[:, 0, 1, rows], pool[1][:].indirect(offs_sb[:, 8 * h : 8 * h + 8]))
+        for h, rows in enumerate(quarters):
+            nc.scalar.copy(keys[h][:], words.rearrange("p u s m -> p s m u")[:, :, rows, :])
         q_codes = keep.tile([P, NQ], U32, name="q_codes", align_bytes=64)
         nc.vector.quantize_mx(
             out=q_codes[:].bitcast(FP8X4), scales=q_scales[:], in_=q_bf[:].rearrange("p q j -> p (q j)")
         )
 
-        scores = [psum.tile([P, P], F32, name=f"scores{b}", tag=f"scores{b}") for b in range(4)]
-        for h, (first, last) in enumerate(pieces):
-            width = 4 * (last - first)
-            if h == 1:
-                nc.vector.tensor_copy(
-                    latents[3][:].bitcast(I32), words.bitcast(I32).rearrange("p u s m -> p s m u")[:, :, 96:128, :]
-                )
-            k_codes = keep.tile([P, width], U32, name=f"k_codes{h}", align_bytes=64)
-            k_scales = keep.tile([P, width], U8, name=f"k_scales{h}", align_bytes=64)
+        scores = [psum.tile([P, P], F32, name=f"scores{h}", tag=f"scores{h}") for h in range(4)]
+        for h in range(4):
+            k_codes = keep.tile([P, P], U32, name=f"k_codes{h}", align_bytes=64)
+            k_scales = keep.tile([P, P], U8, name=f"k_scales{h}", align_bytes=64)
             nc.vector.quantize_mx(
                 out=k_codes[:].bitcast(FP8X4),
                 scales=k_scales[:],
-                in_=latents[h][:].rearrange("p v n u -> p (v n u)").bitcast(BF16),
+                in_=keys[h][:].rearrange("p s m u -> p (s m u)").bitcast(BF16),
             )
             nc.tensor.matmul_mx(
                 out=scores[h][:],
@@ -164,32 +158,32 @@ def tile_attend_x_mla_append256_topk_kernel(tc, qT, cT, new_cT, ts, ch, offs, sl
                 stop=True,
             )
 
-        ts_g = keep.tile([P, 4, P], F32, name="ts_g", tag="latents0", align_bytes=64)
-        for half in range(2):
-            nc.scalar.copy(ts_g[:, :, 64 * half : 64 * half + 64], ts_spread[:, :, 64 * half : 64 * half + 64])
-        early = keep.tile([P, 2, 4 * P], BF16, name="early", tag="latents32", align_bytes=64)
-        copy_values(early[:], turned1, slice(0, 2))
+        ts_free = keep.tile([P, 4, P], F32, name="ts_free", tag="keys0", align_bytes=64)
+        for c in range(2):
+            rows = slice(HALF_ROWS * c, HALF_ROWS * (c + 1))
+            nc.scalar.copy(ts_free[:, :, rows], ts_spread[:, :, rows])
+        values1 = keep.tile([P, 2, 4 * P], BF16, name="values1", tag="keys1", align_bytes=64)
+        copy_values(values1[:], turned1, slice(0, 2))
 
-        a = keep.tile([P, 4, N // 4], F32, name="a", tag="latents64", align_bytes=64)
+        a = keep.tile([P, 4, N // 4], F32, name="a", tag="keys2", align_bytes=64)
         neg_m = keep.tile([P, 1], F32, name="neg_m")
-        for h, (first, last) in enumerate(pieces):
-            part = slice(first, last)
+        for h, rows in enumerate(quarters):
             nc.vector.tensor_tensor(
-                a[:, :, part],
+                a[:, :, rows],
                 scores[h][:].rearrange("p (s m) -> p s m", s=4),
-                ts_g[:, :, part],
+                ts_free[:, :, rows],
                 MULT,
             )
         nc.vector.tensor_reduce(neg_m[:], a[:].rearrange("p s m -> p (s m)"), mybir.AxisListType.X, MAX, negate=True)
 
-        turned0 = turn_words(0, "scores0")
-        v_codes = keep.tile([P, D], U32, name="v_codes", tag="latents0", align_bytes=64)
+        turned0 = turn_pair(0, "scores0")
+        v_codes = keep.tile([P, D], U32, name="v_codes", tag="keys0", align_bytes=64)
         v_scales = keep.tile([P, D], U8, name="v_scales", align_bytes=64)
 
         def quantize_values(first, last, source):
             nc.vector.quantize_mx(out=v_codes[:, first:last].bitcast(FP8X4), scales=v_scales[:, first:last], in_=source)
 
-        quantize_values(256, 512, early[:].rearrange("p h c -> p (h c)"))
+        quantize_values(2 * P, 4 * P, values1[:].rearrange("p c x -> p (c x)"))
 
         prob = keep.tile([P, 4, N // 4], F32, name="prob")
         sums = keep.tile([P, 3], F32, name="sums")
@@ -200,60 +194,62 @@ def tile_attend_x_mla_append256_topk_kernel(tc, qT, cT, new_cT, ts, ch, offs, sl
             )
             nc.tensor.transpose(p_turned[:, s, :], prob[:, s, :], ident[:])
 
-        late = keep.tile([P, 2, 4 * P], BF16, name="late", tag="latents64", align_bytes=64)
-        for half in range(2):
-            copy_values(late[:], turned0, slice(half, half + 1))
+        values0 = keep.tile([P, 2, 4 * P], BF16, name="values0", tag="keys2", align_bytes=64)
+        for c in range(2):
+            copy_values(values0[:], turned0, slice(c, c + 1))
         total = keep.tile([P, 1], F32, name="total")
         inv = keep.tile([P, 1], F32, name="inv")
         nc.vector.tensor_reduce(sums[:, 0:1], prob[:, 0:2].rearrange("p s m -> p (s m)"), mybir.AxisListType.X, ADD)
+
         w_grouped = keep.tile([P, NQ, 4], BF16, name="w_grouped", align_bytes=64)
-        halves = [slice(0, NQ // 2), slice(NQ // 2, NQ)]
-        for rows in halves:
+        query_halves = [slice(0, NQ // 2), slice(NQ // 2, NQ)]
+        for queries in query_halves:
             nc.vector.tensor_tensor(
-                w_grouped[:, rows, :],
-                p_turned[:].rearrange("p s q -> p q s")[:, rows, :],
+                w_grouped[:, queries, :],
+                p_turned[:].rearrange("p s q -> p q s")[:, queries, :],
                 ts_col[:].unsqueeze(1).to_broadcast([P, NQ // 2, 4]),
                 MULT,
             )
         w_codes = keep.tile([P, NQ], U32, name="w_codes", align_bytes=64)
         w_scales = keep.tile([P, NQ], U8, name="w_scales", align_bytes=64)
 
-        def quantize_weights(rows):
+        def quantize_weights(queries):
             nc.vector.quantize_mx(
-                out=w_codes[:, rows].bitcast(FP8X4),
-                scales=w_scales[:, rows],
-                in_=w_grouped[:, rows, :].rearrange("p q s -> p (q s)"),
+                out=w_codes[:, queries].bitcast(FP8X4),
+                scales=w_scales[:, queries],
+                in_=w_grouped[:, queries, :].rearrange("p q s -> p (q s)"),
             )
 
-        quantize_weights(halves[0])
+        quantize_weights(query_halves[0])
         nc.vector.tensor_reduce(total[:], sums[:], mybir.AxisListType.X, ADD)
-        quantize_weights(halves[1])
-        quantize_values(0, 128, late[:, 0])
+        quantize_weights(query_halves[1])
+        quantize_values(0, P, values0[:, 0])
         nc.vector.reciprocal(inv[:], total[:])
-        quantize_values(128, 256, late[:, 1])
+        quantize_values(P, 2 * P, values0[:, 1])
 
         result = keep.tile([P, D], F32, name="result")
-        for half in range(2):
-            y = psum.tile([P, 2, P], F32, name=f"y{half}", tag=f"y{half}")
+        for c in range(2):
+            y = psum.tile([P, 2, P], F32, name=f"y{c}", tag=f"y{c}")
             for u in (1, 0):
-                cols = slice(256 * u + 128 * half, 256 * u + 128 * half + 128)
+                code_cols = slice(P * (2 * u + c), P * (2 * u + c + 1))
                 nc.tensor.matmul_mx(
                     out=y[:, u, :],
                     lhsT=w_codes[:].bitcast(FP8X4),
                     lhsT_scale=w_scales[:],
-                    rhs=v_codes[:, cols].bitcast(FP8X4),
-                    rhs_scale=v_scales[:, cols],
+                    rhs=v_codes[:, code_cols].bitcast(FP8X4),
+                    rhs_scale=v_scales[:, code_cols],
                     start=True,
                     stop=True,
                 )
-            fours = y[:].rearrange("p u (j m) -> p m (u j)", j=2)
-            for first, last in [(0, 64)] if half == 0 else [(0, 32), (32, 64)]:
-                cols = slice(256 * half + 4 * first, 256 * half + 4 * last)
+            in_order = y[:].rearrange("p u (j f) -> p f (u j)", j=2)
+            width = HALF_ROWS // (c + 1)
+            for first in range(0, HALF_ROWS, width):
+                cols = slice(4 * (HALF_ROWS * c + first), 4 * (HALF_ROWS * c + first + width))
                 nc.vector.scalar_tensor_tensor(
-                    result[:, cols].rearrange("p (m t) -> p m t", t=4),
-                    fours[:, first:last],
+                    result[:, cols].rearrange("p (f t) -> p f t", t=4),
+                    in_order[:, first : first + width],
                     inv[:],
-                    ch_sb[:, cols].rearrange("p (m t) -> p m t", t=4),
+                    ch_sb[:, cols].rearrange("p (f t) -> p f t", t=4),
                     MULT,
                     MULT,
                 )

@@ -22,8 +22,6 @@ D = 512
 NQ = 128
 ROWS = 32
 HALF_ROWS = 64
-ORDER = (0, 2, 3, 1)
-SCALAR_SHARE = {2: 384, 3: 352}
 
 FLOPS = 2 * NQ * N * D * 2
 
@@ -33,12 +31,14 @@ def tile_attend_x_mla_append256_topk_kernel(tc, qT, cT, new_cT, ts, ch, offs, sl
     with ExitStack() as ctx:
         lists = ctx.enter_context(tc.tile_pool(name="lists", bufs=1))
         keep = ctx.enter_context(tc.tile_pool(name="keep", bufs=1))
+        late = ctx.enter_context(tc.tile_pool(name="late", bufs=1))
         psum = ctx.enter_context(tc.psum_pool(name="psum", bufs=1))
 
         slots_sb = lists.tile([P, NEW // 16], U16, name="slots_sb")
         offs_sb = lists.tile([P, N // 16], U16, name="offs_sb")
 
-        new_sb = [keep.tile([P, NEW], F32, name=f"new{t}", align_bytes=64) for t in range(4)]
+        new_sb = [keep.tile([P, NEW], F32, name=f"new{t}", align_bytes=64) for t in range(3)]
+        new_sb.append(late.tile([P, NEW], F32, name="new3", offset=1536, align_bytes=64))
         pool = [keep.tile([P, T], F32, name=f"pool{t}", align_bytes=64) for t in range(4)]
         words_flat = keep.tile([P, 2 * N], U32, name="words_flat", align_bytes=64)
         words = words_flat[:].rearrange("p (u s m) -> p u s m", u=2, s=4)
@@ -51,11 +51,11 @@ def tile_attend_x_mla_append256_topk_kernel(tc, qT, cT, new_cT, ts, ch, offs, sl
         pool_view = cT.rearrange("(p j) w -> p j w", j=4)
 
         nc.scalar.dma_start(ts_sb[P - 1 : P, :], ts[0:1, :])
-        nc.sync.dma_start(offs_sb[:], offs)
         nc.sync.dma_start(pool[0][:], pool_view[:, 0, :])
         nc.sync.dma_start(slots_sb[:], slots)
         nc.sync.dma_start(new_sb[0][:], new_view[:, 0, :])
-        for t in ORDER[1:]:
+        nc.sync.dma_start(offs_sb[:], offs)
+        for t in range(1, 4):
             nc.sync.dma_start(pool[t][:], pool_view[:, t, :])
             nc.sync.dma_start(new_sb[t][:], new_view[:, t, :])
         nc.sync.dma_start(q_raw[:], qT[0].rearrange("(p j) w -> p j w", j=4))
@@ -71,45 +71,23 @@ def tile_attend_x_mla_append256_topk_kernel(tc, qT, cT, new_cT, ts, ch, offs, sl
 
         nc.vector.memset(ts_sb[0 : P - 1, :], 0.0)
         ts_row = keep.tile([P, N], F32, name="ts_row", align_bytes=64)
-        nc.vector.tensor_copy(ts_row[:], ts_sb[:].indirect(offs_sb[:]))
+        nc.scalar.activation(out=ts_row[:], in_=ts_sb[:].indirect(offs_sb[:]), func=ACT.Copy)
         ts_turned = psum.tile([P, 4, P], F32, name="ts_turned", tag="p_turned")
         for s in range(4):
             nc.tensor.transpose(ts_turned[:, s, :], ts_row[:].rearrange("p (m s) -> p s m", s=4)[:, s, :], ident[:])
 
-        q_scales = keep.tile([P, NQ], U8, name="q_scales", align_bytes=64)
+        def scatter_on_vector(t, first, last):
+            nc.vector.tensor_copy(pool[t][:].indirect(slots_sb[:, first // 16 : last // 16]), new_sb[t][:, first:last])
 
-        for t in ORDER:
-            nc.vector.tensor_copy(pool[t][:].indirect(slots_sb[:]), new_sb[t][:])
+        def scatter_on_scalar(t, first, last):
+            nc.scalar.activation(
+                out=pool[t][:].indirect(slots_sb[:, first // 16 : last // 16]), in_=new_sb[t][:, first:last], func=ACT.Copy
+            )
 
-        rounded = {t: keep.tile([P, T], BF16, name=f"rounded{t}", tag=f"rounded{t}", align_bytes=64) for t in ORDER[:3]}
-        ts_spread = psum.tile([P, 4, P], F32, name="ts_spread", tag="y0")
-
-        def round_shared(t):
-            share = SCALAR_SHARE[t]
-            nc.scalar.activation(out=rounded[t][:, :share], in_=pool[t][:, :share], func=ACT.Copy)
-            nc.gpsimd.tensor_copy(rounded[t][:, share:], pool[t][:, share:])
-
-        def gather_rounded(t, parts):
-            rows = P // parts
-            for first in range(0, P, rows):
-                nc.scalar.activation(
-                    out=halves[:, t // 2, t % 2, first : first + rows],
-                    in_=rounded[t][:].indirect(offs_sb[:, first // 4 : (first + rows) // 4]),
-                    func=ACT.Copy,
-                )
-
-        nc.scalar.activation(out=rounded[0][:], in_=pool[0][:], func=ACT.Copy)
-        gather_rounded(0, 1)
-        ts_col = keep.tile([P, 4], F32, name="ts_col", tag="rounded0", align_bytes=64)
-        nc.vector.tensor_copy(ts_col[:], ts_turned[:, :, P - 1])
-        for s in range(4):
-            nc.tensor.transpose(ts_spread[:, s, :], ts_col[:, s : s + 1].to_broadcast([P, P]), ident[:])
-        round_shared(2)
-        gather_rounded(2, 1)
-        round_shared(3)
-        q_bf = keep.tile([P, NQ, 4], BF16, name="q_bf", align_bytes=64)
-        nc.gpsimd.tensor_copy(q_bf[:], q_raw[:].rearrange("p j q -> p q j"))
-        gather_rounded(3, 2)
+        def gather(t, rows):
+            nc.vector.tensor_copy(
+                halves[:, t // 2, t % 2, rows], pool[t][:].indirect(offs_sb[:, rows.start // 4 : rows.stop // 4])
+            )
 
         word_floats = words.bitcast(F32)
 
@@ -119,22 +97,46 @@ def tile_attend_x_mla_append256_topk_kernel(tc, qT, cT, new_cT, ts, ch, offs, sl
                 nc.tensor.transpose(turned[:, s, :], word_floats[:, u, s, :], ident[:])
             return turned
 
-        def copy_values(values, turned, part):
+        def copy_values(values, turned, c):
             bank = turned[:].rearrange("p s f -> p (s f)").bitcast(BF16)
             nc.scalar.copy(
-                values.rearrange("p c (j f s) -> p c f j s", j=2, s=4)[:, part],
-                bank.rearrange("p (s c f j) -> p c f j s", s=4, c=2, j=2)[:, part],
+                values.rearrange("p (j f s) -> p f j s", j=2, s=4),
+                bank.rearrange("p (s c f j) -> p c f j s", s=4, c=2, j=2)[:, c],
             )
 
-        turned1 = turn_pair(1, "turned1")
-
+        everything = slice(0, P)
         quarters = [slice(ROWS * h, ROWS * (h + 1)) for h in range(4)]
+        scatter_on_vector(0, 0, NEW)
+        gather(0, everything)
+        scatter_on_scalar(1, 0, NEW)
+        ts_col = keep.tile([P, 4], F32, name="ts_col", tag="new1", align_bytes=64)
+        nc.scalar.copy(ts_col[:], ts_turned[:, :, P - 1])
+        ts_spread = psum.tile([P, 4, P], F32, name="ts_spread", tag="y0")
+        for s in range(4):
+            nc.tensor.transpose(ts_spread[:, s, :], ts_col[:, s : s + 1].to_broadcast([P, P]), ident[:])
+        gather(1, everything)
+        turned0 = turn_pair(0, "turned0")
+        scatter_on_scalar(2, 0, NEW // 2)
+        scatter_on_vector(2, NEW // 2, NEW)
+        gather(2, everything)
+        scatter_on_scalar(3, 0, NEW)
+
+        ts_free = late.tile([P, 4, P], F32, name="ts_free", offset=0, align_bytes=64)
+        nc.scalar.copy(ts_free[:], ts_spread[:])
+        values00 = late.tile([P, 4 * P], BF16, name="values00", offset=2048, align_bytes=64)
+        copy_values(values00[:], turned0, 0)
+
+        q_bf = keep.tile([P, NQ, 4], BF16, name="q_bf", align_bytes=64)
+        nc.gpsimd.tensor_copy(q_bf[:], q_raw[:].rearrange("p j q -> p q j"))
+
         keys = [keep.tile([P, 4, ROWS, 2], U32, name=f"keys{h}", tag=f"keys{h}", align_bytes=64) for h in range(4)]
-        for h, rows in enumerate(quarters):
-            nc.vector.tensor_copy(halves[:, 0, 1, rows], pool[1][:].indirect(offs_sb[:, 8 * h : 8 * h + 8]))
+        for rows in quarters:
+            gather(3, rows)
         for h, rows in enumerate(quarters):
             nc.scalar.copy(keys[h][:], words.rearrange("p u s m -> p s m u")[:, :, rows, :])
+        turned1 = turn_pair(1, "y1")
         q_codes = keep.tile([P, NQ], U32, name="q_codes", align_bytes=64)
+        q_scales = keep.tile([P, NQ], U8, name="q_scales", align_bytes=64)
         nc.vector.quantize_mx(
             out=q_codes[:].bitcast(FP8X4), scales=q_scales[:], in_=q_bf[:].rearrange("p q j -> p (q j)")
         )
@@ -158,12 +160,11 @@ def tile_attend_x_mla_append256_topk_kernel(tc, qT, cT, new_cT, ts, ch, offs, sl
                 stop=True,
             )
 
-        ts_free = keep.tile([P, 4, P], F32, name="ts_free", tag="keys0", align_bytes=64)
-        for c in range(2):
-            rows = slice(HALF_ROWS * c, HALF_ROWS * (c + 1))
-            nc.scalar.copy(ts_free[:, :, rows], ts_spread[:, :, rows])
+        values01 = keep.tile([P, 4 * P], BF16, name="values01", tag="keys0", align_bytes=64)
+        copy_values(values01[:], turned0, 1)
         values1 = keep.tile([P, 2, 4 * P], BF16, name="values1", tag="keys1", align_bytes=64)
-        copy_values(values1[:], turned1, slice(0, 2))
+        for c in range(2):
+            copy_values(values1[:, c], turned1, c)
 
         a = keep.tile([P, 4, N // 4], F32, name="a", tag="keys2", align_bytes=64)
         neg_m = keep.tile([P, 1], F32, name="neg_m")
@@ -176,13 +177,14 @@ def tile_attend_x_mla_append256_topk_kernel(tc, qT, cT, new_cT, ts, ch, offs, sl
             )
         nc.vector.tensor_reduce(neg_m[:], a[:].rearrange("p s m -> p (s m)"), mybir.AxisListType.X, MAX, negate=True)
 
-        turned0 = turn_pair(0, "scores0")
-        v_codes = keep.tile([P, D], U32, name="v_codes", tag="keys0", align_bytes=64)
+        v_codes = late.tile([P, D], U32, name="v_codes", offset=0, align_bytes=64)
         v_scales = keep.tile([P, D], U8, name="v_scales", align_bytes=64)
 
         def quantize_values(first, last, source):
             nc.vector.quantize_mx(out=v_codes[:, first:last].bitcast(FP8X4), scales=v_scales[:, first:last], in_=source)
 
+        quantize_values(0, P, values00[:])
+        quantize_values(P, 2 * P, values01[:])
         quantize_values(2 * P, 4 * P, values1[:].rearrange("p c x -> p (c x)"))
 
         prob = keep.tile([P, 4, N // 4], F32, name="prob")
@@ -194,9 +196,6 @@ def tile_attend_x_mla_append256_topk_kernel(tc, qT, cT, new_cT, ts, ch, offs, sl
             )
             nc.tensor.transpose(p_turned[:, s, :], prob[:, s, :], ident[:])
 
-        values0 = keep.tile([P, 2, 4 * P], BF16, name="values0", tag="keys2", align_bytes=64)
-        for c in range(2):
-            copy_values(values0[:], turned0, slice(c, c + 1))
         total = keep.tile([P, 1], F32, name="total")
         inv = keep.tile([P, 1], F32, name="inv")
         nc.vector.tensor_reduce(sums[:, 0:1], prob[:, 0:2].rearrange("p s m -> p (s m)"), mybir.AxisListType.X, ADD)
@@ -223,9 +222,7 @@ def tile_attend_x_mla_append256_topk_kernel(tc, qT, cT, new_cT, ts, ch, offs, sl
         quantize_weights(query_halves[0])
         nc.vector.tensor_reduce(total[:], sums[:], mybir.AxisListType.X, ADD)
         quantize_weights(query_halves[1])
-        quantize_values(0, P, values0[:, 0])
         nc.vector.reciprocal(inv[:], total[:])
-        quantize_values(P, 2 * P, values0[:, 1])
 
         result = keep.tile([P, D], F32, name="result")
         for c in range(2):

@@ -51,10 +51,10 @@ def tile_attend_x_mla_append256_topk_kernel(tc, qT, cT, new_cT, ts, ch, offs, sl
         pool_view = cT.rearrange("(p j) w -> p j w", j=4)
 
         nc.scalar.dma_start(ts_sb[P - 1 : P, :], ts[0:1, :])
+        nc.sync.dma_start(offs_sb[:], offs)
         nc.sync.dma_start(pool[0][:], pool_view[:, 0, :])
         nc.sync.dma_start(slots_sb[:], slots)
         nc.sync.dma_start(new_sb[0][:], new_view[:, 0, :])
-        nc.sync.dma_start(offs_sb[:], offs)
         for t in range(1, 4):
             nc.sync.dma_start(pool[t][:], pool_view[:, t, :])
             nc.sync.dma_start(new_sb[t][:], new_view[:, t, :])
@@ -106,6 +106,15 @@ def tile_attend_x_mla_append256_topk_kernel(tc, qT, cT, new_cT, ts, ch, offs, sl
 
         everything = slice(0, P)
         quarters = [slice(ROWS * h, ROWS * (h + 1)) for h in range(4)]
+        def gather_row(row, rows):
+            nc.scalar.activation(
+                out=row[:], in_=pool[1][:].indirect(offs_sb[:, rows.start // 4 : rows.stop // 4]), func=ACT.Copy
+            )
+
+        def place_views(row, rows):
+            return halves[:, 0, 1, rows].rearrange("p m s -> p s m"), row[:].rearrange("p (m s) -> p s m", s=4)
+
+        early, rest = slice(0, 3 * ROWS), quarters[3]
         scatter_on_vector(0, 0, NEW)
         gather(0, everything)
         scatter_on_scalar(1, 0, NEW)
@@ -114,17 +123,20 @@ def tile_attend_x_mla_append256_topk_kernel(tc, qT, cT, new_cT, ts, ch, offs, sl
         ts_spread = psum.tile([P, 4, P], F32, name="ts_spread", tag="y0")
         for s in range(4):
             nc.tensor.transpose(ts_spread[:, s, :], ts_col[:, s : s + 1].to_broadcast([P, P]), ident[:])
-        gather(1, everything)
-        turned0 = turn_pair(0, "turned0")
-        scatter_on_scalar(2, 0, NEW // 2)
-        scatter_on_vector(2, NEW // 2, NEW)
+        row_early = keep.tile([P, 4 * 3 * ROWS], BF16, name="row_early", tag="pool0", align_bytes=64)
+        gather_row(row_early, early)
+        nc.gpsimd.tensor_copy(*place_views(row_early, early))
+        scatter_on_vector(2, 0, NEW)
         gather(2, everything)
         scatter_on_scalar(3, 0, NEW)
-
+        row_rest = late.tile([P, 4 * ROWS], BF16, name="row_rest", offset=2048, align_bytes=64)
+        gather_row(row_rest, rest)
         ts_free = late.tile([P, 4, P], F32, name="ts_free", offset=0, align_bytes=64)
-        nc.scalar.copy(ts_free[:], ts_spread[:])
-        values00 = late.tile([P, 4 * P], BF16, name="values00", offset=2048, align_bytes=64)
-        copy_values(values00[:], turned0, 0)
+        for c in range(2):
+            rows = slice(HALF_ROWS * c, HALF_ROWS * (c + 1))
+            nc.scalar.copy(ts_free[:, :, rows], ts_spread[:, :, rows])
+        nc.scalar.copy(*place_views(row_rest, rest))
+        turned0 = turn_pair(0, "turned0")
 
         q_bf = keep.tile([P, NQ, 4], BF16, name="q_bf", align_bytes=64)
         nc.gpsimd.tensor_copy(q_bf[:], q_raw[:].rearrange("p j q -> p q j"))
@@ -134,7 +146,6 @@ def tile_attend_x_mla_append256_topk_kernel(tc, qT, cT, new_cT, ts, ch, offs, sl
             gather(3, rows)
         for h, rows in enumerate(quarters):
             nc.scalar.copy(keys[h][:], words.rearrange("p u s m -> p s m u")[:, :, rows, :])
-        turned1 = turn_pair(1, "y1")
         q_codes = keep.tile([P, NQ], U32, name="q_codes", align_bytes=64)
         q_scales = keep.tile([P, NQ], U8, name="q_scales", align_bytes=64)
         nc.vector.quantize_mx(
@@ -160,11 +171,9 @@ def tile_attend_x_mla_append256_topk_kernel(tc, qT, cT, new_cT, ts, ch, offs, sl
                 stop=True,
             )
 
-        values01 = keep.tile([P, 4 * P], BF16, name="values01", tag="keys0", align_bytes=64)
-        copy_values(values01[:], turned0, 1)
-        values1 = keep.tile([P, 2, 4 * P], BF16, name="values1", tag="keys1", align_bytes=64)
+        values0 = keep.tile([P, 2, 4 * P], BF16, name="values0", tag="keys1", align_bytes=64)
         for c in range(2):
-            copy_values(values1[:, c], turned1, c)
+            copy_values(values0[:, c], turned0, c)
 
         a = keep.tile([P, 4, N // 4], F32, name="a", tag="keys2", align_bytes=64)
         neg_m = keep.tile([P, 1], F32, name="neg_m")
@@ -183,9 +192,8 @@ def tile_attend_x_mla_append256_topk_kernel(tc, qT, cT, new_cT, ts, ch, offs, sl
         def quantize_values(first, last, source):
             nc.vector.quantize_mx(out=v_codes[:, first:last].bitcast(FP8X4), scales=v_scales[:, first:last], in_=source)
 
-        quantize_values(0, P, values00[:])
-        quantize_values(P, 2 * P, values01[:])
-        quantize_values(2 * P, 4 * P, values1[:].rearrange("p c x -> p (c x)"))
+        quantize_values(0, 2 * P, values0[:].rearrange("p c x -> p (c x)"))
+        turned1 = turn_pair(1, "scores0")
 
         prob = keep.tile([P, 4, N // 4], F32, name="prob")
         sums = keep.tile([P, 3], F32, name="sums")
@@ -196,6 +204,9 @@ def tile_attend_x_mla_append256_topk_kernel(tc, qT, cT, new_cT, ts, ch, offs, sl
             )
             nc.tensor.transpose(p_turned[:, s, :], prob[:, s, :], ident[:])
 
+        values1 = keep.tile([P, 2, 4 * P], BF16, name="values1", tag="keys2", align_bytes=64)
+        for c in range(2):
+            copy_values(values1[:, c], turned1, c)
         total = keep.tile([P, 1], F32, name="total")
         inv = keep.tile([P, 1], F32, name="inv")
         nc.vector.tensor_reduce(sums[:, 0:1], prob[:, 0:2].rearrange("p s m -> p (s m)"), mybir.AxisListType.X, ADD)
@@ -222,12 +233,14 @@ def tile_attend_x_mla_append256_topk_kernel(tc, qT, cT, new_cT, ts, ch, offs, sl
         quantize_weights(query_halves[0])
         nc.vector.tensor_reduce(total[:], sums[:], mybir.AxisListType.X, ADD)
         quantize_weights(query_halves[1])
+        quantize_values(2 * P, 3 * P, values1[:, 0])
         nc.vector.reciprocal(inv[:], total[:])
+        quantize_values(3 * P, 4 * P, values1[:, 1])
 
         result = keep.tile([P, D], F32, name="result")
         for c in range(2):
             y = psum.tile([P, 2, P], F32, name=f"y{c}", tag=f"y{c}")
-            for u in (1, 0):
+            for u in range(2):
                 code_cols = slice(P * (2 * u + c), P * (2 * u + c + 1))
                 nc.tensor.matmul_mx(
                     out=y[:, u, :],

@@ -31,14 +31,12 @@ def tile_attend_x_mla_append256_topk_kernel(tc, qT, cT, new_cT, ts, ch, offs, sl
     with ExitStack() as ctx:
         lists = ctx.enter_context(tc.tile_pool(name="lists", bufs=1))
         keep = ctx.enter_context(tc.tile_pool(name="keep", bufs=1))
-        late = ctx.enter_context(tc.tile_pool(name="late", bufs=1))
         psum = ctx.enter_context(tc.psum_pool(name="psum", bufs=1))
 
         slots_sb = lists.tile([P, NEW // 16], U16, name="slots_sb")
         offs_sb = lists.tile([P, N // 16], U16, name="offs_sb")
 
-        new_sb = [keep.tile([P, NEW], F32, name=f"new{t}", align_bytes=64) for t in range(3)]
-        new_sb.append(late.tile([P, NEW], F32, name="new3", offset=1536, align_bytes=64))
+        new_sb = [keep.tile([P, NEW], F32, name=f"new{t}", align_bytes=64) for t in range(4)]
         pool = [keep.tile([P, T], F32, name=f"pool{t}", align_bytes=64) for t in range(4)]
         words_flat = keep.tile([P, 2 * N], U32, name="words_flat", align_bytes=64)
         words = words_flat[:].rearrange("p (u s m) -> p u s m", u=2, s=4)
@@ -106,44 +104,36 @@ def tile_attend_x_mla_append256_topk_kernel(tc, qT, cT, new_cT, ts, ch, offs, sl
 
         everything = slice(0, P)
         quarters = [slice(ROWS * h, ROWS * (h + 1)) for h in range(4)]
-        def gather_row(row, rows):
+        def gather_and_place(t, rows, tag):
+            row = keep.tile([P, 4 * (rows.stop - rows.start)], BF16, name=f"row_{tag}", tag=tag, align_bytes=64)
             nc.scalar.activation(
-                out=row[:], in_=pool[1][:].indirect(offs_sb[:, rows.start // 4 : rows.stop // 4]), func=ACT.Copy
+                out=row[:], in_=pool[t][:].indirect(offs_sb[:, rows.start // 4 : rows.stop // 4]), func=ACT.Copy
+            )
+            nc.gpsimd.tensor_copy(
+                halves[:, t // 2, t % 2, rows].rearrange("p m s -> p s m"), row[:].rearrange("p (m s) -> p s m", s=4)
             )
 
-        def place_views(row, rows):
-            return halves[:, 0, 1, rows].rearrange("p m s -> p s m"), row[:].rearrange("p (m s) -> p s m", s=4)
-
-        early, rest = slice(0, 3 * ROWS), quarters[3]
         scatter_on_vector(0, 0, NEW)
         gather(0, everything)
         scatter_on_scalar(1, 0, NEW)
-        ts_col = keep.tile([P, 4], F32, name="ts_col", tag="new1", align_bytes=64)
-        nc.scalar.copy(ts_col[:], ts_turned[:, :, P - 1])
+        gather_and_place(1, everything, "pool0")
+        scatter_on_vector(2, 0, NEW)
+        ts_col = keep.tile([P, 4], F32, name="ts_col", tag="new2", align_bytes=64)
+        nc.vector.tensor_copy(ts_col[:], ts_turned[:, :, P - 1])
         ts_spread = psum.tile([P, 4, P], F32, name="ts_spread", tag="y0")
         for s in range(4):
             nc.tensor.transpose(ts_spread[:, s, :], ts_col[:, s : s + 1].to_broadcast([P, P]), ident[:])
-        row_early = keep.tile([P, 4 * 3 * ROWS], BF16, name="row_early", tag="pool0", align_bytes=64)
-        gather_row(row_early, early)
-        nc.gpsimd.tensor_copy(*place_views(row_early, early))
-        scatter_on_vector(2, 0, NEW)
         gather(2, everything)
         scatter_on_scalar(3, 0, NEW)
-        row_rest = late.tile([P, 4 * ROWS], BF16, name="row_rest", offset=2048, align_bytes=64)
-        gather_row(row_rest, rest)
-        ts_free = late.tile([P, 4, P], F32, name="ts_free", offset=0, align_bytes=64)
-        for c in range(2):
-            rows = slice(HALF_ROWS * c, HALF_ROWS * (c + 1))
-            nc.scalar.copy(ts_free[:, :, rows], ts_spread[:, :, rows])
-        nc.scalar.copy(*place_views(row_rest, rest))
         turned0 = turn_pair(0, "turned0")
 
         q_bf = keep.tile([P, NQ, 4], BF16, name="q_bf", align_bytes=64)
         nc.gpsimd.tensor_copy(q_bf[:], q_raw[:].rearrange("p j q -> p q j"))
 
         keys = [keep.tile([P, 4, ROWS, 2], U32, name=f"keys{h}", tag=f"keys{h}", align_bytes=64) for h in range(4)]
-        for rows in quarters:
+        for rows in quarters[:3]:
             gather(3, rows)
+        gather_and_place(3, quarters[3], "pool2")
         for h, rows in enumerate(quarters):
             nc.scalar.copy(keys[h][:], words.rearrange("p u s m -> p s m u")[:, :, rows, :])
         q_codes = keep.tile([P, NQ], U32, name="q_codes", align_bytes=64)
@@ -171,6 +161,10 @@ def tile_attend_x_mla_append256_topk_kernel(tc, qT, cT, new_cT, ts, ch, offs, sl
                 stop=True,
             )
 
+        ts_free = keep.tile([P, 4, P], F32, name="ts_free", tag="keys0", align_bytes=64)
+        for c in range(2):
+            rows = slice(HALF_ROWS * c, HALF_ROWS * (c + 1))
+            nc.scalar.copy(ts_free[:, :, rows], ts_spread[:, :, rows])
         values0 = keep.tile([P, 2, 4 * P], BF16, name="values0", tag="keys1", align_bytes=64)
         for c in range(2):
             copy_values(values0[:, c], turned0, c)
@@ -186,7 +180,7 @@ def tile_attend_x_mla_append256_topk_kernel(tc, qT, cT, new_cT, ts, ch, offs, sl
             )
         nc.vector.tensor_reduce(neg_m[:], a[:].rearrange("p s m -> p (s m)"), mybir.AxisListType.X, MAX, negate=True)
 
-        v_codes = late.tile([P, D], U32, name="v_codes", offset=0, align_bytes=64)
+        v_codes = keep.tile([P, D], U32, name="v_codes", tag="keys0", align_bytes=64)
         v_scales = keep.tile([P, D], U8, name="v_scales", align_bytes=64)
 
         def quantize_values(first, last, source):

@@ -59,11 +59,6 @@ def tile_attend_x_mla_append256_topk_kernel(tc, qT, cT, new_cT, ts, ch, offs, sl
         nc.sync.dma_start(q_raw[:], qT[0].rearrange("(p j) w -> p j w", j=4))
         nc.sync.dma_start(ch_sb[:], ch)
 
-        warm = keep.tile([P, 1], F32, name="warm")
-        nc.vector.memset(warm[:], 0.0)
-        warm_out = keep.tile([P, 1], F32, name="warm_out")
-        nc.scalar.activation(out=warm_out[:], in_=warm[:], func=ACT.Exp)
-
         ident = keep.tile([P, P], F32, name="ident")
         make_identity(nc, ident[:])
 
@@ -104,28 +99,38 @@ def tile_attend_x_mla_append256_topk_kernel(tc, qT, cT, new_cT, ts, ch, offs, sl
 
         everything = slice(0, P)
         quarters = [slice(ROWS * h, ROWS * (h + 1)) for h in range(4)]
-        def gather_and_place(t, rows, tag):
+        def gather_and_place(t, rows, tag, on_scalar, placer):
             row = keep.tile([P, 4 * (rows.stop - rows.start)], BF16, name=f"row_{tag}", tag=tag, align_bytes=64)
-            nc.scalar.activation(
-                out=row[:], in_=pool[t][:].indirect(offs_sb[:, rows.start // 4 : rows.stop // 4]), func=ACT.Copy
-            )
-            nc.gpsimd.tensor_copy(
+            window = pool[t][:].indirect(offs_sb[:, rows.start // 4 : rows.stop // 4])
+            if on_scalar:
+                nc.scalar.activation(out=row[:], in_=window, func=ACT.Copy)
+            else:
+                nc.vector.tensor_copy(row[:], window)
+            placer.tensor_copy(
                 halves[:, t // 2, t % 2, rows].rearrange("p m s -> p s m"), row[:].rearrange("p (m s) -> p s m", s=4)
             )
 
         scatter_on_vector(0, 0, NEW)
         gather(0, everything)
         scatter_on_scalar(1, 0, NEW)
-        gather_and_place(1, everything, "pool0")
-        scatter_on_vector(2, 0, NEW)
-        ts_col = keep.tile([P, 4], F32, name="ts_col", tag="new2", align_bytes=64)
-        nc.vector.tensor_copy(ts_col[:], ts_turned[:, :, P - 1])
+        ts_col = keep.tile([P, 4], F32, name="ts_col", tag="new1", align_bytes=64)
+        nc.scalar.copy(ts_col[:], ts_turned[:, :, P - 1])
         ts_spread = psum.tile([P, 4, P], F32, name="ts_spread", tag="y0")
         for s in range(4):
             nc.tensor.transpose(ts_spread[:, s, :], ts_col[:, s : s + 1].to_broadcast([P, P]), ident[:])
+        gather_and_place(1, slice(0, 3 * ROWS), "pool0", True, nc.gpsimd)
+        scatter_on_vector(2, 0, NEW)
+        gather_and_place(1, quarters[3], "new2", False, nc.gpsimd)
         gather(2, everything)
         scatter_on_scalar(3, 0, NEW)
-        turned0 = turn_pair(0, "turned0")
+        turned0 = turn_pair(0, "p_turned")
+
+        def copy_spread(c, tag):
+            half = keep.tile([P, 4, HALF_ROWS], F32, name=f"ts_free{c}", tag=tag, align_bytes=64)
+            nc.scalar.copy(half[:], ts_spread[:, :, HALF_ROWS * c : HALF_ROWS * (c + 1)])
+            return half
+
+        ts_free = [copy_spread(0, "new3")]
 
         q_bf = keep.tile([P, NQ, 4], BF16, name="q_bf", align_bytes=64)
         nc.gpsimd.tensor_copy(q_bf[:], q_raw[:].rearrange("p j q -> p q j"))
@@ -133,7 +138,7 @@ def tile_attend_x_mla_append256_topk_kernel(tc, qT, cT, new_cT, ts, ch, offs, sl
         keys = [keep.tile([P, 4, ROWS, 2], U32, name=f"keys{h}", tag=f"keys{h}", align_bytes=64) for h in range(4)]
         for rows in quarters[:3]:
             gather(3, rows)
-        gather_and_place(3, quarters[3], "pool2")
+        gather_and_place(3, quarters[3], "row3", True, nc.vector)
         for h, rows in enumerate(quarters):
             nc.scalar.copy(keys[h][:], words.rearrange("p u s m -> p s m u")[:, :, rows, :])
         q_codes = keep.tile([P, NQ], U32, name="q_codes", align_bytes=64)
@@ -161,10 +166,7 @@ def tile_attend_x_mla_append256_topk_kernel(tc, qT, cT, new_cT, ts, ch, offs, sl
                 stop=True,
             )
 
-        ts_free = keep.tile([P, 4, P], F32, name="ts_free", tag="keys0", align_bytes=64)
-        for c in range(2):
-            rows = slice(HALF_ROWS * c, HALF_ROWS * (c + 1))
-            nc.scalar.copy(ts_free[:, :, rows], ts_spread[:, :, rows])
+        ts_free.append(copy_spread(1, "keys0"))
         values0 = keep.tile([P, 2, 4 * P], BF16, name="values0", tag="keys1", align_bytes=64)
         for c in range(2):
             copy_values(values0[:, c], turned0, c)
@@ -175,7 +177,7 @@ def tile_attend_x_mla_append256_topk_kernel(tc, qT, cT, new_cT, ts, ch, offs, sl
             nc.vector.tensor_tensor(
                 a[:, :, rows],
                 scores[h][:].rearrange("p (s m) -> p s m", s=4),
-                ts_free[:, :, rows],
+                ts_free[h // 2][:, :, quarters[h % 2]],
                 MULT,
             )
         nc.vector.tensor_reduce(neg_m[:], a[:].rearrange("p s m -> p (s m)"), mybir.AxisListType.X, MAX, negate=True)

@@ -93,8 +93,8 @@ def tile_attend_x_mla_append256_topk_kernel(tc, qT, cT, new_cT, ts, ch, offs, sl
         def copy_values(values, turned, c):
             bank = turned[:].rearrange("p s f -> p (s f)").bitcast(BF16)
             nc.scalar.copy(
-                values.rearrange("p (j f s) -> p f j s", j=2, s=4),
-                bank.rearrange("p (s c f j) -> p c f j s", s=4, c=2, j=2)[:, c],
+                values.rearrange("p (k j f s) -> p k f j s", k=2, j=2, s=4),
+                bank.rearrange("p (s c k f j) -> p c k f j s", s=4, c=2, k=2, j=2)[:, c],
             )
 
         everything = slice(0, P)
@@ -135,11 +135,15 @@ def tile_attend_x_mla_append256_topk_kernel(tc, qT, cT, new_cT, ts, ch, offs, sl
         q_bf = keep.tile([P, NQ, 4], BF16, name="q_bf", align_bytes=64)
         nc.gpsimd.tensor_copy(q_bf[:], q_raw[:].rearrange("p j q -> p q j"))
 
-        keys = [keep.tile([P, 4, ROWS, 2], U32, name=f"keys{h}", tag=f"keys{h}", align_bytes=64) for h in range(4)]
+        pieces = quarters[:3] + [slice(3 * ROWS, 3 * ROWS + ROWS // 2), slice(3 * ROWS + ROWS // 2, P)]
+        keys = [
+            keep.tile([P, 4, rows.stop - rows.start, 2], U32, name=f"keys{h}", tag=f"keys{h}", align_bytes=64)
+            for h, rows in enumerate(pieces)
+        ]
         for rows in quarters[:3]:
             gather(3, rows)
         gather_and_place(3, quarters[3], "row3", True, nc.vector)
-        for h, rows in enumerate(quarters):
+        for h, rows in enumerate(pieces):
             nc.scalar.copy(keys[h][:], words.rearrange("p u s m -> p s m u")[:, :, rows, :])
         q_codes = keep.tile([P, NQ], U32, name="q_codes", align_bytes=64)
         q_scales = keep.tile([P, NQ], U8, name="q_scales", align_bytes=64)
@@ -147,10 +151,12 @@ def tile_attend_x_mla_append256_topk_kernel(tc, qT, cT, new_cT, ts, ch, offs, sl
             out=q_codes[:].bitcast(FP8X4), scales=q_scales[:], in_=q_bf[:].rearrange("p q j -> p (q j)")
         )
 
-        scores = [psum.tile([P, P], F32, name=f"scores{h}", tag=f"scores{h}") for h in range(4)]
-        for h in range(4):
-            k_codes = keep.tile([P, P], U32, name=f"k_codes{h}", align_bytes=64)
-            k_scales = keep.tile([P, P], U8, name=f"k_scales{h}", align_bytes=64)
+        scores = []
+        for h, rows in enumerate(pieces):
+            width = 4 * (rows.stop - rows.start)
+            scores.append(psum.tile([P, width], F32, name=f"scores{h}", tag=f"scores{h}"))
+            k_codes = keep.tile([P, width], U32, name=f"k_codes{h}", align_bytes=64)
+            k_scales = keep.tile([P, width], U8, name=f"k_scales{h}", align_bytes=64)
             nc.vector.quantize_mx(
                 out=k_codes[:].bitcast(FP8X4),
                 scales=k_scales[:],
@@ -173,11 +179,12 @@ def tile_attend_x_mla_append256_topk_kernel(tc, qT, cT, new_cT, ts, ch, offs, sl
 
         a = keep.tile([P, 4, N // 4], F32, name="a", tag="keys2", align_bytes=64)
         neg_m = keep.tile([P, 1], F32, name="neg_m")
-        for h, rows in enumerate(quarters):
+        for h, rows in enumerate(pieces):
+            c = rows.start // HALF_ROWS
             nc.vector.tensor_tensor(
                 a[:, :, rows],
                 scores[h][:].rearrange("p (s m) -> p s m", s=4),
-                ts_free[h // 2][:, :, quarters[h % 2]],
+                ts_free[c][:, :, rows.start - HALF_ROWS * c : rows.stop - HALF_ROWS * c],
                 MULT,
             )
         nc.vector.tensor_reduce(neg_m[:], a[:].rearrange("p s m -> p (s m)"), mybir.AxisListType.X, MAX, negate=True)
@@ -185,10 +192,13 @@ def tile_attend_x_mla_append256_topk_kernel(tc, qT, cT, new_cT, ts, ch, offs, sl
         v_codes = keep.tile([P, D], U32, name="v_codes", tag="keys0", align_bytes=64)
         v_scales = keep.tile([P, D], U8, name="v_scales", align_bytes=64)
 
-        def quantize_values(first, last, source):
-            nc.vector.quantize_mx(out=v_codes[:, first:last].bitcast(FP8X4), scales=v_scales[:, first:last], in_=source)
+        def quantize_values(u, part, values):
+            cols = slice(P * part + HALF_ROWS * u, P * part + HALF_ROWS * (u + 1))
+            source = values[:].rearrange("p c (k x) -> p (c k) x", k=2)[:, part]
+            nc.vector.quantize_mx(out=v_codes[:, cols].bitcast(FP8X4), scales=v_scales[:, cols], in_=source)
 
-        quantize_values(0, 2 * P, values0[:].rearrange("p c x -> p (c x)"))
+        for part in range(4):
+            quantize_values(0, part, values0)
         turned1 = turn_pair(1, "scores0")
 
         prob = keep.tile([P, 4, N // 4], F32, name="prob")
@@ -206,6 +216,8 @@ def tile_attend_x_mla_append256_topk_kernel(tc, qT, cT, new_cT, ts, ch, offs, sl
         total = keep.tile([P, 1], F32, name="total")
         inv = keep.tile([P, 1], F32, name="inv")
         nc.vector.tensor_reduce(sums[:, 0:1], prob[:, 0:2].rearrange("p s m -> p (s m)"), mybir.AxisListType.X, ADD)
+        nc.vector.tensor_reduce(total[:], sums[:], mybir.AxisListType.X, ADD)
+        nc.vector.reciprocal(inv[:], total[:])
 
         w_grouped = keep.tile([P, NQ, 4], BF16, name="w_grouped", align_bytes=64)
         query_halves = [slice(0, NQ // 2), slice(NQ // 2, NQ)]
@@ -227,36 +239,32 @@ def tile_attend_x_mla_append256_topk_kernel(tc, qT, cT, new_cT, ts, ch, offs, sl
             )
 
         quantize_weights(query_halves[0])
-        nc.vector.tensor_reduce(total[:], sums[:], mybir.AxisListType.X, ADD)
+        quantize_values(1, 0, values1)
         quantize_weights(query_halves[1])
-        quantize_values(2 * P, 3 * P, values1[:, 0])
-        nc.vector.reciprocal(inv[:], total[:])
-        quantize_values(3 * P, 4 * P, values1[:, 1])
+        for part in range(1, 4):
+            quantize_values(1, part, values1)
 
         result = keep.tile([P, D], F32, name="result")
-        for c in range(2):
-            y = psum.tile([P, 2, P], F32, name=f"y{c}", tag=f"y{c}")
-            for u in range(2):
-                code_cols = slice(P * (2 * u + c), P * (2 * u + c + 1))
-                nc.tensor.matmul_mx(
-                    out=y[:, u, :],
-                    lhsT=w_codes[:].bitcast(FP8X4),
-                    lhsT_scale=w_scales[:],
-                    rhs=v_codes[:, code_cols].bitcast(FP8X4),
-                    rhs_scale=v_scales[:, code_cols],
-                    start=True,
-                    stop=True,
-                )
-            in_order = y[:].rearrange("p u (j f) -> p f (u j)", j=2)
-            width = HALF_ROWS // (c + 1)
-            for first in range(0, HALF_ROWS, width):
-                cols = slice(4 * (HALF_ROWS * c + first), 4 * (HALF_ROWS * c + first + width))
-                nc.vector.scalar_tensor_tensor(
-                    result[:, cols].rearrange("p (f t) -> p f t", t=4),
-                    in_order[:, first : first + width],
-                    inv[:],
-                    ch_sb[:, cols].rearrange("p (f t) -> p f t", t=4),
-                    MULT,
-                    MULT,
-                )
-                nc.sync.dma_start(out[0][:, cols], result[:, cols])
+        for part, tag in enumerate(("y0", "y1", "scores1", "scores2")):
+            cols = slice(P * part, P * (part + 1))
+            y = psum.tile([P, P], F32, name=f"y{part}", tag=tag)
+            nc.tensor.matmul_mx(
+                out=y[:],
+                lhsT=w_codes[:].bitcast(FP8X4),
+                lhsT_scale=w_scales[:],
+                rhs=v_codes[:, cols].bitcast(FP8X4),
+                rhs_scale=v_scales[:, cols],
+                start=True,
+                stop=True,
+            )
+            nc.vector.scalar_tensor_tensor(
+                result[:, cols].rearrange("p (f t) -> p f t", t=4),
+                y[:].rearrange("p (t f) -> p f t", t=4),
+                inv[:],
+                ch_sb[:, cols].rearrange("p (f t) -> p f t", t=4),
+                MULT,
+                MULT,
+            )
+            if part != 2:
+                stored = slice(min(cols.start, 2 * P), cols.stop)
+                nc.sync.dma_start(out[0][:, stored], result[:, stored])

@@ -135,15 +135,11 @@ def tile_attend_x_mla_append256_topk_kernel(tc, qT, cT, new_cT, ts, ch, offs, sl
         q_bf = keep.tile([P, NQ, 4], BF16, name="q_bf", align_bytes=64)
         nc.gpsimd.tensor_copy(q_bf[:], q_raw[:].rearrange("p j q -> p q j"))
 
-        pieces = quarters[:3] + [slice(3 * ROWS, 3 * ROWS + ROWS // 2), slice(3 * ROWS + ROWS // 2, P)]
-        keys = [
-            keep.tile([P, 4, rows.stop - rows.start, 2], U32, name=f"keys{h}", tag=f"keys{h}", align_bytes=64)
-            for h, rows in enumerate(pieces)
-        ]
+        keys = [keep.tile([P, 4, ROWS, 2], U32, name=f"keys{h}", tag=f"keys{h}", align_bytes=64) for h in range(4)]
         for rows in quarters[:3]:
             gather(3, rows)
         gather_and_place(3, quarters[3], "row3", True, nc.vector)
-        for h, rows in enumerate(pieces):
+        for h, rows in enumerate(quarters):
             nc.scalar.copy(keys[h][:], words.rearrange("p u s m -> p s m u")[:, :, rows, :])
         q_codes = keep.tile([P, NQ], U32, name="q_codes", align_bytes=64)
         q_scales = keep.tile([P, NQ], U8, name="q_scales", align_bytes=64)
@@ -151,12 +147,10 @@ def tile_attend_x_mla_append256_topk_kernel(tc, qT, cT, new_cT, ts, ch, offs, sl
             out=q_codes[:].bitcast(FP8X4), scales=q_scales[:], in_=q_bf[:].rearrange("p q j -> p (q j)")
         )
 
-        scores = []
-        for h, rows in enumerate(pieces):
-            width = 4 * (rows.stop - rows.start)
-            scores.append(psum.tile([P, width], F32, name=f"scores{h}", tag=f"scores{h}"))
-            k_codes = keep.tile([P, width], U32, name=f"k_codes{h}", align_bytes=64)
-            k_scales = keep.tile([P, width], U8, name=f"k_scales{h}", align_bytes=64)
+        scores = [psum.tile([P, P], F32, name=f"scores{h}", tag=f"scores{h}") for h in range(4)]
+        for h in range(4):
+            k_codes = keep.tile([P, P], U32, name=f"k_codes{h}", align_bytes=64)
+            k_scales = keep.tile([P, P], U8, name=f"k_scales{h}", align_bytes=64)
             nc.vector.quantize_mx(
                 out=k_codes[:].bitcast(FP8X4),
                 scales=k_scales[:],
@@ -179,12 +173,11 @@ def tile_attend_x_mla_append256_topk_kernel(tc, qT, cT, new_cT, ts, ch, offs, sl
 
         a = keep.tile([P, 4, N // 4], F32, name="a", tag="keys2", align_bytes=64)
         neg_m = keep.tile([P, 1], F32, name="neg_m")
-        for h, rows in enumerate(pieces):
-            c = rows.start // HALF_ROWS
+        for h, rows in enumerate(quarters):
             nc.vector.tensor_tensor(
                 a[:, :, rows],
                 scores[h][:].rearrange("p (s m) -> p s m", s=4),
-                ts_free[c][:, :, rows.start - HALF_ROWS * c : rows.stop - HALF_ROWS * c],
+                ts_free[h // 2][:, :, quarters[h % 2]],
                 MULT,
             )
         nc.vector.tensor_reduce(neg_m[:], a[:].rearrange("p s m -> p (s m)"), mybir.AxisListType.X, MAX, negate=True)

@@ -36,7 +36,9 @@ def tile_attend_x_mla_append256_topk_kernel(tc, qT, cT, new_cT, ts, ch, offs, sl
         slots_sb = lists.tile([P, NEW // 16], U16, name="slots_sb")
         offs_sb = lists.tile([P, N // 16], U16, name="offs_sb")
 
-        new_sb = [keep.tile([P, NEW], F32, name=f"new{t}", align_bytes=64) for t in range(4)]
+        new12 = keep.tile([P, 2, NEW], F32, name="new12", align_bytes=64)
+        new_sb = [keep.tile([P, NEW], F32, name="new0", align_bytes=64), new12[:, 0], new12[:, 1]]
+        new_sb.append(keep.tile([P, NEW], F32, name="new3", align_bytes=64))
         pool = [keep.tile([P, T], F32, name=f"pool{t}", align_bytes=64) for t in range(4)]
         words_flat = keep.tile([P, 2 * N], U32, name="words_flat", align_bytes=64)
         words = words_flat[:].rearrange("p (u s m) -> p u s m", u=2, s=4)
@@ -49,22 +51,28 @@ def tile_attend_x_mla_append256_topk_kernel(tc, qT, cT, new_cT, ts, ch, offs, sl
         pool_view = cT.rearrange("(p j) w -> p j w", j=4)
 
         nc.scalar.dma_start(ts_sb[P - 1 : P, :], ts[0:1, :])
-        nc.sync.dma_start(offs_sb[:], offs)
         nc.sync.dma_start(pool[0][:], pool_view[:, 0, :])
         nc.sync.dma_start(slots_sb[:], slots)
         nc.sync.dma_start(new_sb[0][:], new_view[:, 0, :])
-        for t in range(1, 4):
+        nc.sync.dma_start(offs_sb[:], offs)
+        nc.sync.dma_start(pool[1][:], pool_view[:, 1, :])
+        nc.sync.dma_start(new12[:], new_view[:, 1:3, :])
+        for t in range(2, 4):
             nc.sync.dma_start(pool[t][:], pool_view[:, t, :])
-            nc.sync.dma_start(new_sb[t][:], new_view[:, t, :])
+        nc.sync.dma_start(new_sb[3][:], new_view[:, 3, :])
         nc.sync.dma_start(q_raw[:], qT[0].rearrange("(p j) w -> p j w", j=4))
         nc.sync.dma_start(ch_sb[:], ch)
+
+        warm = keep.tile([P, 2], F32, name="warm")
+        nc.vector.memset(warm[:, 0:1], 0.0)
+        nc.scalar.activation(out=warm[:, 1:2], in_=warm[:, 0:1], func=ACT.Exp)
 
         ident = keep.tile([P, P], F32, name="ident")
         make_identity(nc, ident[:])
 
         nc.vector.memset(ts_sb[0 : P - 1, :], 0.0)
         ts_row = keep.tile([P, N], F32, name="ts_row", align_bytes=64)
-        nc.scalar.activation(out=ts_row[:], in_=ts_sb[:].indirect(offs_sb[:]), func=ACT.Copy)
+        nc.vector.tensor_copy(ts_row[:], ts_sb[:].indirect(offs_sb[:]))
         ts_turned = psum.tile([P, 4, P], F32, name="ts_turned", tag="p_turned")
         for s in range(4):
             nc.tensor.transpose(ts_turned[:, s, :], ts_row[:].rearrange("p (m s) -> p s m", s=4)[:, s, :], ident[:])
@@ -99,28 +107,30 @@ def tile_attend_x_mla_append256_topk_kernel(tc, qT, cT, new_cT, ts, ch, offs, sl
 
         everything = slice(0, P)
         quarters = [slice(ROWS * h, ROWS * (h + 1)) for h in range(4)]
-        def gather_and_place(t, rows, tag, on_scalar, placer):
+
+        def gather_and_place(t, rows, tag, placer):
             row = keep.tile([P, 4 * (rows.stop - rows.start)], BF16, name=f"row_{tag}", tag=tag, align_bytes=64)
             window = pool[t][:].indirect(offs_sb[:, rows.start // 4 : rows.stop // 4])
-            if on_scalar:
-                nc.scalar.activation(out=row[:], in_=window, func=ACT.Copy)
-            else:
-                nc.vector.tensor_copy(row[:], window)
+            nc.scalar.activation(out=row[:], in_=window, func=ACT.Copy)
             placer.tensor_copy(
                 halves[:, t // 2, t % 2, rows].rearrange("p m s -> p s m"), row[:].rearrange("p (m s) -> p s m", s=4)
             )
 
-        scatter_on_vector(0, 0, NEW)
+        scatter_on_scalar(0, 0, NEW)
         gather(0, everything)
         scatter_on_scalar(1, 0, NEW)
-        ts_col = keep.tile([P, 4], F32, name="ts_col", tag="new1", align_bytes=64)
-        nc.scalar.copy(ts_col[:], ts_turned[:, :, P - 1])
+        ts_col = new_sb[1][:, 0:4]
+        nc.scalar.copy(ts_col, ts_turned[:, :, P - 1])
         ts_spread = psum.tile([P, 4, P], F32, name="ts_spread", tag="y0")
         for s in range(4):
             nc.tensor.transpose(ts_spread[:, s, :], ts_col[:, s : s + 1].to_broadcast([P, P]), ident[:])
-        gather_and_place(1, slice(0, 3 * ROWS), "pool0", True, nc.gpsimd)
+        gather_and_place(1, slice(0, 3 * ROWS), "pool0", nc.gpsimd)
         scatter_on_vector(2, 0, NEW)
-        gather_and_place(1, quarters[3], "new2", False, nc.gpsimd)
+        strip = new_sb[2][:, 0 : 4 * ROWS]
+        nc.vector.tensor_copy(strip, pool[1][:].indirect(offs_sb[:, 3 * ROWS // 4 :]))
+        nc.gpsimd.tensor_copy(
+            halves[:, 0, 1, quarters[3]].rearrange("p m s -> p s m"), strip.rearrange("p (m s) -> p s m", s=4)
+        )
         gather(2, everything)
         scatter_on_scalar(3, 0, NEW)
         turned0 = turn_pair(0, "p_turned")
@@ -138,7 +148,7 @@ def tile_attend_x_mla_append256_topk_kernel(tc, qT, cT, new_cT, ts, ch, offs, sl
         keys = [keep.tile([P, 4, ROWS, 2], U32, name=f"keys{h}", tag=f"keys{h}", align_bytes=64) for h in range(4)]
         for rows in quarters[:3]:
             gather(3, rows)
-        gather_and_place(3, quarters[3], "row3", True, nc.vector)
+        gather_and_place(3, quarters[3], "row3", nc.vector)
         for h, rows in enumerate(quarters):
             nc.scalar.copy(keys[h][:], words.rearrange("p u s m -> p s m u")[:, :, rows, :])
         q_codes = keep.tile([P, NQ], U32, name="q_codes", align_bytes=64)
@@ -171,16 +181,19 @@ def tile_attend_x_mla_append256_topk_kernel(tc, qT, cT, new_cT, ts, ch, offs, sl
         for c in range(2):
             copy_values(values0[:, c], turned0, c)
 
-        a = keep.tile([P, 4, N // 4], F32, name="a", tag="keys2", align_bytes=64)
+        a = keep.tile([P, N + 1], F32, name="a", tag="keys2", align_bytes=64)
+        a_quarters = a[:, 0:N].rearrange("p (h s m) -> p h s m", h=4, s=4)
         neg_m = keep.tile([P, 1], F32, name="neg_m")
-        for h, rows in enumerate(quarters):
+        for h in range(4):
+            if h == 3:
+                nc.vector.tensor_reduce(a[:, N : N + 1], a[:, 0:P], mybir.AxisListType.X, MAX)
             nc.vector.tensor_tensor(
-                a[:, :, rows],
+                a_quarters[:, h],
                 scores[h][:].rearrange("p (s m) -> p s m", s=4),
                 ts_free[h // 2][:, :, quarters[h % 2]],
                 MULT,
             )
-        nc.vector.tensor_reduce(neg_m[:], a[:].rearrange("p s m -> p (s m)"), mybir.AxisListType.X, MAX, negate=True)
+        nc.vector.tensor_reduce(neg_m[:], a[:, P:], mybir.AxisListType.X, MAX, negate=True)
 
         v_codes = keep.tile([P, D], U32, name="v_codes", tag="keys0", align_bytes=64)
         v_scales = keep.tile([P, D], U8, name="v_scales", align_bytes=64)
@@ -199,7 +212,11 @@ def tile_attend_x_mla_append256_topk_kernel(tc, qT, cT, new_cT, ts, ch, offs, sl
         p_turned = psum.tile([P, 4, NQ], F32, name="p_turned", tag="p_turned")
         for s in range(4):
             nc.scalar.activation(
-                out=prob[:, s], in_=a[:, s], func=ACT.Exp, bias=neg_m[:], accum_out=sums[:, s - 1 : s] if s >= 2 else None
+                out=prob[:, s].rearrange("p (h m) -> p h m", h=4),
+                in_=a_quarters[:, :, s],
+                func=ACT.Exp,
+                bias=neg_m[:],
+                accum_out=sums[:, s - 1 : s] if s >= 2 else None,
             )
             nc.tensor.transpose(p_turned[:, s, :], prob[:, s, :], ident[:])
 
@@ -218,7 +235,7 @@ def tile_attend_x_mla_append256_topk_kernel(tc, qT, cT, new_cT, ts, ch, offs, sl
             nc.vector.tensor_tensor(
                 w_grouped[:, queries, :],
                 p_turned[:].rearrange("p s q -> p q s")[:, queries, :],
-                ts_col[:].unsqueeze(1).to_broadcast([P, NQ // 2, 4]),
+                ts_col.unsqueeze(1).to_broadcast([P, NQ // 2, 4]),
                 MULT,
             )
         w_codes = keep.tile([P, NQ], U32, name="w_codes", align_bytes=64)

from contextlib import ExitStack

import concourse.mybir as mybir
from concourse.masks import make_identity

F32 = mybir.dt.float32
BF16 = mybir.dt.bfloat16
U32 = mybir.dt.uint32
U16 = mybir.dt.uint16
U8 = mybir.dt.uint8
FP8X4 = mybir.dt.float8_e4m3fn_x4
MULT = mybir.AluOpType.mult
ADD = mybir.AluOpType.add
MAX = mybir.AluOpType.max
ACT = mybir.ActivationFunctionType

P = 128
T = 1024
NEW = 256
N = 512
D = 512
NQ = 128
ROWS = 32
HALF_ROWS = 64

FLOPS = 2 * NQ * N * D * 2


def tile_attend_x_mla_append256_topk_kernel(tc, qT, cT, new_cT, ts, ch, offs, slots, out):
    nc = tc.nc
    with ExitStack() as ctx:
        lists = ctx.enter_context(tc.tile_pool(name="lists", bufs=1))
        keep = ctx.enter_context(tc.tile_pool(name="keep", bufs=1))
        psum = ctx.enter_context(tc.psum_pool(name="psum", bufs=1))

        slots_sb = lists.tile([P, NEW // 16], U16, name="slots_sb")
        offs_sb = lists.tile([P, N // 16], U16, name="offs_sb")

        new12 = keep.tile([P, 2, NEW], F32, name="new12", align_bytes=64)
        new_sb = [keep.tile([P, NEW], F32, name="new0", align_bytes=64), new12[:, 0], new12[:, 1]]
        new_sb.append(keep.tile([P, NEW], F32, name="new3", align_bytes=64))
        pool = [keep.tile([P, T], F32, name=f"pool{t}", align_bytes=64) for t in range(4)]
        words_flat = keep.tile([P, 2 * N], U32, name="words_flat", align_bytes=64)
        words = words_flat[:].rearrange("p (u s m) -> p u s m", u=2, s=4)
        halves = words_flat[:].bitcast(BF16).rearrange("p (u s m h) -> p u h m s", u=2, s=4, h=2)
        q_raw = keep.tile([P, 4, NQ], F32, name="q_raw")
        ts_sb = keep.tile([P, T], F32, name="ts_sb")
        ch_sb = keep.tile([P, D], F32, name="ch_sb")

        new_view = new_cT.rearrange("(p j) w -> p j w", j=4)
        pool_view = cT.rearrange("(p j) w -> p j w", j=4)

        nc.scalar.dma_start(ts_sb[P - 1 : P, :], ts[0:1, :])
        nc.sync.dma_start(pool[0][:], pool_view[:, 0, :])
        nc.sync.dma_start(slots_sb[:], slots)
        nc.sync.dma_start(new_sb[0][:], new_view[:, 0, :])
        nc.sync.dma_start(offs_sb[:], offs)
        nc.sync.dma_start(pool[1][:], pool_view[:, 1, :])
        nc.sync.dma_start(new12[:], new_view[:, 1:3, :])
        for t in range(2, 4):
            nc.sync.dma_start(pool[t][:], pool_view[:, t, :])
        nc.sync.dma_start(new_sb[3][:], new_view[:, 3, :])
        nc.sync.dma_start(q_raw[:], qT[0].rearrange("(p j) w -> p j w", j=4))
        nc.sync.dma_start(ch_sb[:], ch)

        warm = keep.tile([P, 2], F32, name="warm")
        nc.vector.memset(warm[:, 0:1], 0.0)
        nc.scalar.activation(out=warm[:, 1:2], in_=warm[:, 0:1], func=ACT.Exp)

        ident = keep.tile([P, P], F32, name="ident")
        make_identity(nc, ident[:])

        nc.vector.memset(ts_sb[0 : P - 1, :], 0.0)
        ts_row = keep.tile([P, N], F32, name="ts_row", align_bytes=64)
        nc.vector.tensor_copy(ts_row[:], ts_sb[:].indirect(offs_sb[:]))
        ts_turned = psum.tile([P, 4, P], F32, name="ts_turned", tag="p_turned")
        for s in range(4):
            nc.tensor.transpose(ts_turned[:, s, :], ts_row[:].rearrange("p (m s) -> p s m", s=4)[:, s, :], ident[:])

        def scatter_on_vector(t, first, last):
            nc.vector.tensor_copy(pool[t][:].indirect(slots_sb[:, first // 16 : last // 16]), new_sb[t][:, first:last])

        def scatter_on_scalar(t, first, last):
            nc.scalar.activation(
                out=pool[t][:].indirect(slots_sb[:, first // 16 : last // 16]), in_=new_sb[t][:, first:last], func=ACT.Copy
            )

        def gather(t, rows):
            nc.vector.tensor_copy(
                halves[:, t // 2, t % 2, rows], pool[t][:].indirect(offs_sb[:, rows.start // 4 : rows.stop // 4])
            )

        word_floats = words.bitcast(F32)

        def turn_pair(u, tag):
            turned = psum.tile([P, 4, P], F32, name=f"turned{u}", tag=tag)
            for s in range(4):
                nc.tensor.transpose(turned[:, s, :], word_floats[:, u, s, :], ident[:])
            return turned

        def copy_values(values, turned, c):
            bank = turned[:].rearrange("p s f -> p (s f)").bitcast(BF16)
            nc.scalar.copy(
                values.rearrange("p (k j f s) -> p k f j s", k=2, j=2, s=4),
                bank.rearrange("p (s c k f j) -> p c k f j s", s=4, c=2, k=2, j=2)[:, c],
            )

        everything = slice(0, P)
        quarters = [slice(ROWS * h, ROWS * (h + 1)) for h in range(4)]

        def gather_and_place(t, rows, tag, placer):
            row = keep.tile([P, 4 * (rows.stop - rows.start)], BF16, name=f"row_{tag}", tag=tag, align_bytes=64)
            window = pool[t][:].indirect(offs_sb[:, rows.start // 4 : rows.stop // 4])
            nc.scalar.activation(out=row[:], in_=window, func=ACT.Copy)
            placer.tensor_copy(
                halves[:, t // 2, t % 2, rows].rearrange("p m s -> p s m"), row[:].rearrange("p (m s) -> p s m", s=4)
            )

        scatter_on_scalar(0, 0, NEW)
        gather(0, everything)
        scatter_on_scalar(1, 0, NEW)
        ts_col = new_sb[1][:, 0:4]
        nc.scalar.copy(ts_col, ts_turned[:, :, P - 1])
        ts_spread = psum.tile([P, 4, P], F32, name="ts_spread", tag="y0")
        for s in range(4):
            nc.tensor.transpose(ts_spread[:, s, :], ts_col[:, s : s + 1].to_broadcast([P, P]), ident[:])
        gather_and_place(1, slice(0, 3 * ROWS), "pool0", nc.gpsimd)
        scatter_on_vector(2, 0, NEW)
        strip = new_sb[2][:, 0 : 4 * ROWS]
        nc.vector.tensor_copy(strip, pool[1][:].indirect(offs_sb[:, 3 * ROWS // 4 :]))
        nc.gpsimd.tensor_copy(
            halves[:, 0, 1, quarters[3]].rearrange("p m s -> p s m"), strip.rearrange("p (m s) -> p s m", s=4)
        )
        gather(2, everything)
        scatter_on_scalar(3, 0, NEW)
        turned0 = turn_pair(0, "p_turned")

        def copy_spread(c, tag):
            half = keep.tile([P, 4, HALF_ROWS], F32, name=f"ts_free{c}", tag=tag, align_bytes=64)
            nc.scalar.copy(half[:], ts_spread[:, :, HALF_ROWS * c : HALF_ROWS * (c + 1)])
            return half

        ts_free = [copy_spread(0, "new3")]

        q_bf = keep.tile([P, NQ, 4], BF16, name="q_bf", align_bytes=64)
        nc.gpsimd.tensor_copy(q_bf[:], q_raw[:].rearrange("p j q -> p q j"))

        keys = [keep.tile([P, 4, ROWS, 2], U32, name=f"keys{h}", tag=f"keys{h}", align_bytes=64) for h in range(4)]
        for rows in quarters[:3]:
            gather(3, rows)
        gather_and_place(3, quarters[3], "row3", nc.vector)
        for h, rows in enumerate(quarters):
            nc.scalar.copy(keys[h][:], words.rearrange("p u s m -> p s m u")[:, :, rows, :])
        q_codes = keep.tile([P, NQ], U32, name="q_codes", align_bytes=64)
        q_scales = keep.tile([P, NQ], U8, name="q_scales", align_bytes=64)
        nc.vector.quantize_mx(
            out=q_codes[:].bitcast(FP8X4), scales=q_scales[:], in_=q_bf[:].rearrange("p q j -> p (q j)")
        )

        scores = [psum.tile([P, P], F32, name=f"scores{h}", tag=f"scores{h}") for h in range(4)]
        for h in range(4):
            k_codes = keep.tile([P, P], U32, name=f"k_codes{h}", align_bytes=64)
            k_scales = keep.tile([P, P], U8, name=f"k_scales{h}", align_bytes=64)
            nc.vector.quantize_mx(
                out=k_codes[:].bitcast(FP8X4),
                scales=k_scales[:],
                in_=keys[h][:].rearrange("p s m u -> p (s m u)").bitcast(BF16),
            )
            nc.tensor.matmul_mx(
                out=scores[h][:],
                lhsT=q_codes[:].bitcast(FP8X4),
                lhsT_scale=q_scales[:],
                rhs=k_codes[:].bitcast(FP8X4),
                rhs_scale=k_scales[:],
                start=True,
                stop=True,
            )

        ts_free.append(copy_spread(1, "keys0"))
        values0 = keep.tile([P, 2, 4 * P], BF16, name="values0", tag="keys1", align_bytes=64)
        for c in range(2):
            copy_values(values0[:, c], turned0, c)

        a = keep.tile([P, N + 1], F32, name="a", tag="keys2", align_bytes=64)
        a_quarters = a[:, 0:N].rearrange("p (h s m) -> p h s m", h=4, s=4)
        neg_m = keep.tile([P, 1], F32, name="neg_m")
        for h in range(4):
            if h == 3:
                nc.vector.tensor_reduce(a[:, N : N + 1], a[:, 0:P], mybir.AxisListType.X, MAX)
            nc.vector.tensor_tensor(
                a_quarters[:, h],
                scores[h][:].rearrange("p (s m) -> p s m", s=4),
                ts_free[h // 2][:, :, quarters[h % 2]],
                MULT,
            )
        nc.vector.tensor_reduce(neg_m[:], a[:, P:], mybir.AxisListType.X, MAX, negate=True)

        v_codes = keep.tile([P, D], U32, name="v_codes", tag="keys0", align_bytes=64)
        v_scales = keep.tile([P, D], U8, name="v_scales", align_bytes=64)

        def quantize_values(u, part, values):
            cols = slice(P * part + HALF_ROWS * u, P * part + HALF_ROWS * (u + 1))
            source = values[:].rearrange("p c (k x) -> p (c k) x", k=2)[:, part]
            nc.vector.quantize_mx(out=v_codes[:, cols].bitcast(FP8X4), scales=v_scales[:, cols], in_=source)

        for part in range(4):
            quantize_values(0, part, values0)
        turned1 = turn_pair(1, "scores0")

        prob = keep.tile([P, 4, N // 4], F32, name="prob")
        sums = keep.tile([P, 3], F32, name="sums")
        p_turned = psum.tile([P, 4, NQ], F32, name="p_turned", tag="p_turned")
        for s in range(4):
            nc.scalar.activation(
                out=prob[:, s].rearrange("p (h m) -> p h m", h=4),
                in_=a_quarters[:, :, s],
                func=ACT.Exp,
                bias=neg_m[:],
                accum_out=sums[:, s - 1 : s] if s >= 2 else None,
            )
            nc.tensor.transpose(p_turned[:, s, :], prob[:, s, :], ident[:])

        values1 = keep.tile([P, 2, 4 * P], BF16, name="values1", tag="keys2", align_bytes=64)
        for c in range(2):
            copy_values(values1[:, c], turned1, c)
        total = keep.tile([P, 1], F32, name="total")
        inv = keep.tile([P, 1], F32, name="inv")
        nc.vector.tensor_reduce(sums[:, 0:1], prob[:, 0:2].rearrange("p s m -> p (s m)"), mybir.AxisListType.X, ADD)
        nc.vector.tensor_reduce(total[:], sums[:], mybir.AxisListType.X, ADD)
        nc.vector.reciprocal(inv[:], total[:])

        w_grouped = keep.tile([P, NQ, 4], BF16, name="w_grouped", align_bytes=64)
        query_halves = [slice(0, NQ // 2), slice(NQ // 2, NQ)]
        for queries in query_halves:
            nc.vector.tensor_tensor(
                w_grouped[:, queries, :],
                p_turned[:].rearrange("p s q -> p q s")[:, queries, :],
                ts_col.unsqueeze(1).to_broadcast([P, NQ // 2, 4]),
                MULT,
            )
        w_codes = keep.tile([P, NQ], U32, name="w_codes", align_bytes=64)
        w_scales = keep.tile([P, NQ], U8, name="w_scales", align_bytes=64)

        def quantize_weights(queries):
            nc.vector.quantize_mx(
                out=w_codes[:, queries].bitcast(FP8X4),
                scales=w_scales[:, queries],
                in_=w_grouped[:, queries, :].rearrange("p q s -> p (q s)"),
            )

        quantize_weights(query_halves[0])
        quantize_values(1, 0, values1)
        quantize_weights(query_halves[1])
        for part in range(1, 4):
            quantize_values(1, part, values1)

        result = keep.tile([P, D], F32, name="result")
        for part, tag in enumerate(("y0", "y1", "scores1", "scores2")):
            cols = slice(P * part, P * (part + 1))
            y = psum.tile([P, P], F32, name=f"y{part}", tag=tag)
            nc.tensor.matmul_mx(
                out=y[:],
                lhsT=w_codes[:].bitcast(FP8X4),
                lhsT_scale=w_scales[:],
                rhs=v_codes[:, cols].bitcast(FP8X4),
                rhs_scale=v_scales[:, cols],
                start=True,
                stop=True,
            )
            nc.vector.scalar_tensor_tensor(
                result[:, cols].rearrange("p (f t) -> p f t", t=4),
                y[:].rearrange("p (t f) -> p f t", t=4),
                inv[:],
                ch_sb[:, cols].rearrange("p (f t) -> p f t", t=4),
                MULT,
                MULT,
            )
            if part != 2:
                stored = slice(min(cols.start, 2 * P), cols.stop)
                nc.sync.dma_start(out[0][:, stored], result[:, stored])
